import numpy as np, ml_dtypes
CORES = [3,11,19,27,35,43,51,59]
N = 8
BF = ml_dtypes.bfloat16
def gentries(a):
    return np.ascontiguousarray(a.reshape(8, 16, -1).transpose(0, 2, 1)).reshape(8, -1)
def gtable(e):
    e = np.asarray(e); return np.ascontiguousarray(e.reshape(8, -1, 16).transpose(0, 2, 1)).reshape(128, -1).astype(np.int32)
R, M, L, F, RO = 256, 768, 2, 512, 3
V = R + L * M
AT = [0] + [R + i * M for i in range(L + 1)]
LEV = np.repeat(np.arange(L + 1), np.diff(AT))
TOP = np.concatenate([2 * np.array(AT)[LEV[R:]], np.full(R, 2 * V)])
LOW = np.array(AT)[LEV + 1]
def under(rng, shape, top):
    return np.minimum((rng.random(shape) * top).astype(np.int64), np.asarray(top) - 1)
def parts(rng):
    i = np.arange(16)[:, None]; sh = (N, 8, 1, V)
    p = rng.integers(0, 16, sh); p2 = (p + rng.integers(1, 16, sh)) % 16
    t = 1 + (255 * rng.random(sh) ** (1.5 + LEV)).astype(np.int64); t2 = 1 + (255 * rng.random(sh) ** (1.5 + LEV)).astype(np.int64)
    x = np.where(i == p, t, 0); x = np.where((i == p2) & (rng.random(sh) < 0.125), t2, x); x = np.where(rng.random(sh) < 0.02, 0, x)
    s = (256 * rng.random((N, 8, 16, R)) ** 1.5).astype(np.int64)
    c = rng.integers(0, 256, (N, 8, 16, R + F)) * (rng.random((N, 8, 16, R + F)) > 0.15)
    half = rng.random(sh) < 0.75
    o = np.argsort(rng.random((N, 8, 16, V)) + 10 * (half & (i >= 8)), axis=2)
    k = np.where(half, rng.choice(np.array([0, 1, 1, 2, 2, 3, 4, 8]), sh), rng.choice(np.array([1, 2, 3, 5, 12, 16]), sh))
    e = np.where(o < k, under(rng, (N, 8, 16, V), TOP), 2 * V)
    a = LOW + under(rng, (N, 8, 2, V), V + R + F - LOW)
    return x, s, c[..., :R].copy(), c[..., R:].copy(), e, a
def rich(rng, x, v):
    k = rng.integers(3, 17, (N, 8, 1, V)); o = np.argsort(rng.random(x.shape), axis=2)
    return np.where(rng.random((N, 8, 1, V)) < 0.25, np.where(o < k, v, 0), x)
def pack(x, s, q, c, e, a):
    def b(v):
        return np.ascontiguousarray(v.reshape(N, 128, -1)).astype(np.float32).astype(BF)
    return {"piv": b(x), "safe": b(s), "lem": b(q), "leaf": b(c), "uses": np.ascontiguousarray(e.reshape(N, 128, V)).astype(np.int32), "prem": np.stack([gtable(v) for v in a.reshape(N, 8, 2 * V)])}
def setup_inputs(rng):
    return pack(*parts(rng))
def setup_inputs_turn(rng):
    x, s, q, c, e, a = parts(rng); i = np.arange(16)[:, None]
    j = rng.integers(0, 16, (N, 8, 1, 1)); w = rng.integers(0, 7, (N, 8, 1, V))
    w[..., :7] = np.arange(7)
    one, two = i == j, i == (j + 8) % 16
    m = np.where(w == 0, one, np.where(w == 1, two, np.where(w == 2, one | two, np.where(w == 3, i < 8, np.where(w == 4, i >= 8, w == 5)))))
    n = under(rng, (N, 8, 16, V), TOP); n = n - (n & 1) * (rng.random(n.shape) < 0.5)
    x = np.where(rng.random((N, 8, 1, V)) < 0.3, 0, x)
    return pack(x, s, q, c, np.where(m, n, 2 * V), a)
def setup_inputs_ties(rng):
    x, s, q, c, e, a = parts(rng); v = np.array([0, 1, 127, 128, 129, 254, 255])
    x = rich(rng, x, 1)
    x = np.where(x > 0, rng.choice(np.array([1, 127, 128, 129, 255]), x.shape), 0); nx = np.roll(x, 8, axis=2)
    s, q, c = rng.choice(v, s.shape), rng.choice(v, q.shape), rng.choice(v, c.shape)
    s[..., 0] = x[..., 0]; s[..., 1] = np.maximum(x[..., 1] - 1, 0); s[..., 2] = np.maximum(x[..., 2], nx[..., 2]); s[..., 3] = nx[..., 3]
    return pack(x, s, q, c, e, a)
def setup_inputs_alike(rng):
    x, s, q, c, e, a = parts(rng); on = e < 2 * V
    e[:, 1] = np.where(on[:, 1], under(rng, (N, 1, V), TOP), 2 * V)
    e[:, 2] = np.where(on[:, 2], np.where(rng.random((N, 16, V)) < 0.5, 0, TOP - 1), 2 * V)
    e[:, 3] = 2 * V
    e[:, 4] = np.where(on[:, 4], TOP - 1 - rng.integers(0, 16, (N, 16, V)), 2 * V)
    e[:, 5] = under(rng, (N, 16, V), TOP)
    a[:, 1, 1] = a[:, 1, 0]; a[:, 2] = np.where(rng.random((N, 2, V)) < 0.5, LOW, V + R + F - 1)
    a[:, 4] = V + rng.integers(0, R, (N, 2, V)); a[:, 5] = V + R + rng.integers(0, F, (N, 2, V)); a[:, 6] = LOW
    return pack(x, s, q, c, e, a)
def setup_inputs_late(rng):
    x, s, q, c, e, a = parts(rng); g = int(rng.integers(0, 8)); s[:] = 0
    q2, c2 = rng.integers(200, 256, q.shape), rng.integers(200, 256, c.shape); q2[:, g] = q[:, g]; c2[:, g] = c[:, g]
    e[..., V - R:] = np.where(rng.random((N, 8, 1, R)) < 0.5, 2 * V, e[..., V - R:])
    return pack(x, s, q2, c2, e, a)
def setup_inputs_spread(rng):
    x, s, q, c, e, a = parts(rng)
    def u(n):
        return np.minimum((np.exp2(8 * rng.random((N, 8, 1, n))) * rng.random((N, 8, 16, n))).astype(np.int64), 255)
    x = np.where(x > 0, np.minimum(np.exp2(8 * rng.random(x.shape)).astype(np.int64), 255), 0)
    x = rich(rng, x, np.maximum(u(V), 1))
    m = rng.random((N, 8, 16, V)) < rng.random((N, 8, 1, V)) ** 3
    return pack(x, u(R), u(R), u(F), np.where(m, under(rng, (N, 8, 16, V), TOP), 2 * V), a)
def check_inputs(d):
    bad = []
    for k in ("piv", "safe", "lem", "leaf"):
        v = np.asarray(d[k]).astype(np.float32)
        if not np.all((v >= 0) & (v <= 255) & (v == np.floor(v))): bad.append("whole numbers from 0 to 255 in " + k)
    e = np.asarray(d["uses"]).astype(np.int64)
    if not np.all(((e >= 0) & (e < TOP)) | (e == 2 * V)): bad.append("range of uses")
    a = np.stack([gentries(v) for v in d["prem"]]).astype(np.int64).reshape(N, 8, 2, V)
    if not np.all((a >= LOW) & (a < V + R + F)): bad.append("range of prem")
    return bad
def least(S, e):
    return np.stack([[np.min(np.take(S[q, g], e[q, g], axis=1), axis=1) for g in range(8)] for q in range(N)])
def splice(e, st):
    K = np.zeros((N, 8, 1, 2 * V + 1), bool)
    K[:, :, 0, 2 * R:2 * V:2] = st[..., R:] == 1; K[:, :, 0, 2 * R + 1:2 * V:2] = st[..., R:] == 2
    loose = np.take_along_axis(K, e, 3); has = np.any(loose, axis=2, keepdims=True); j = np.argmax(loose, axis=2)[:, :, None]
    this = (np.arange(16)[:, None] == j) & has
    u = np.take_along_axis(e, j, 2) >> 1
    t = np.roll(np.take_along_axis(e, np.where(has, u - R, 0), 3), 8, axis=2)
    hit = np.any((t != 2 * V) & (e != 2 * V) & ~this, axis=2, keepdims=True)
    return np.where(has & ~hit, np.where(t != 2 * V, t, np.where(this, 2 * V, e)), e)
def reference(piv, safe, lem, leaf, uses, prem):
    def w(v):
        return v.astype(np.float32).astype(np.int64).reshape(N, 8, 16, -1)
    x = w(piv); nx = np.roll(x, 8, axis=2)
    s = np.full((N, 8, 16, V), 255, np.int64); s[..., :R] = w(safe)
    C = np.zeros((N, 8, 16, V + R + F), np.int64); C[..., V:V + R] = w(lem); C[..., V + R:] = w(leaf)
    e = uses.astype(np.int64).reshape(N, 8, 16, V)
    a = np.stack([gentries(v) for v in prem]).astype(np.int64).reshape(N, 8, 2, V)
    st = np.zeros((N, 8, V), np.int64); S = np.full((N, 8, 16, 2 * V + 1), 255, np.int64); gs = None
    for rnd in range(RO):
        old = st[:, :, None] > 0
        if rnd:
            s[..., :R] = np.where(old[..., :R], s[..., :R], np.roll(gs, 1, axis=0))
            C[..., V:V + R] = np.roll(C[..., :R], -1, axis=0)
            e = splice(e, st)
        for l in range(L + 1):
            i, j = AT[l], AT[l + 1]
            if l: s[..., i:j] = np.where(old[..., i:j], s[..., i:j], least(S, e[..., i - R:j - R]))
            y, p, n = s[..., i:j], x[..., i:j], nx[..., i:j]; b = st[..., i:j]
            b = np.where(b > 0, b, np.where(np.all(y >= p, axis=2), 1, np.where(np.all(y >= n, axis=2), 2, 0)))
            st[..., i:j] = b; b = b[:, :, None]
            S[..., 2 * i:2 * j:2] = np.where(b == 0, np.maximum(y, p), np.where(b == 1, y, 255))
            S[..., 2 * i + 1:2 * j:2] = np.where(b == 0, np.maximum(y, n), np.where(b == 2, y, 255))
        gs = least(S, e[..., V - R:])
        for l in range(L, -1, -1):
            i, j = AT[l], AT[l + 1]; p, n = x[..., i:j], nx[..., i:j]; b = st[..., i:j]
            A = np.take_along_axis(C, a[:, :, :1, i:j], 3); B = np.take_along_axis(C, a[:, :, 1:, i:j], 3)
            b = np.where(b > 0, b, np.where(~np.all(A >= p, axis=2), 1, np.where(~np.all(B >= n, axis=2), 2, 0)))
            st[..., i:j] = b; b = b[:, :, None]
            C[..., i:j] = np.where(b == 1, A, np.where(b == 2, B, np.maximum(np.where(p > 0, 0, A), np.where(n > 0, 0, B))))
    return {"yc": np.ascontiguousarray(C[..., :V]).reshape(N, 128, V).astype(np.float32).astype(BF), "ys": np.concatenate([s, gs], axis=3).reshape(N, 128, V + R).astype(np.float32).astype(BF)}

@@ -1,0 +1,553 @@
+from concourse.mybir import AluOpType as A, AxisListType, ActivationFunctionType as AF
+
+R, M, V, F, RO = 256, 768, 1792, 512, 3
+E = 2 * V
+W = 256
+U = 64
+BF, F4, I4, U2 = "bfloat16", "float32", "int32", "uint16"
+
+SCRATCH = {}
+
+
+def _b(name, n, d=BF):
+    SCRATCH[name] = ("sbuf", [128, n], d)
+
+
+for _n in ("one", "I", "tb", "ON", "PM", "t1", "t2", "LO", "HI", "E0", "E8", "g1", "g2", "GA", "GB", "QA", "QB", "QF", "HA", "HB", "NB", "PB", "JN", "ksi"):
+    _b(_n, 128)
+_b("P32", 128, F4); _b("J32", 128, F4); _b("sela", 2048, F4); _b("pw", 1, F4)
+_b("R1", 32 * U); _b("R2", 32 * U)
+_b("x", V); _b("s", V); _b("ui", V, I4); _b("pi", 224, I4); _b("po", 224, U2)
+_b("ou", V, U2); _b("ov1", 1024, U2); _b("ov2", 1024, U2)
+_b("lt0", 1552, F4); _b("lt1", 1552, F4); _b("lg0", 256, F4); _b("lg1", 256, F4)
+_b("S1", 528); _b("S2", 3600); _b("S3", 3600); _b("K2", 3600); _b("K3", 3600)
+for _r in range(RO):
+    _b("C%d" % _r, V + R + F); _b("sa%d" % _r, R); _b("gs%d" % _r, R)
+_b("ga", 16 * M); _b("sc", 16 * M); _b("kg", 16 * 384); _b("ks", 16 * M)
+_b("fd", V); _b("dm", V)
+for _i in range(3):
+    _b("v%d" % _i, 512); _b("z%d" % _i, 512); _b("ab%d" % _i, 512); _b("tm%d" % _i, 256)
+_b("th", 1024); _b("P", 1024, F4); _b("tg", 1024, F4); _b("lm", 1024); _b("hm", 1024); _b("ch", 1024); _b("nl", 1024, F4)
+_b("w1", 64, I4); _b("w2", 64, I4); _b("wu", 64, U2)
+BANKS = ["b%d" % _i for _i in range(8)]
+for _n in BANKS:
+    SCRATCH[_n] = ("psum", [128, 512], F4)
+ND = 64
+SEMAPHORES = ["eV", "eS", "eP", "eG"] + ["d%d" % _i for _i in range(ND)] + ["%s%d" % (_p, _r) for _p in ("ra", "rb", "la", "lb") for _r in range(RO - 1)]
+EXT = {"piv": BF, "safe": BF, "lem": BF, "leaf": BF, "uses": I4, "prem": I4, "yc": BF, "ys": BF}
+
+CYC, XLAT = 0.83, 150.0
+PEN, SLACK, FAC = 8000.0, 150.0, (0.6, 0.7)
+
+
+def _psum(v):
+    return v[0] in BANKS
+
+
+def _two(v):
+    return (SCRATCH[v[0]][2] if v[0] in SCRATCH else EXT[v[0]]) in (BF, U2)
+
+
+def _hi(v):
+    return v[1] + (v[2] - 1) * v[3] + 1
+
+
+def _over(a, b):
+    if a[0] >= b[1] or b[0] >= a[1]:
+        return False
+    return not (a[2] == b[2] and a[2] > 1 and (a[0] - b[0]) % a[2])
+
+
+def _covers(a, b):
+    return a[0] <= b[0] and a[1] >= b[1] and (a[2] == 1 or (a[2] == b[2] and (a[0] - b[0]) % a[2] == 0))
+
+
+def _program():
+    ops, bufs, last, nd = [], {}, {}, [0]
+
+    def add(kind, engs, cost, reads, writes, **kw):
+        i = len(ops)
+        preds = {}
+        for v in reads:
+            reg = (v[1], _hi(v), v[3]); b = bufs.setdefault(v[0], {"w": [], "r": []})
+            for (q, j) in b["w"]:
+                if _over(q, reg):
+                    preds[j] = True
+        for v in writes:
+            reg = (v[1], _hi(v), v[3]); b = bufs.setdefault(v[0], {"w": [], "r": []})
+            for (q, j) in b["w"]:
+                if _over(q, reg):
+                    preds[j] = True
+            for (q, j) in b["r"]:
+                if _over(q, reg):
+                    preds.setdefault(j, False)
+        for v in list(reads) + list(writes):
+            if _psum(v) and v[0] in last and last[v[0]] != i:
+                preds.setdefault(last[v[0]], None)
+        for v in list(reads) + list(writes):
+            if _psum(v):
+                last[v[0]] = i
+        preds.pop(i, None)
+        for v in writes:
+            reg = (v[1], _hi(v), v[3]); b = bufs[v[0]]
+            b["w"] = [z for z in b["w"] if not _covers(reg, z[0])] + [(reg, i)]
+            b["r"] = [z for z in b["r"] if not _covers(reg, z[0])]
+        for v in reads:
+            bufs[v[0]]["r"].append(((v[1], _hi(v), v[3]), i))
+        op = {"kind": kind, "engs": engs, "cost": cost, "preds": preds, "id": i, "lat": 0.0, "sem": None}
+        op.update(kw)
+        ops.append(op)
+        return i
+
+    def c(name, lo, n, st=1):
+        return (name, lo, n, st)
+
+    def all_(name):
+        return (name, 0, SCRATCH[name][1][1], 1)
+
+    def dma(out, in_):
+        k = nd[0]; nd[0] += 1
+        n = max(out[2], in_[2]) * (2 if _two(out) else 4)
+        add("dma", ("Y",), 60.0, [in_], [out], out=out, in_=in_, lat=2000.0 + n * 128 / 150.0, sem=("d%d" % k, 16))
+
+    def memset(out, val):
+        add("memset", ("V",), 60 + out[2] * CYC * (.5 if _two(out) else 1), [], [out], out=out, val=val)
+
+    def tt(out, a, b, op):
+        add("tt", ("V",), 60 + out[2] * CYC * (1 if _psum(a) or _psum(b) else 2), [a, b], [out], out=out, a=a, b=b, op=op)
+
+    def _fast(out, a):
+        return .5 if _two(out) and _two(a) and not _psum(a) else 1
+
+    def ts(out, a, s1, op0, s2=None, op1=None):
+        rd = [a] + ([s1] if isinstance(s1, tuple) else [])
+        add("ts", ("V",), 60 + out[2] * CYC * _fast(out, a), rd, [out], out=out, a=a, s1=s1, s2=s2, op0=op0, op1=op1)
+
+    def vcopy(out, a):
+        add("vcopy", ("V",), 60 + out[2] * CYC * _fast(out, a), [a], [out], out=out, a=a)
+
+    def act(out, a, func, scale=1.0, bias=0.0):
+        add("act", ("S",), 70 + out[2] * CYC, [a], [out], out=out, a=a, func=func, scale=scale, bias=bias)
+
+    def either(out, a, func, scale, bias, s1, op0, s2=None, op1=None):
+        add("either", ("S", "V"), 70 + out[2] * CYC, [a], [out], out=out, a=a, func=func, scale=scale, bias=bias, s1=s1, op0=op0, s2=s2, op1=op1)
+
+    def ecopy(out, a):
+        add("ecopy", ("S", "V"), 65 + out[2] * CYC, [a], [out], out=out, a=a)
+
+    def scan(out, d0, d1, op0, op1):
+        add("scan", ("V",), 60 + out[2] * CYC * .5, [d0, d1], [out], out=out, d0=d0, d1=d1, op0=op0, op1=op1)
+
+    def gather(out, win, off):
+        add("gather", ("S", "V"), 60 + out[2] * CYC * 1.5, [win, off], [out], out=out, win=win, off=off)
+
+    def mm(out, lhs, rhs, start, stop, fp=False):
+        add("mm", ("P",), 30 + max(64, out[2]) * .75 * (4 if fp else 1), [lhs, rhs], [out], out=out, lhs=lhs, rhs=rhs, start=start, stop=stop)
+
+    def group(out, terms, fp=False):
+        for k, (l, r) in enumerate(terms):
+            mm(out, all_(l), r, k == 0, k == len(terms) - 1, fp)
+
+    def asel(out, in_, pat, op, base, cm):
+        add("asel", ("G",), 170 + out[2] * CYC * 2, [in_], [out], out=out, in_=in_, pat=pat, op=op, base=base, cm=cm)
+
+    def fill(out, val):
+        add("iota", ("G",), 130 + out[2] * CYC * 2, [], [out], out=out, val=val)
+
+    dma(c("s", 0, R), c("safe", 0, R))
+    dma(c("x", 0, R), c("piv", 0, R))
+    dma(c("ui", 0, M), c("uses", 0, M))
+    dma(c("x", R, V - R), c("piv", R, V - R))
+    dma(c("ui", M, 1024), c("uses", M, 1024))
+    dma(all_("pi"), c("prem", 0, 224))
+    dma(c("C0", V, R), c("lem", 0, R))
+    for r in range(RO):
+        dma(c("C%d" % r, V + R, F), c("leaf", 0, F))
+    memset(all_("one"), 1.0)
+    asel(all_("I"), all_("one"), [[-1, 128]], A.is_equal, 0, 1)
+    asel(all_("tb"), all_("one"), [[-16, 8], [0, 16]], A.is_ge, 0, 1)
+    asel(all_("ON"), all_("tb"), [[16, 8], [0, 16]], A.is_ge, 15, -1)
+    asel(all_("t1"), all_("ON"), [[-1, 128]], A.is_equal, -8, 1)
+    asel(all_("t2"), all_("ON"), [[-1, 128]], A.is_equal, 8, 1)
+    tt(all_("PM"), all_("t1"), all_("t2"), A.add)
+
+    def half(out, in_, h):
+        asel(all_(out), all_(in_), [[0, 8], [1, 2], [0, 8]], A.is_equal, -h, 0)
+
+    def mix(out, a, b):
+        ts(all_("g1"), all_("E0"), float(a), A.mult)
+        ts(all_("g2"), all_("E8"), float(b), A.mult)
+        tt(all_(out), all_("g1"), all_("g2"), A.add)
+    half("LO", "ON", 0)
+    half("HI", "ON", 1)
+    asel(all_("E0"), all_("ON"), [[-16, 8], [0, 16]], A.is_equal, 0, 1)
+    asel(all_("E8"), all_("ON"), [[-16, 8], [0, 16]], A.is_equal, -8, 1)
+    mix("GA", -2048, 1024)
+    ts(all_("GB"), all_("GA"), -1.0, A.mult)
+    tt(all_("QB"), all_("HI"), all_("LO"), A.subtract)
+    ts(all_("QA"), all_("QB"), -32.0, A.mult)
+    half("t1", "GA", 0)
+    half("t2", "GA", 1)
+    tt(all_("QF"), all_("t2"), all_("t1"), A.subtract)
+    mix("HA", -256, 256)
+    ts(all_("HB"), all_("HA"), -1.0, A.mult)
+    mix("PB", 128, 128)
+    ts(all_("NB"), all_("PB"), -1.0, A.mult)
+    ts(all_("JN"), all_("ON"), -1.0, A.mult)
+    memset(all_("R1"), 0.0); memset(c("R1", 0, 2 * U, 16), 255.0)
+    fill(c("S1", 512, 16), 255); fill(c("S2", 2048, 1552), 255); fill(c("S3", E, 16), 255)
+    for k in range(3):
+        ts(c("ou", k * W, W), c("ui", k * W, W), 512, A.min)
+    for k in range(3, 7):
+        vcopy(c("ou", k * W, W), c("ui", k * W, W))
+    for n0, w, t in ((1024, 768, 1792), (256, 768, 1024), (0, 256, 256)):
+        for h in (0, 112):
+            k = h + n0 // 16
+            ts(c("po", k, w // 16), c("pi", k, w // 16), -t, A.add)
+    fill(c("K2", 0, 512), 0); fill(c("K2", 2048, 1552), 0); fill(c("K3", 0, 512), 0); fill(c("K3", E, 16), 0)
+
+    def late():
+        memset(all_("R2"), 2.0); memset(c("R2", 0, 2 * U, 16), 0.0)
+        scan(all_("ksi"), c("R2", 0, 128), all_("I"), A.mult, A.max)
+        add("red", ("V",), 80.0, [c("ksi", 15, 8, 16)], [all_("pw")], out=all_("pw"), a=c("ksi", 15, 8, 16))
+        vcopy(all_("P32"), all_("PM"))
+        ts(all_("J32"), all_("I"), -1.0, A.mult)
+        fill(all_("sela"), 1)
+        asel(all_("sela"), all_("sela"), [[1, 16], [0, 8], [-1, 16]], A.is_equal, 0, 0)
+        asel(all_("sela"), all_("sela"), [[0, 16], [-16, 8], [0, 16]], A.is_ge, 0, 1)
+        asel(all_("sela"), all_("sela"), [[0, 16], [16, 8], [0, 16]], A.is_ge, 15, -1)
+        for k in range(6):
+            ts(c("lt0", k * W, W), c("ui", k * W, W), -1.0, A.mult, float(E), A.add)
+        ts(all_("lg0"), c("ui", 1536, W), -1.0, A.mult, float(E), A.add)
+        memset(c("lt0", 1536, 16), 0.0); memset(c("lt1", 1536, 16), 0.0)
+        dma(c("lt1", 0, M), c("lt0", 0, M))
+
+    def lists(win, off, o0, n, gbuf, sbuf, g0, pat, op0, op1):
+        size = SCRATCH[gbuf][1][1]
+        for k in range(0, n, 2 * U):
+            at = (g0 + k) * 16 % size
+            for h in (0, U):
+                gather(c(gbuf, at + 16 * h, 16 * U), win, c(off, o0 + k + h, U))
+            scan(c(sbuf, (g0 + k) * 16, 32 * U), all_(pat), c(gbuf, at, 32 * U), op0, op1)
+
+    def premises(r, n0, stream):
+        lo = 256 if n0 < R else 1024 if n0 < 1024 else 1792
+        win = c("C%d" % r, lo, V + R + F - lo)
+        for h in (0, 1):
+            gather(c("ab%d" % stream, h * W, W), win, c("po", 112 * h + n0 // 16, W // 16))
+
+    def down(r, n0, stream, Mv):
+        p, q = "b%d" % (2 * stream), "b%d" % (2 * stream + 1)
+        x, s, v = c("x", n0, W), c("s", n0, W), "v%d" % stream
+        if r:
+            dm = c("dm", n0, W)
+            group(c(q, 0, W), [("I", s), ("NB", dm)])
+            group(c(q, W, W), [("I", s), ("PB", dm)])
+            group(c(p, 0, W), [("I", x), ("HA", dm)])
+            group(c(p, W, W), [("PM", x), ("HB", dm)])
+            tm = c("tm%d" % stream, 0, W)
+            tt(tm, Mv, c(q, 0, W), A.min)
+            tt(s, tm, c(q, W, W), A.max)
+        else:
+            group(c(p, 0, W), [("I", x)])
+            group(c(p, W, W), [("PM", x)])
+            if Mv is not None:
+                ecopy(s, Mv)
+        tt(c(v, 0, W), s, c(p, 0, W), A.is_lt)
+        tt(c(v, W, W), s, c(p, W, W), A.is_lt)
+        group(c(q, 0, W), [("LO", c(v, 0, W)), ("HI", c(v, W, W))])
+        if n0 >= 1024:
+            premises(r, n0, stream)
+            tt(c("z%d" % stream, 0, 2 * W), c("ab%d" % stream, 0, 2 * W), c(p, 0, 2 * W), A.is_lt)
+        fd = c("fd", n0, W)
+        either(fd, c(q, 0, W), AF.Relu, -1.0, 1.0, 0.0, A.is_equal)
+        group(c(p, 0, W), [("I", x), ("GA", fd)])
+        group(c(p, W, W), [("PM", x), ("GB", fd)])
+        t = "S1" if n0 < R else "S2" if n0 < 1024 else "S3"
+        tt(c(t, 2 * n0, W, 2), s, c(p, 0, W), A.max)
+        tt(c(t, 2 * n0 + 1, W, 2), s, c(p, W, W), A.max)
+
+    def up(r, n0, stream):
+        p, q = "b%d" % (2 * stream), "b%d" % (2 * stream + 1)
+        x, fd, dm = c("x", n0, W), c("fd", n0, W), c("dm", n0, W)
+        ab, v, C = "ab%d" % stream, "v%d" % stream, "C%d" % r
+        if n0 >= 1024:
+            v = "z%d" % stream
+        else:
+            group(c(p, 0, W), [("I", x)])
+            group(c(p, W, W), [("PM", x)])
+            premises(r, n0, stream)
+            tt(c(v, 0, 2 * W), c(ab, 0, 2 * W), c(p, 0, 2 * W), A.is_lt)
+        group(c(q, 0, W), [("QA", c(v, 0, W)), ("QB", c(v, W, W)), ("QF", fd)])
+        act(dm, c(q, 0, W), AF.Sign, 1.0, -0.5)
+        group(c(p, 0, W), [("I", x), ("HA", dm)])
+        group(c(p, W, W), [("PM", x), ("HB", dm)])
+        if r < RO - 1 and n0 >= R:
+            k = "K2" if n0 < 1024 else "K3"
+            act(c(k, 2 * n0 + 1, W, 2), c(p, 0, W), AF.Sign, 1.0, -255.5)
+            act(c(k, 2 * n0, W, 2), c(p, W, W), AF.Sign, 1.0, -255.5)
+        either(c(p, 0, 2 * W), c(p, 0, 2 * W), AF.Relu, -1024.0, 512.0, 0.0, A.is_le, 512.0, A.mult)
+        tm = c("tm%d" % stream, 0, W)
+        tt(tm, c(ab, 0, W), c(p, 0, W), A.min)
+        tt(c(p, W, W), c(ab, W, W), c(p, W, W), A.min)
+        tt(c(C, n0, W), tm, c(p, W, W), A.max)
+        if r == RO - 1:
+            dma(c("yc", n0, W), c(C, n0, W))
+
+    def kscan(r, part):
+        off, o0 = ("ou", M) if r == 1 else ("ov1", 0)
+        if part == 0:
+            lists(all_("K2"), off, o0, M, "kg", "ks", 0, "R2", A.mult, A.max)
+        else:
+            lists(all_("K3"), off, o0 + M, R, "kg", "ks", 0, "R2", A.mult, A.max)
+
+    def splice(r, part):
+        lt, ov = "lt%d" % (r - 1), "ov%d" % r
+        c0, n = (0, M) if part == 0 else (M, R)
+
+        def L(k):
+            return c(lt, M + k, W) if part == 0 else c("lg%d" % (r - 1), k, W)
+        for k in range(0, n, W):
+            ts(c("th", c0 + k, W), c("ks", 16 * k + 15, W, 16), all_("pw"), A.is_equal)
+            tt(c("P", c0 + k, W), c("th", c0 + k, W), L(k), A.mult)
+        w = c("b6", 0, n // 16); wo = c0 // 16; m = n // 16
+        for q in range(16):
+            mm(w, c("sela", 128 * q, 128), c("P", c0 + q, m, 16), q == 0, q == 15, True)
+        ts(c("w1", wo, m), w, -1.0, A.mult, float(E - 512), A.add)
+        ts(c("w2", wo, m), c("w1", wo, m), 1, A.arith_shift_right)
+        vcopy(c("wu", wo, m), c("w2", wo, m))
+        for k in range(0, n, W):
+            gather(c("tg", c0 + k, W), all_(lt), c("wu", wo + k // 16, 16))
+        for k in range(0, n, W):
+            z = "b%d" % (7 - (k // W) % 2)
+            P, lm, hm = c("P", c0 + k, W), c("lm", c0 + k, W), c("hm", c0 + k, W)
+            group(c(z, 0, W), [("P32", c("tg", c0 + k, W)), ("J32", P)], fp=True)
+            tt(lm, P, c(z, 0, W), A.min)
+            tt(hm, L(k), c(z, 0, W), A.min)
+            group(c(z, W, W), [("ON", hm), ("JN", lm)])
+            either(c("ch", c0 + k, W), c(z, W, W), AF.Relu, -1.0, 1.0, 0.0, A.is_equal)
+            tt(c("tg", c0 + k, W), c("ch", c0 + k, W), c(z, 0, W), A.mult)
+            if r == 1:
+                nl = c("lt1", M + k, W) if part == 0 else c("lg1", k, W)
+            else:
+                nl = c("nl", c0 + k, W)
+            tt(nl, c("tg", c0 + k, W), L(k), A.add)
+            ts(c(ov, c0 + k, W), nl, -1.0, A.mult, float(E), A.add)
+
+    def send(src, dst, lo, to, rs, ls):
+        j = add("send", ("G",), 300.0, [src], [], src=src, dst=dst, at=(lo, lo + R), to=to, rs=rs, lat=2500.0, sem=(ls, 8))
+        add("arrive", ("R",), 0.0, [], [c(dst, lo, R)], lat=1000.0, sem=(rs, 8), after=j)
+
+    for r in range(RO):
+        off2, o2 = ("ou", M) if r == 0 else ("ov%d" % r, 0)
+        if r:
+            kscan(r, 0)
+        down(r, 0, 0, None if r == 0 else all_("sa%d" % r))
+        dma(c("S2", 0, 512), c("S1", 0, 512))
+        if r:
+            splice(r, 0)
+        for k in range(3):
+            lists(all_("S1"), "ou", k * W, W, "ga", "sc", k * W, "R1", A.max, A.min)
+            down(r, R + k * W, (k + 1) % 3, c("sc", 16 * k * W + 15, W, 16))
+        dma(c("S3", 0, 2048), c("S2", 0, 2048))
+        if r == 0:
+            late()
+        else:
+            kscan(r, 1)
+            splice(r, 1)
+        for k in range(3):
+            lists(all_("S2"), off2, o2 + k * W, W, "ga", "sc", k * W, "R1", A.max, A.min)
+            down(r, 1024 + k * W, k, c("sc", 16 * k * W + 15, W, 16))
+        if r == RO - 1:
+            for k in range(7):
+                dma(c("ys", k * W, W), c("s", k * W, W))
+        lists(all_("S3"), off2, o2 + M, R, "ga", "sc", 0, "R1", A.max, A.min)
+        gs = all_("gs%d" % r)
+        ecopy(gs, c("sc", 15, R, 16))
+        if r < RO - 1:
+            send(gs, "sa%d" % (r + 1), 0, 1, "ra%d" % r, "la%d" % r)
+        else:
+            dma(c("ys", V, R), gs)
+        for k in range(3):
+            up(r, 1024 + k * W, k)
+        for k in range(3):
+            up(r, R + k * W, k)
+        if r < RO - 1:
+            dma(c("K3", 512, 1536), c("K2", 512, 1536))
+        up(r, 0, 0)
+        if r < RO - 1:
+            send(c("C%d" % r, 0, R), "C%d" % (r + 1), V, -1, "rb%d" % r, "lb%d" % r)
+    return ops
+
+
+def _schedule(ops):
+    n = len(ops)
+    for o in ops:
+        if "after" in o:
+            o["preds"].setdefault(o["after"], False)
+    succ = [[] for _ in range(n)]
+    left = [len(o["preds"]) for o in ops]
+    for o in ops:
+        for p in o["preds"]:
+            succ[p].append(o["id"])
+    rank = [0.0] * n
+    for i in range(n - 1, -1, -1):
+        o = ops[i]
+        acc, best = 0.0, 0.0
+        for j in sorted(succ[i], key=lambda j: -rank[j]):
+            best = max(best, rank[j] + 100 + acc)
+            acc += ops[j]["cost"] * FAC[ops[j]["kind"] == "gather"]
+        rank[i] = o["cost"] + o["lat"] + best
+    free = {"V": 0.0, "S": 0.0, "P": 0.0, "G": 0.0, "Y": 0.0, "R": 0.0}
+    done, eng, order = [0.0] * n, [None] * n, []
+    ready = [i for i in range(n) if left[i] == 0]
+    while ready:
+        cand, first = [], 1e18
+        for i in ready:
+            o = ops[i]
+            for e in o["engs"]:
+                t = free[e]
+                for p, hard in o["preds"].items():
+                    d = done[p]
+                    if eng[p] != e or ops[p]["sem"]:
+                        d += XLAT
+                    elif hard is not None and e != "P":
+                        d += 60.0
+                    if d > t:
+                        t = d
+                cand.append((t, i, e))
+                if t < first:
+                    first = t
+        best = None
+        for t, i, e in cand:
+            if t <= first + SLACK:
+                pr = rank[i]
+                if len(ops[i]["engs"]) > 1 and e == "V":
+                    pr -= PEN if ops[i]["kind"] == "gather" else PEN * 0.3
+                if best is None or pr > best[0] or (pr == best[0] and t < best[1]):
+                    best = (pr, t, i, e)
+        pr, t, i, e = best
+        o = ops[i]
+        eng[i] = e
+        if e != "R":
+            free[e] = t + o["cost"]
+        done[i] = t + o["cost"] + o["lat"]
+        order.append(i)
+        ready.remove(i)
+        for j in succ[i]:
+            left[j] -= 1
+            if left[j] == 0:
+                ready.append(j)
+    return order, eng, max(done)
+
+
+def _waits(ops, order, eng):
+    pos = {i: k for k, i in enumerate(order)}
+    count = {"V": 0, "S": 0, "P": 0, "G": 0}
+    know = {e: {} for e in "VSPGYR"}
+    sem, clock, need, final, waited = {}, {}, {}, {}, {}
+    for i in order:
+        o, e = ops[i], eng[i]
+        k = know[e]
+        w = {}
+        if e != "R":
+            ps = [p for p, hard in o["preds"].items() if ops[p]["sem"] or eng[p] != e or (hard is not None and e != "P")]
+            ps.sort(key=lambda p: -pos[p])
+            for p in ps:
+                s, val = sem[p]
+                if k.get(s, 0) >= val:
+                    continue
+                w[s] = max(w.get(s, 0), val)
+                k[s] = val
+                for a, b in clock[p].items():
+                    if k.get(a, 0) < b:
+                        k[a] = b
+        need[i] = sorted(w.items())
+        for s, val in w.items():
+            waited[s] = max(waited.get(s, 0), val)
+        if o["sem"]:
+            sem[i] = o["sem"]
+        else:
+            count[e] += 1
+            sem[i] = ("e" + e, count[e])
+        final[sem[i][0]] = max(final.get(sem[i][0], 0), sem[i][1])
+        clock[i] = dict(k) if e != "R" else {}
+    tail = [(s, v) for s, v in sorted(final.items()) if waited.get(s, 0) < v]
+    return need, sem, tail
+
+
+_PLAN = {}
+
+
+def _plan():
+    if not _PLAN:
+        ops = _program()
+        order, eng, est = _schedule(ops)
+        need, sem, tail = _waits(ops, order, eng)
+        _PLAN.update({"ops": ops, "order": order, "eng": eng, "need": need, "sem": sem, "tail": tail, "est": est})
+    return _PLAN
+
+
+def rank_program(g, core, T, topo):
+    rank = T.rank_of(core)
+    if rank is None:
+        return
+    pl = _plan()
+    queue = {"V": g.vector, "S": g.scalar, "P": g.tensor, "G": g, "Y": g.sync}
+
+    def ap(v):
+        if v[3] == 1:
+            return T[v[0]][:, v[1]:v[1] + v[2]]
+        return T[v[0]][:, v[1]:_hi(v):v[3]]
+
+    for i in pl["order"]:
+        o, e = pl["ops"][i], pl["eng"][i]
+        if e == "R":
+            continue
+        q = queue[e]
+        for s, val in pl["need"][i]:
+            q.wait_ge(T.sem[s], val)
+        kind = o["kind"]
+        s, val = pl["sem"][i]
+        if kind == "send":
+            dst = T.cores[(rank + o["to"]) % len(T.cores)]
+            rid, pid, se = topo.addr(dst)
+            g.remote_dma(out_ap=T[o["dst"]][:, o["at"][0]:o["at"][1]], in_ap=ap(o["src"]), remote_sem=T.sem[o["rs"]], local_sem=T.sem[s],
+                         pid=pid, routing_id=rid, dma_engine_mask=topo.mask(core, dst))
+            continue
+        if kind == "dma":
+            q.dma_start(out=ap(o["out"]), in_=ap(o["in_"])).then_inc(T.sem[s], 16)
+            continue
+        out = ap(o["out"])
+        if kind == "memset":
+            x = q.memset(out, o["val"])
+        elif kind == "tt":
+            x = q.tensor_tensor(out, ap(o["a"]), ap(o["b"]), o["op"])
+        elif kind == "ts" or (kind == "either" and e == "V"):
+            s1 = ap(o["s1"]) if isinstance(o["s1"], tuple) else o["s1"]
+            if o["op1"] is None:
+                x = q.tensor_scalar(out, ap(o["a"]), s1, None, o["op0"])
+            else:
+                x = q.tensor_scalar(out, ap(o["a"]), s1, o["s2"], o["op0"], o["op1"])
+        elif kind == "vcopy" or (kind == "ecopy" and e == "V"):
+            x = q.tensor_copy(out, ap(o["a"]))
+        elif kind == "ecopy":
+            x = q.activation(out, ap(o["a"]), AF.Copy)
+        elif kind == "act" or kind == "either":
+            x = q.activation(out, ap(o["a"]), o["func"], bias=o["bias"], scale=o["scale"])
+        elif kind == "scan":
+            x = q.tensor_tensor_scan(out, ap(o["d0"]), ap(o["d1"]), 0.0, o["op0"], o["op1"])
+        elif kind == "red":
+            x = q.tensor_reduce(out, ap(o["a"]), AxisListType.X, A.max)
+        elif kind == "gather":
+            src = ap(o["win"]).indirect(ap(o["off"]))
+            x = q.tensor_copy(out, src) if e == "V" else q.activation(out, src, AF.Copy)
+        elif kind == "mm":
+            x = q.matmul(out, ap(o["lhs"]), ap(o["rhs"]), o["start"], o["stop"])
+        elif kind == "asel":
+            x = q.affine_select(out, ap(o["in_"]), o["pat"], o["op"], 0.0, o["base"], o["cm"])
+        else:
+            x = q.iota(out, [[0, o["out"][2]]], o["val"], 0, allow_small_or_imprecise_dtypes=True)
+        x.then_inc(T.sem[s], 1)
+    for s, val in pl["tail"]:
+        g.wait_ge(T.sem[s], val)

@@ -2,9 +2,15 @@ from concourse.mybir import AluOpType as A, AxisListType, ActivationFunctionType
 
 R, M, V, F, RO = 256, 768, 1792, 512, 3
 E = 2 * V
+H = V
 W = 256
 U = 64
-BF, F4, I4, U2 = "bfloat16", "float32", "int32", "uint16"
+BF, F2, F4, I4, U2 = "bfloat16", "float16", "float32", "int32", "uint16"
+BIG = 8192.0
+
+ONE = ((4, 5), (1, 4, 5, 6), (1, 4, 5, 6))
+STEST = ()
+EARLY, GHOST, KU = True, 1, 32
 
 SCRATCH = {}
 
@@ -13,22 +19,25 @@ def _b(name, n, d=BF):
     SCRATCH[name] = ("sbuf", [128, n], d)
 
 
-for _n in ("one", "I", "tb", "ON", "PM", "t1", "t2", "LO", "HI", "E0", "E8", "g1", "g2", "GA", "GB", "QA", "QB", "QF", "HA", "HB", "NB", "PB", "JN", "ksi"):
+for _n in ("I", "tb", "ON", "PM", "t1", "t2", "DL", "DH", "LO", "HI", "B", "g1", "g2", "g3", "g4", "GA", "QA", "QB", "QF", "HA", "HB", "NB", "PB",
+           "NON", "NI", "CF", "C1m", "C2m", "BON", "NBON"):
     _b(_n, 128)
-_b("P32", 128, F4); _b("J32", 128, F4); _b("sela", 2048, F4); _b("pw", 1, F4)
-_b("R1", 32 * U); _b("R2", 32 * U)
-_b("x", V); _b("s", V); _b("ui", V, I4); _b("pi", 224, I4); _b("po", 224, U2)
-_b("ou", V, U2); _b("ov1", 1024, U2); _b("ov2", 1024, U2)
-_b("lt0", 1552, F4); _b("lt1", 1552, F4); _b("lg0", 256, F4); _b("lg1", 256, F4)
-_b("S1", 528); _b("S2", 3600); _b("S3", 3600); _b("K2", 3600); _b("K3", 3600)
+_b("D2", 128, F4); _b("one", W); _b("sg", 1, F4)
+_b("WF", 2048); _b("sa", 2048); _b("w0", 64, F4)
+_b("R8", 1024); _b("R16", 1024)
+_b("x", V); _b("s", V); _b("zi", V); _b("ui", V, I4); _b("pi", 224, I4); _b("po", 224, U2)
+_b("oF", M, U2); _b("oN", M, U2); _b("OL", M, F2)
 for _r in range(RO):
-    _b("C%d" % _r, V + R + F); _b("sa%d" % _r, R); _b("gs%d" % _r, R)
-_b("ga", 16 * M); _b("sc", 16 * M); _b("kg", 16 * 384); _b("ks", 16 * M)
-_b("fd", V); _b("dm", V)
+    _b("ov%d" % _r, 1024, U2); _b("O%d" % _r, 1024, F2)
+    _b("C%d" % _r, V + R + F); _b("ar%d" % _r, R); _b("gs%d" % _r, R)
+_b("lt0", 1552, F4); _b("lt1", 1552, F4)
+_b("S1", 528); _b("S2", 3600); _b("S3", 3600); _b("K", 3600)
+_b("ga", 16 * M); _b("sc", 16 * M); _b("kg", 48 * W)
+_b("fd", V); _b("d0", R)
 for _i in range(3):
     _b("v%d" % _i, 512); _b("z%d" % _i, 512); _b("ab%d" % _i, 512); _b("tm%d" % _i, 256)
-_b("th", 1024); _b("P", 1024, F4); _b("tg", 1024, F4); _b("lm", 1024); _b("hm", 1024); _b("ch", 1024); _b("nl", 1024, F4)
-_b("w1", 64, I4); _b("w2", 64, I4); _b("wu", 64, U2)
+_b("Ox", 1024, F2); _b("tg", 1024, F2); _b("cc", 1024, F2); _b("mm", 1024, F2)
+_b("w1", 64, I4); _b("wu", 64, U2)
 BANKS = ["b%d" % _i for _i in range(8)]
 for _n in BANKS:
     SCRATCH[_n] = ("psum", [128, 512], F4)
@@ -36,7 +45,7 @@ ND = 64
 SEMAPHORES = ["eV", "eS", "eP", "eG"] + ["d%d" % _i for _i in range(ND)] + ["%s%d" % (_p, _r) for _p in ("ra", "rb", "la", "lb") for _r in range(RO - 1)]
 EXT = {"piv": BF, "safe": BF, "lem": BF, "leaf": BF, "uses": I4, "prem": I4, "yc": BF, "ys": BF}
 
-CYC, XLAT = 0.83, 150.0
+CYC, XLAT, GCY, PCY = 0.83, 150.0, 1.5, 0.6
 PEN, SLACK, FAC = 8000.0, 150.0, (0.6, 0.7)
 
 
@@ -45,7 +54,7 @@ def _psum(v):
 
 
 def _two(v):
-    return (SCRATCH[v[0]][2] if v[0] in SCRATCH else EXT[v[0]]) in (BF, U2)
+    return (SCRATCH[v[0]][2] if v[0] in SCRATCH else EXT[v[0]]) in (BF, F2, U2)
 
 
 def _hi(v):
@@ -65,7 +74,7 @@ def _covers(a, b):
 def _program():
     ops, bufs, last, nd = [], {}, {}, [0]
 
-    def add(kind, engs, cost, reads, writes, **kw):
+    def add(kind, engs, cyc, reads, writes, **kw):
         i = len(ops)
         preds = {}
         for v in reads:
@@ -94,7 +103,7 @@ def _program():
             b["r"] = [z for z in b["r"] if not _covers(reg, z[0])]
         for v in reads:
             bufs[v[0]]["r"].append(((v[1], _hi(v), v[3]), i))
-        op = {"kind": kind, "engs": engs, "cost": cost, "preds": preds, "id": i, "lat": 0.0, "sem": None}
+        op = {"kind": kind, "engs": engs, "cyc": cyc, "preds": preds, "id": i, "lat": 0.0, "sem": None}
         op.update(kw)
         ops.append(op)
         return i
@@ -105,54 +114,62 @@ def _program():
     def all_(name):
         return (name, 0, SCRATCH[name][1][1], 1)
 
-    def dma(out, in_):
-        k = nd[0]; nd[0] += 1
-        n = max(out[2], in_[2]) * (2 if _two(out) else 4)
-        add("dma", ("Y",), 60.0, [in_], [out], out=out, in_=in_, lat=2000.0 + n * 128 / 150.0, sem=("d%d" % k, 16))
-
-    def memset(out, val):
-        add("memset", ("V",), 60 + out[2] * CYC * (.5 if _two(out) else 1), [], [out], out=out, val=val)
-
-    def tt(out, a, b, op):
-        add("tt", ("V",), 60 + out[2] * CYC * (1 if _psum(a) or _psum(b) else 2), [a, b], [out], out=out, a=a, b=b, op=op)
-
     def _fast(out, a):
         return .5 if _two(out) and _two(a) and not _psum(a) else 1
 
+    def dma(out, in_):
+        k = nd[0]; nd[0] += 1
+        n = max(out[2], in_[2]) * (2 if _two(out) else 4)
+        add("dma", "Y", {"Y": (60, 0, 0, 0)}, [in_], [out], out=out, in_=in_, lat=2000.0 + n * 128 / 150.0, sem=("d%d" % k, 16))
+
+    def memset(out, val):
+        add("memset", "V", {"V": (60, out[2] * (.5 if _two(out) else 1), 0, 0)}, [], [out], out=out, val=val)
+
+    def tt(out, a, b, op):
+        add("tt", "V", {"V": (60, out[2] * (1 if _psum(a) or _psum(b) else 2), 0, 0)}, [a, b], [out], out=out, a=a, b=b, op=op)
+
     def ts(out, a, s1, op0, s2=None, op1=None):
         rd = [a] + ([s1] if isinstance(s1, tuple) else [])
-        add("ts", ("V",), 60 + out[2] * CYC * _fast(out, a), rd, [out], out=out, a=a, s1=s1, s2=s2, op0=op0, op1=op1)
+        add("ts", "V", {"V": (60, out[2] * _fast(out, a), 0, 0)}, rd, [out], out=out, a=a, s1=s1, s2=s2, op0=op0, op1=op1)
 
     def vcopy(out, a):
-        add("vcopy", ("V",), 60 + out[2] * CYC * _fast(out, a), [a], [out], out=out, a=a)
+        add("copy", "V", {"V": (60, out[2] * _fast(out, a), 0, 0)}, [a], [out], out=out, a=a)
 
-    def act(out, a, func, scale=1.0, bias=0.0):
-        add("act", ("S",), 70 + out[2] * CYC, [a], [out], out=out, a=a, func=func, scale=scale, bias=bias)
+    def either(out, a, func, scale, bias, s1, op0, s2=None, op1=None, engs="SV"):
+        rd = [a] + ([s1] if isinstance(s1, tuple) else [])
+        add("either", engs, {"S": (70, out[2], 0, 0), "V": (60, out[2] * _fast(out, a), 0, 0)}, rd, [out], out=out, a=a,
+            func=func, scale=scale, bias=bias, s1=s1, op0=op0, s2=s2, op1=op1)
 
-    def either(out, a, func, scale, bias, s1, op0, s2=None, op1=None):
-        add("either", ("S", "V"), 70 + out[2] * CYC, [a], [out], out=out, a=a, func=func, scale=scale, bias=bias, s1=s1, op0=op0, s2=s2, op1=op1)
+    def scaled(out, a, k):
+        either(out, a, AF.Copy, float(k), 0.0, float(k), A.mult)
 
     def ecopy(out, a):
-        add("ecopy", ("S", "V"), 65 + out[2] * CYC, [a], [out], out=out, a=a)
+        add("copy", "SV", {"S": (70, out[2], 0, 0), "V": (60, out[2] * _fast(out, a), 0, 0)}, [a], [out], out=out, a=a)
 
     def scan(out, d0, d1, op0, op1):
-        add("scan", ("V",), 60 + out[2] * CYC * .5, [d0, d1], [out], out=out, d0=d0, d1=d1, op0=op0, op1=op1)
+        add("scan", "V", {"V": (60, out[2] * .5, 0, 0)}, [d0, d1], [out], out=out, d0=d0, d1=d1, op0=op0, op1=op1)
 
-    def gather(out, win, off):
-        add("gather", ("S", "V"), 60 + out[2] * CYC * 1.5, [win, off], [out], out=out, win=win, off=off)
+    def gather(out, win, off, engs="SV"):
+        add("gather", engs, {"S": (65, 0, out[2], 0), "V": (50, 0, out[2], 0)}, [win, off], [out], out=out, win=win, off=off)
 
-    def mm(out, lhs, rhs, start, stop, fp=False):
-        add("mm", ("P",), 30 + max(64, out[2]) * .75 * (4 if fp else 1), [lhs, rhs], [out], out=out, lhs=lhs, rhs=rhs, start=start, stop=stop)
+    def gmin(out, win, off, b):
+        add("gmin", "V", {"V": (50, 0, out[2], 0)}, [win, off, b], [out], out=out, win=win, off=off, b=b)
 
-    def group(out, terms, fp=False):
+    def mm(out, lhs, rhs, start, stop):
+        add("mm", "P", {"P": (30, 0, 0, max(64, out[2]))}, [lhs, rhs], [out], out=out, lhs=lhs, rhs=rhs, start=start, stop=stop)
+
+    def group(out, terms):
         for k, (l, r) in enumerate(terms):
-            mm(out, all_(l), r, k == 0, k == len(terms) - 1, fp)
+            mm(out, l if isinstance(l, tuple) else all_(l), r, k == 0, k == len(terms) - 1)
 
     def asel(out, in_, pat, op, base, cm):
-        add("asel", ("G",), 170 + out[2] * CYC * 2, [in_], [out], out=out, in_=in_, pat=pat, op=op, base=base, cm=cm)
+        add("asel", "G", {"G": (170, out[2] * 2, 0, 0)}, [in_], [out], out=out, in_=in_, pat=pat, op=op, base=base, cm=cm)
+
+    def iota(out, pat, base, cm):
+        add("iota", "G", {"G": (130, out[2] * 2, 0, 0)}, [], [out], out=out, pat=pat, base=base, cm=cm)
 
     def fill(out, val):
-        add("iota", ("G",), 130 + out[2] * CYC * 2, [], [out], out=out, val=val)
+        iota(out, [[0, out[2]]], val, 0)
 
     dma(c("s", 0, R), c("safe", 0, R))
     dma(c("x", 0, R), c("piv", 0, R))
@@ -163,72 +180,125 @@ def _program():
     dma(c("C0", V, R), c("lem", 0, R))
     for r in range(RO):
         dma(c("C%d" % r, V + R, F), c("leaf", 0, F))
+    one = c("one", 0, 128)
     memset(all_("one"), 1.0)
-    asel(all_("I"), all_("one"), [[-1, 128]], A.is_equal, 0, 1)
-    asel(all_("tb"), all_("one"), [[-16, 8], [0, 16]], A.is_ge, 0, 1)
-    asel(all_("ON"), all_("tb"), [[16, 8], [0, 16]], A.is_ge, 15, -1)
-    asel(all_("t1"), all_("ON"), [[-1, 128]], A.is_equal, -8, 1)
-    asel(all_("t2"), all_("ON"), [[-1, 128]], A.is_equal, 8, 1)
+    iota(all_("D2"), [[-16, 8], [248, 2], [-1, 8]], 0, 1)
+    for n, k in (("DL", 0), ("DH", 256), ("t1", 8), ("t2", 248)):
+        ts(all_(n), all_("D2"), float(k), A.is_equal)
+    tt(all_("I"), all_("DL"), all_("DH"), A.add)
     tt(all_("PM"), all_("t1"), all_("t2"), A.add)
+    asel(all_("tb"), one, [[-16, 8], [0, 16]], A.is_ge, 0, 1)
+    asel(all_("ON"), all_("tb"), [[16, 8], [0, 16]], A.is_ge, 15, -1)
 
     def half(out, in_, h):
         asel(all_(out), all_(in_), [[0, 8], [1, 2], [0, 8]], A.is_equal, -h, 0)
 
-    def mix(out, a, b):
-        ts(all_("g1"), all_("E0"), float(a), A.mult)
-        ts(all_("g2"), all_("E8"), float(b), A.mult)
-        tt(all_(out), all_("g1"), all_("g2"), A.add)
+    def row(out, k, a):
+        ts(all_(out), all_("B"), float(k), A.is_equal, float(a), A.mult)
+
+    def mix(out, a, b, t="g1", u="g2"):
+        row(t, 0, a); row(u, 8, b)
+        tt(all_(out), all_(t), all_(u), A.add)
     half("LO", "ON", 0)
     half("HI", "ON", 1)
-    asel(all_("E0"), all_("ON"), [[-16, 8], [0, 16]], A.is_equal, 0, 1)
-    asel(all_("E8"), all_("ON"), [[-16, 8], [0, 16]], A.is_equal, -8, 1)
-    mix("GA", -2048, 1024)
-    ts(all_("GB"), all_("GA"), -1.0, A.mult)
-    tt(all_("QB"), all_("HI"), all_("LO"), A.subtract)
-    ts(all_("QA"), all_("QB"), -32.0, A.mult)
-    half("t1", "GA", 0)
-    half("t2", "GA", 1)
-    tt(all_("QF"), all_("t2"), all_("t1"), A.subtract)
-    mix("HA", -256, 256)
-    ts(all_("HB"), all_("HA"), -1.0, A.mult)
-    mix("PB", 128, 128)
-    ts(all_("NB"), all_("PB"), -1.0, A.mult)
-    ts(all_("JN"), all_("ON"), -1.0, A.mult)
-    memset(all_("R1"), 0.0); memset(c("R1", 0, 2 * U, 16), 255.0)
-    fill(c("S1", 512, 16), 255); fill(c("S2", 2048, 1552), 255); fill(c("S3", E, 16), 255)
+    scaled(all_("NON"), all_("ON"), -1)
+    iota(all_("B"), [[-16, 8], [0, 16]], 0, 1)
+    row("HB", 0, 256)
+    mix("GA", -512, 256)
+    memset(all_("R8"), 0.0); memset(c("R8", 0, 128, 8), 255.0)
+    memset(all_("R16"), 0.0); memset(c("R16", 0, 64, 16), 255.0)
+    memset(c("S1", 512, 16), 255.0)
+    fill(c("S2", 2048, 1552), 255); fill(c("S3", E, 16), 255)
+
+    def halves(out, src, bank, cap):
+        ev, od = c(src[0], src[1], W // 2, 2), c(src[0], src[1] + 1, W // 2, 2)
+        group(c(bank[0], bank[1], W // 2), [("DL", ev), ("DH", od)])
+        group(c(bank[0], bank[1] + W // 2, W // 2), [("t1", ev), ("t2", od)])
+        ts(out, bank, float(H), A.add, float(cap), A.min)
+
     for k in range(3):
-        ts(c("ou", k * W, W), c("ui", k * W, W), 512, A.min)
-    for k in range(3, 7):
-        vcopy(c("ou", k * W, W), c("ui", k * W, W))
-    for n0, w, t in ((1024, 768, 1792), (256, 768, 1024), (0, 256, 256)):
-        for h in (0, 112):
-            k = h + n0 // 16
-            ts(c("po", k, w // 16), c("pi", k, w // 16), -t, A.add)
-    fill(c("K2", 0, 512), 0); fill(c("K2", 2048, 1552), 0); fill(c("K3", 0, 512), 0); fill(c("K3", E, 16), 0)
+        if any(k in ONE[r] for r in range(RO)):
+            ts(c("oN", k * W, W), c("ui", k * W, W), 512, A.min)
+        ts(c("OL", k * W, W), c("ui", k * W, W), -H, A.add)
+        if any(k not in ONE[r] for r in range(RO)):
+            halves(c("oF", k * W, W), c("OL", k * W, W), c("b%d" % (6 + k % 2), 0, W), 512)
+
+    def second(k):
+        ts(c("O0", k * W, W), c("ui", M + k * W, W), -H, A.add)
+        if k + 3 in ONE[0]:
+            vcopy(c("ov0", k * W, W), c("ui", M + k * W, W))
+        else:
+            halves(c("ov0", k * W, W), c("O0", k * W, W), c("b%d" % (7 - k % 2), 0, W), E)
+        if k < 3:
+            n0, w, t = ((1024, 768, 1792), (256, 768, 1024), (0, 256, 256))[k]
+            for h in (0, 112):
+                j = h + n0 // 16
+                ts(c("po", j, w // 16), c("pi", j, w // 16), -t, A.add)
+
+    def widen(out, src, bank):
+        group(bank, [("I", src)])
+        ecopy(out, bank)
 
     def late():
-        memset(all_("R2"), 2.0); memset(c("R2", 0, 2 * U, 16), 0.0)
-        scan(all_("ksi"), c("R2", 0, 128), all_("I"), A.mult, A.max)
-        add("red", ("V",), 80.0, [c("ksi", 15, 8, 16)], [all_("pw")], out=all_("pw"), a=c("ksi", 15, 8, 16))
-        vcopy(all_("P32"), all_("PM"))
-        ts(all_("J32"), all_("I"), -1.0, A.mult)
-        fill(all_("sela"), 1)
-        asel(all_("sela"), all_("sela"), [[1, 16], [0, 8], [-1, 16]], A.is_equal, 0, 0)
-        asel(all_("sela"), all_("sela"), [[0, 16], [-16, 8], [0, 16]], A.is_ge, 0, 1)
-        asel(all_("sela"), all_("sela"), [[0, 16], [16, 8], [0, 16]], A.is_ge, 15, -1)
+        scaled(all_("HA"), all_("HB"), -1)
+        row("PB", 8, 256)
+        scaled(all_("NB"), all_("PB"), -1)
+        scaled(all_("g3"), all_("LO"), 8192)
+        tt(all_("QA"), all_("g3"), all_("HI"), A.add)
+        tt(all_("QB"), all_("HI"), all_("LO"), A.subtract)
+        mix("g3", 2.0 ** 28, -2.0 ** 27)
+        mix("g4", 1, 1)
+        half("g1", "g3", 0); half("g2", "g4", 1)
+        tt(all_("QF"), all_("g1"), all_("g2"), A.add)
+        if STEST:
+            scaled(all_("NI"), all_("I"), -1)
+        for k in range(0, V, 2 * W):
+            n = min(2 * W, V - k)
+            ts(c("zi", k, n), c("x", k, n), 0.0, A.is_equal, 255.0, A.mult)
+        tt(all_("g4"), all_("DH"), all_("DL"), A.subtract)
+        add("red", "V", {"V": (60, 128, 0, 0)}, [all_("g4")], [all_("sg")], out=all_("sg"), a=all_("g4"))
+        scaled(all_("CF"), all_("I"), H - 4096)
+        mix("C1m", -BIG * 16 * H, H)
+        scaled(all_("C2m"), all_("C1m"), -1)
+        scaled(all_("BON"), all_("ON"), BIG)
+        scaled(all_("NBON"), all_("ON"), -BIG)
+        iota(all_("WF"), [[512, 16], [0, 8], [-512, 16]], 256, 0)
+        asel(all_("WF"), all_("WF"), [[-1, 16], [0, 8], [1, 16]], A.is_ge, 0, 0)
+        asel(all_("WF"), all_("WF"), [[0, 16], [-16, 8], [0, 16]], A.is_ge, 0, 1)
+        asel(all_("WF"), all_("WF"), [[0, 16], [16, 8], [0, 16]], A.is_ge, 15, -1)
+        asel(all_("sa"), all_("WF"), [[1, 16], [0, 8], [-1, 16]], A.is_equal, 0, 0)
+        for k in range(0, 2048, 512):
+            scaled(c("sa", k, 512), c("sa", k, 512), -1.0 / 512)
+        fill(c("K", 0, 512), 0); fill(c("K", E, 16), 0)
         for k in range(6):
-            ts(c("lt0", k * W, W), c("ui", k * W, W), -1.0, A.mult, float(E), A.add)
-        ts(all_("lg0"), c("ui", 1536, W), -1.0, A.mult, float(E), A.add)
-        memset(c("lt0", 1536, 16), 0.0); memset(c("lt1", 1536, 16), 0.0)
+            widen(c("lt0", k * W, W), c("OL", k * W, W) if k < 3 else c("O0", (k - 3) * W, W), c("b%d" % (6 + k % 2), 0, W))
+        memset(c("lt0", 1536, 16), float(H)); memset(c("lt1", 1536, 16), float(H))
         dma(c("lt1", 0, M), c("lt0", 0, M))
 
-    def lists(win, off, o0, n, gbuf, sbuf, g0, pat, op0, op1):
-        size = SCRATCH[gbuf][1][1]
-        for k in range(0, n, 2 * U):
-            at = (g0 + k) * 16 % size
-            for h in (0, U):
-                gather(c(gbuf, at + 16 * h, 16 * U), win, c(off, o0 + k + h, U))
-            scan(c(sbuf, (g0 + k) * 16, 32 * U), all_(pat), c(gbuf, at, 32 * U), op0, op1)
+    def offsets(r, k):
+        if k >= 3:
+            return "ov%d" % r, (k - 3) * W
+        return ("oN" if k in ONE[r] else "oF"), k * W
+
+    def lists(r, k):
+        win = all_("S1" if k < 3 else "S2" if k < 6 else "S3")
+        off, o0 = offsets(r, k)
+        g0 = (k % 3) * 16 * W
+        if k in ONE[r]:
+            for h in range(0, W, U):
+                gather(c("ga", g0 + 16 * h, 16 * U), win, c(off, o0 + h, U))
+                scan(c("sc", g0 + 16 * h, 16 * U), all_("R16"), c("ga", g0 + 16 * h, 16 * U), A.max, A.min)
+            return c("sc", g0 + 15, W, 16)
+        s0 = g0 + (k // 3 % 2) * 8 * W
+        for h in range(0, W // 2, U):
+            a, b = c("ga", g0 + 16 * h, 16 * U), c("ga", g0 + 8 * W + 16 * h, 16 * U)
+            gather(a, win, c(off, o0 + h, U))
+            gmin(b, win, c(off, o0 + W // 2 + h, U), a)
+            scan(c("sc", s0 + 16 * h, 16 * U), all_("R8"), b, A.max, A.min)
+        return c("sc", s0 + 7, W, 8)
+
+    def state(n0):
+        return all_("d0") if n0 < R else c("K", 2 * n0, W, 2)
 
     def premises(r, n0, stream):
         lo = 256 if n0 < R else 1024 if n0 < 1024 else 1792
@@ -238,146 +308,160 @@ def _program():
 
     def down(r, n0, stream, Mv):
         p, q = "b%d" % (2 * stream), "b%d" % (2 * stream + 1)
-        x, s, v = c("x", n0, W), c("s", n0, W), "v%d" % stream
+        x, s, dm = c("x", n0, W), c("s", n0, W), state(n0)
+        sv = s
         if r:
-            dm = c("dm", n0, W)
-            group(c(q, 0, W), [("I", s), ("NB", dm)])
-            group(c(q, W, W), [("I", s), ("PB", dm)])
+            group(c(q, W, W), [("I", Mv), ("NB", dm)])
             group(c(p, 0, W), [("I", x), ("HA", dm)])
             group(c(p, W, W), [("PM", x), ("HB", dm)])
-            tm = c("tm%d" % stream, 0, W)
-            tt(tm, Mv, c(q, 0, W), A.min)
-            tt(s, tm, c(q, W, W), A.max)
+            tt(s, s, c(q, W, W), A.max)
         else:
             group(c(p, 0, W), [("I", x)])
             group(c(p, W, W), [("PM", x)])
             if Mv is not None:
-                ecopy(s, Mv)
-        tt(c(v, 0, W), s, c(p, 0, W), A.is_lt)
-        tt(c(v, W, W), s, c(p, W, W), A.is_lt)
-        group(c(q, 0, W), [("LO", c(v, 0, W)), ("HI", c(v, W, W))])
+                sv = Mv
+        t = "S1" if n0 < R else "S2" if n0 < 1024 else "S3"
+        ta, tb = c(t, 2 * n0, W, 2), c(t, 2 * n0 + 1, W, 2)
+        tt(ta, sv, c(p, 0, W), A.max)
+        tt(tb, sv, c(p, W, W), A.max)
+        group(c(q, 0, W), [("NON", sv), ("LO", ta), ("HI", tb)])
+        fd = c("fd", n0, W)
+        either(fd, c(q, 0, W), AF.Relu, -1.0, 1.0, 0.0, A.is_equal)
+        group(c(q, 0, W), [("GA", fd)])
+        group(c(q, W, W), [("HB", fd)])
+        tt(ta, ta, c(q, 0, W), A.max)
+        tt(tb, tb, c(q, W, W), A.max)
+        if sv != s:
+            ecopy(s, sv)
         if n0 >= 1024:
             premises(r, n0, stream)
             tt(c("z%d" % stream, 0, 2 * W), c("ab%d" % stream, 0, 2 * W), c(p, 0, 2 * W), A.is_lt)
-        fd = c("fd", n0, W)
-        either(fd, c(q, 0, W), AF.Relu, -1.0, 1.0, 0.0, A.is_equal)
-        group(c(p, 0, W), [("I", x), ("GA", fd)])
-        group(c(p, W, W), [("PM", x), ("GB", fd)])
-        t = "S1" if n0 < R else "S2" if n0 < 1024 else "S3"
-        tt(c(t, 2 * n0, W, 2), s, c(p, 0, W), A.max)
-        tt(c(t, 2 * n0 + 1, W, 2), s, c(p, W, W), A.max)
 
     def up(r, n0, stream):
         p, q = "b%d" % (2 * stream), "b%d" % (2 * stream + 1)
-        x, fd, dm = c("x", n0, W), c("fd", n0, W), c("dm", n0, W)
+        x, s, fd, dm, zi = c("x", n0, W), c("s", n0, W), c("fd", n0, W), state(n0), c("zi", n0, W)
         ab, v, C = "ab%d" % stream, "v%d" % stream, "C%d" % r
         if n0 >= 1024:
             v = "z%d" % stream
+        elif n0 in STEST:
+            premises(r, n0, stream)
+            group(c(p, 0, W), [("I", x), ("NI", c(ab, 0, W))])
+            group(c(p, W, W), [("PM", x), ("NI", c(ab, W, W))])
+            either(c(v, 0, 2 * W), c(p, 0, 2 * W), AF.Relu, 1.0, 0.0, 0.0, A.max)
         else:
             group(c(p, 0, W), [("I", x)])
             group(c(p, W, W), [("PM", x)])
             premises(r, n0, stream)
             tt(c(v, 0, 2 * W), c(ab, 0, 2 * W), c(p, 0, 2 * W), A.is_lt)
-        group(c(q, 0, W), [("QA", c(v, 0, W)), ("QB", c(v, W, W)), ("QF", fd)])
-        act(dm, c(q, 0, W), AF.Sign, 1.0, -0.5)
-        group(c(p, 0, W), [("I", x), ("HA", dm)])
-        group(c(p, W, W), [("PM", x), ("HB", dm)])
-        if r < RO - 1 and n0 >= R:
-            k = "K2" if n0 < 1024 else "K3"
-            act(c(k, 2 * n0 + 1, W, 2), c(p, 0, W), AF.Sign, 1.0, -255.5)
-            act(c(k, 2 * n0, W, 2), c(p, W, W), AF.Sign, 1.0, -255.5)
-        either(c(p, 0, 2 * W), c(p, 0, 2 * W), AF.Relu, -1024.0, 512.0, 0.0, A.is_le, 512.0, A.mult)
+        group(c(q, 0, W), [("QF", fd), ("QA", c(v, 0, W)), ("QB", c(v, W, W))])
+        either(dm, c(q, 0, W), AF.Sign, 1.0, 0.0, -1.0, A.max, 1.0, A.min)
+        group(c(p, 0, W), [("I", zi), ("HB", dm)])
+        group(c(p, W, W), [("PM", zi), ("HA", dm)])
         tm = c("tm%d" % stream, 0, W)
         tt(tm, c(ab, 0, W), c(p, 0, W), A.min)
         tt(c(p, W, W), c(ab, W, W), c(p, W, W), A.min)
         tt(c(C, n0, W), tm, c(p, W, W), A.max)
         if r == RO - 1:
             dma(c("yc", n0, W), c(C, n0, W))
+            return
+        if n0 >= R:
+            either(c("K", 2 * n0 + 1, W, 2), dm, AF.Copy, all_("sg"), 0.0, all_("sg"), A.mult)
+        group(c(q, W, W), [("I", s), ("PB", dm)])
+        either(s, c(q, W, W), AF.Relu, 1.0, -256.0, -256.0, A.add, 0.0, A.max)
 
-    def kscan(r, part):
-        off, o0 = ("ou", M) if r == 1 else ("ov1", 0)
-        if part == 0:
-            lists(all_("K2"), off, o0, M, "kg", "ks", 0, "R2", A.mult, A.max)
+    def wrap(out, src, k0):
+        group(out, [(c("sa", 128 * q, 128), c(src, k0 + q, out[2], 16)) for q in range(16)])
+
+    def sums(r):
+        w = c("b6", W, 64)
+        wrap(w, "O%d" % r, 0)
+        either(all_("w0"), w, AF.Identity, -1.0, 1535.75, -1.0, A.mult, 1535.75, A.add)
+
+    def splice(r, k):
+        O, On, k0, z = "O%d" % (r - 1), "O%d" % r, (k - 3) * W, "b%d" % (6 + k % 2)
+        off, o0 = offsets(r - 1, k)
+        g0 = (k % 3) * 16 * W
+        for h in range(0, W, KU):
+            gather(c("kg", g0 + 16 * h, 16 * KU), all_("K"), c(off, o0 + h, KU))
+        if k in ONE[r - 1]:
+            parts = [(0, W, 1, lambda j: j)]
         else:
-            lists(all_("K3"), off, o0 + M, R, "kg", "ks", 0, "R2", A.mult, A.max)
-
-    def splice(r, part):
-        lt, ov = "lt%d" % (r - 1), "ov%d" % r
-        c0, n = (0, M) if part == 0 else (M, R)
-
-        def L(k):
-            return c(lt, M + k, W) if part == 0 else c("lg%d" % (r - 1), k, W)
-        for k in range(0, n, W):
-            ts(c("th", c0 + k, W), c("ks", 16 * k + 15, W, 16), all_("pw"), A.is_equal)
-            tt(c("P", c0 + k, W), c("th", c0 + k, W), L(k), A.mult)
-        w = c("b6", 0, n // 16); wo = c0 // 16; m = n // 16
-        for q in range(16):
-            mm(w, c("sela", 128 * q, 128), c("P", c0 + q, m, 16), q == 0, q == 15, True)
-        ts(c("w1", wo, m), w, -1.0, A.mult, float(E - 512), A.add)
-        ts(c("w2", wo, m), c("w1", wo, m), 1, A.arith_shift_right)
-        vcopy(c("wu", wo, m), c("w2", wo, m))
-        for k in range(0, n, W):
-            gather(c("tg", c0 + k, W), all_(lt), c("wu", wo + k // 16, 16))
-        for k in range(0, n, W):
-            z = "b%d" % (7 - (k // W) % 2)
-            P, lm, hm = c("P", c0 + k, W), c("lm", c0 + k, W), c("hm", c0 + k, W)
-            group(c(z, 0, W), [("P32", c("tg", c0 + k, W)), ("J32", P)], fp=True)
-            tt(lm, P, c(z, 0, W), A.min)
-            tt(hm, L(k), c(z, 0, W), A.min)
-            group(c(z, W, W), [("ON", hm), ("JN", lm)])
-            either(c("ch", c0 + k, W), c(z, W, W), AF.Relu, -1.0, 1.0, 0.0, A.is_equal)
-            tt(c("tg", c0 + k, W), c("ch", c0 + k, W), c(z, 0, W), A.mult)
-            if r == 1:
-                nl = c("lt1", M + k, W) if part == 0 else c("lg1", k, W)
-            else:
-                nl = c("nl", c0 + k, W)
-            tt(nl, c("tg", c0 + k, W), L(k), A.add)
-            ts(c(ov, c0 + k, W), nl, -1.0, A.mult, float(E), A.add)
+            parts = [(0, W // 2, 2, lambda j: j if j < 8 else 8 * W + j - 8), (1, W // 2, 2, lambda j: j if j >= 8 else 8 * W + j + 8)]
+        for h, n, st, at in parts:
+            group(c(z, h * n, n), [("CF", c("one", 0, n))] + [(c("WF", 128 * j, 128), c("kg", g0 + at(j), n, 16)) for j in range(16)])
+        for h, n, st, at in parts:
+            tt(c("Ox", k0 + h, n, st), c(O, k0 + h, n, st), c(z, h * n, n), A.max)
+        m = W // 16
+        w = c(z, W, m); wo = k0 // 16
+        wrap(w, "Ox", k0)
+        tt(c("w1", wo, m), c("w0", wo, m), w, A.add)
+        vcopy(c("wu", wo, m), c("w1", wo, m))
+        Ox, tg, cc, mv, on = c("Ox", k0, W), c("tg", k0, W), c("cc", k0, W), c("mm", k0, W), c("one", 0, W)
+        gather(tg, all_("lt1" if r == 2 and k == 6 else "lt0"), c("wu", wo, m), "V")
+        group(c(z, 0, W), [("PM", tg)])
+        tt(cc, Ox, c(z, 0, W), A.max)
+        group(c(z, W, W), [("C1m", on), ("BON", cc)])
+        group(c(z, 0, W), [("C2m", on), ("NBON", cc), ("I", Ox), ("PM", tg)])
+        tt(mv, c(O, k0, W), c(z, W, W), A.max)
+        nl = c(On, k0, W)
+        tt(nl, mv, c(z, 0, W), A.min)
+        if k in ONE[r]:
+            group(c(z, W, W), [("I", nl)])
+            ts(c("ov%d" % r, k0, W), c(z, W, W), float(H), A.add)
+        else:
+            halves(c("ov%d" % r, k0, W), nl, c(z, W, W), E)
+        if r == 1 and k < 6:
+            widen(c("lt1", M + k0, W), nl, c(z, 0, W))
 
     def send(src, dst, lo, to, rs, ls):
-        j = add("send", ("G",), 300.0, [src], [], src=src, dst=dst, at=(lo, lo + R), to=to, rs=rs, lat=2500.0, sem=(ls, 8))
-        add("arrive", ("R",), 0.0, [], [c(dst, lo, R)], lat=1000.0, sem=(rs, 8), after=j)
+        j = add("send", "G", {"G": (300, 0, 0, 0)}, [src], [], src=src, dst=dst, at=(lo, lo + R), to=to, rs=rs, lat=2500.0, sem=(ls, 8))
+        add("arrive", "R", {"R": (0, 0, 0, 0)}, [], [c(dst, lo, R)], lat=1000.0, sem=(rs, 8), after=j)
 
     for r in range(RO):
-        off2, o2 = ("ou", M) if r == 0 else ("ov%d" % r, 0)
-        if r:
-            kscan(r, 0)
-        down(r, 0, 0, None if r == 0 else all_("sa%d" % r))
+        down(r, 0, 0, None if r == 0 else all_("ar%d" % r))
         dma(c("S2", 0, 512), c("S1", 0, 512))
-        if r:
-            splice(r, 0)
         for k in range(3):
-            lists(all_("S1"), "ou", k * W, W, "ga", "sc", k * W, "R1", A.max, A.min)
-            down(r, R + k * W, (k + 1) % 3, c("sc", 16 * k * W + 15, W, 16))
+            if r and EARLY:
+                splice(r, 3 + k)
+            down(r, R + k * W, (k + 1) % 3, lists(r, k))
+            if r and not EARLY:
+                splice(r, 3 + k)
+            if r == 0:
+                second(k)
         dma(c("S3", 0, 2048), c("S2", 0, 2048))
-        if r == 0:
-            late()
-        else:
-            kscan(r, 1)
-            splice(r, 1)
         for k in range(3):
-            lists(all_("S2"), off2, o2 + k * W, W, "ga", "sc", k * W, "R1", A.max, A.min)
-            down(r, 1024 + k * W, k, c("sc", 16 * k * W + 15, W, 16))
+            down(r, 1024 + k * W, k, lists(r, 3 + k))
+            if k == 0 and r:
+                splice(r, 6)
+            if k == 0 and r == 0:
+                second(3)
+                late()
         if r == RO - 1:
             for k in range(7):
                 dma(c("ys", k * W, W), c("s", k * W, W))
-        lists(all_("S3"), off2, o2 + M, R, "ga", "sc", 0, "R1", A.max, A.min)
+        else:
+            sums(r)
+        for k in range(GHOST):
+            up(r, 1024 + k * W, k)
         gs = all_("gs%d" % r)
-        ecopy(gs, c("sc", 15, R, 16))
+        ecopy(gs, lists(r, 6))
         if r < RO - 1:
-            send(gs, "sa%d" % (r + 1), 0, 1, "ra%d" % r, "la%d" % r)
+            send(gs, "ar%d" % (r + 1), 0, 1, "ra%d" % r, "la%d" % r)
         else:
             dma(c("ys", V, R), gs)
-        for k in range(3):
+        for k in range(GHOST, 3):
             up(r, 1024 + k * W, k)
         for k in range(3):
             up(r, R + k * W, k)
-        if r < RO - 1:
-            dma(c("K3", 512, 1536), c("K2", 512, 1536))
         up(r, 0, 0)
         if r < RO - 1:
             send(c("C%d" % r, 0, R), "C%d" % (r + 1), V, -1, "rb%d" % r, "lb%d" % r)
     return ops
+
+
+def _cost(o, e):
+    f, n, g, p = o["cyc"][e]
+    return f + CYC * (n + g * GCY) + p * PCY
 
 
 def _schedule(ops):
@@ -390,14 +474,15 @@ def _schedule(ops):
     for o in ops:
         for p in o["preds"]:
             succ[p].append(o["id"])
+    base = [_cost(o, o["engs"][0]) for o in ops]
     rank = [0.0] * n
     for i in range(n - 1, -1, -1):
         o = ops[i]
         acc, best = 0.0, 0.0
         for j in sorted(succ[i], key=lambda j: -rank[j]):
             best = max(best, rank[j] + 100 + acc)
-            acc += ops[j]["cost"] * FAC[ops[j]["kind"] == "gather"]
-        rank[i] = o["cost"] + o["lat"] + best
+            acc += base[j] * FAC[ops[j]["kind"] in ("gather", "gmin")]
+        rank[i] = base[i] + o["lat"] + best
     free = {"V": 0.0, "S": 0.0, "P": 0.0, "G": 0.0, "Y": 0.0, "R": 0.0}
     done, eng, order = [0.0] * n, [None] * n, []
     ready = [i for i in range(n) if left[i] == 0]
@@ -430,8 +515,8 @@ def _schedule(ops):
         o = ops[i]
         eng[i] = e
         if e != "R":
-            free[e] = t + o["cost"]
-        done[i] = t + o["cost"] + o["lat"]
+            free[e] = t + _cost(o, e)
+        done[i] = t + _cost(o, e) + o["lat"]
         order.append(i)
         ready.remove(i)
         for j in succ[i]:
@@ -439,6 +524,159 @@ def _schedule(ops):
             if left[j] == 0:
                 ready.append(j)
     return order, eng, max(done)
+
+
+STEAL, PEN, TOL, MIX, PASSES = 200.0, 4.0, 0.0, 0.6, 4
+
+
+def _forward(ops, succ, lst, tol):
+    n = len(ops)
+    left = [len(o["preds"]) for o in ops]
+    free = {e: 0.0 for e in "VSPGYR"}
+    done, eng, order, rdy = [None] * n, [None] * n, [], {}
+
+    def enter(i):
+        o = ops[i]; r = {}
+        for e in o["engs"]:
+            t = 0.0
+            for p, hard in o["preds"].items():
+                d = done[p]
+                if eng[p] != e or ops[p]["sem"]:
+                    d += XLAT
+                elif hard is not None and e != "P":
+                    d += 60.0
+                if d > t:
+                    t = d
+            r[e] = t
+        rdy[i] = r
+
+    def coming():
+        est = {i: min(max(free[e], t) for e, t in r.items()) for i, r in rdy.items()}
+        front = list(rdy)
+        for _ in range(5):
+            nxt = []
+            for i in front:
+                for j in succ[i]:
+                    if j in est:
+                        continue
+                    t = 0.0
+                    for p in ops[j]["preds"]:
+                        if done[p] is not None:
+                            d = done[p]
+                        elif p in est:
+                            d = est[p] + ops[p]["min"] + ops[p]["lat"]
+                        else:
+                            t = None
+                            break
+                        d += 0 if ops[p]["engs"] == ops[j]["engs"] == "P" else XLAT
+                        if d > t:
+                            t = d
+                    if t is not None:
+                        est[j] = t; nxt.append(j)
+            front = nxt
+        return est
+    for i in range(n):
+        if left[i] == 0:
+            enter(i)
+    while rdy:
+        est = pick = None
+        for e in "RYGPSV":
+            cand = []
+            for i, r in rdy.items():
+                if e in r:
+                    t = max(free[e], r[e]); p = lst[i]
+                    if e == "V" and "S" in r:
+                        if max(free["S"], r["S"]) - t < STEAL:
+                            continue
+                        p += PEN * ops[i]["cost"]["V"]
+                    cand.append((t, p, i))
+            if not cand:
+                continue
+            t0 = min(cand)[0]
+            if pick is not None and t0 >= pick[0]:
+                continue
+            now = sorted([x for x in cand if x[0] <= t0 + 1], key=lambda x: x[1])
+            ok = now[0]
+            if e in "VS":
+                if est is None:
+                    est = coming()
+                soon = [(t, lst[j]) for j, t in est.items() if e in ops[j]["engs"] and t0 + 1 < t < t0 + 1500 and (e == "S" or ops[j]["engs"] == "V")]
+                ok = None
+                for t, p, i in now:
+                    end = t + ops[i]["cost"][e]
+                    if not any(u < end and l + tol < end and l < p for u, l in soon):
+                        ok = (t, p, i)
+                        break
+                if ok is None:
+                    free[e] = min([u for u, l in soon if l < now[-1][1]] + [x[0] for x in cand if x[0] > t0 + 1])
+                    pick = None
+                    break
+            pick = (ok[0], ok[2], e)
+        if pick is None:
+            continue
+        t, i, e = pick
+        o = ops[i]
+        eng[i] = e
+        if e != "R":
+            free[e] = t + o["cost"][e]
+        done[i] = t + o["cost"][e] + o["lat"]
+        order.append(i)
+        del rdy[i]
+        for j in succ[i]:
+            left[j] -= 1
+            if left[j] == 0:
+                enter(j)
+    return order, eng, done
+
+
+def _backward(ops, succ, eng, done):
+    n = len(ops)
+    st = {e: [] for e in "VSPGY"}; en = {e: [] for e in "VSPGY"}
+    back = [0.0] * n
+    for i in sorted(range(n), key=lambda i: (-done[i], -i)):
+        o, e = ops[i], eng[i]
+        t = o["lat"]
+        for j in succ[i]:
+            d = back[j] + o["lat"]
+            if eng[j] != e or o["sem"]:
+                d += XLAT
+            elif ops[j]["preds"][i] is not None and e != "P":
+                d += 60.0
+            if d > t:
+                t = d
+        c = o["cost"][e]
+        if e != "R":
+            S, N = st[e], en[e]
+            k = len(N)
+            while k and N[k - 1] > t:
+                k -= 1
+            while k < len(S) and S[k] < t + c:
+                t = max(t, N[k])
+                k += 1
+            S.insert(k, t); N.insert(k, t + c)
+        back[i] = t + c
+    end = max(back)
+    return [(end - b) * 0.97 for b in back]
+
+
+def _schedule(ops):
+    n = len(ops)
+    succ = [[] for _ in ops]
+    for o in ops:
+        if "after" in o:
+            o["preds"].setdefault(o["after"], False)
+        o["cost"] = {e: _cost(o, e) for e in o["engs"]}
+        o["min"] = min(o["cost"].values())
+        for p in o["preds"]:
+            succ[p].append(o["id"])
+    lst, best = [i * 110.0 for i in range(n)], None
+    for k in range(PASSES):
+        order, eng, done = _forward(ops, succ, lst, TOL if k else 1e9)
+        if best is None or max(done) < best[2]:
+            best = (order, eng, max(done))
+        new = _backward(ops, succ, eng, done)
+        lst = [MIX * a + (1 - MIX) * b for a, b in zip(new, lst)] if k else new
+    return best
 
 
 def _waits(ops, order, eng):
@@ -496,6 +734,8 @@ def rank_program(g, core, T, topo):
     queue = {"V": g.vector, "S": g.scalar, "P": g.tensor, "G": g, "Y": g.sync}
 
     def ap(v):
+        if not isinstance(v, tuple):
+            return v
         if v[3] == 1:
             return T[v[0]][:, v[1]:v[1] + v[2]]
         return T[v[0]][:, v[1]:_hi(v):v[3]]
@@ -524,30 +764,29 @@ def rank_program(g, core, T, topo):
         elif kind == "tt":
             x = q.tensor_tensor(out, ap(o["a"]), ap(o["b"]), o["op"])
         elif kind == "ts" or (kind == "either" and e == "V"):
-            s1 = ap(o["s1"]) if isinstance(o["s1"], tuple) else o["s1"]
             if o["op1"] is None:
-                x = q.tensor_scalar(out, ap(o["a"]), s1, None, o["op0"])
+                x = q.tensor_scalar(out, ap(o["a"]), ap(o["s1"]), None, o["op0"])
             else:
-                x = q.tensor_scalar(out, ap(o["a"]), s1, o["s2"], o["op0"], o["op1"])
-        elif kind == "vcopy" or (kind == "ecopy" and e == "V"):
-            x = q.tensor_copy(out, ap(o["a"]))
-        elif kind == "ecopy":
-            x = q.activation(out, ap(o["a"]), AF.Copy)
-        elif kind == "act" or kind == "either":
-            x = q.activation(out, ap(o["a"]), o["func"], bias=o["bias"], scale=o["scale"])
+                x = q.tensor_scalar(out, ap(o["a"]), ap(o["s1"]), o["s2"], o["op0"], o["op1"])
+        elif kind == "copy":
+            x = q.tensor_copy(out, ap(o["a"])) if e == "V" else q.activation(out, ap(o["a"]), AF.Copy)
+        elif kind == "either":
+            x = q.activation(out, ap(o["a"]), o["func"], bias=o["bias"], scale=ap(o["scale"]))
         elif kind == "scan":
             x = q.tensor_tensor_scan(out, ap(o["d0"]), ap(o["d1"]), 0.0, o["op0"], o["op1"])
         elif kind == "red":
-            x = q.tensor_reduce(out, ap(o["a"]), AxisListType.X, A.max)
+            x = q.tensor_reduce(out, ap(o["a"]), AxisListType.X, A.add)
         elif kind == "gather":
             src = ap(o["win"]).indirect(ap(o["off"]))
             x = q.tensor_copy(out, src) if e == "V" else q.activation(out, src, AF.Copy)
+        elif kind == "gmin":
+            x = q.tensor_tensor(out, ap(o["win"]).indirect(ap(o["off"])), ap(o["b"]), A.min)
         elif kind == "mm":
             x = q.matmul(out, ap(o["lhs"]), ap(o["rhs"]), o["start"], o["stop"])
         elif kind == "asel":
             x = q.affine_select(out, ap(o["in_"]), o["pat"], o["op"], 0.0, o["base"], o["cm"])
         else:
-            x = q.iota(out, [[0, o["out"][2]]], o["val"], 0, allow_small_or_imprecise_dtypes=True)
+            x = q.iota(out, o["pat"], o["base"], o["cm"], allow_small_or_imprecise_dtypes=True)
         x.then_inc(T.sem[s], 1)
     for s, val in pl["tail"]:
         g.wait_ge(T.sem[s], val)

@@ -1,3 +1,5 @@
+import math
+
 from concourse.mybir import AluOpType as A, AxisListType, ActivationFunctionType as AF
 
 R, M, V, F, RO = 256, 768, 1792, 512, 3
@@ -8,9 +10,13 @@ U = 64
 BF, F2, F4, I4, U2 = "bfloat16", "float16", "float32", "int32", "uint16"
 BIG = 8192.0
 
-ONE = ((4, 5), (1, 4, 5, 6), (1, 4, 5, 6))
+ONE = ((0, 1, 4, 6), (4, 5, 6), (4, 5, 6))
 STEST = ()
-EARLY, GHOST, KU = True, 1, 32
+PIECES = ((32, 96), (64, 64), (64, 64), (64, 64))
+KS = ((32,) * 8, (32,) * 8, (64,) * 4, (64,) * 4)
+GAP, SUM, SHORT = ((), (), ()), (range(7),) * 3, ((), (), range(7))
+EARLY, GHOST, AHEAD = False, 0, False
+FAR = {"ra0": 6000.0, "ra1": 4000.0, "rb0": 9000.0, "rb1": 9000.0}
 
 SCRATCH = {}
 
@@ -20,17 +26,16 @@ def _b(name, n, d=BF):
 
 
 for _n in ("I", "tb", "ON", "PM", "t1", "t2", "DL", "DH", "LO", "HI", "B", "g1", "g2", "g3", "g4", "GA", "QA", "QB", "QF", "HA", "HB", "NB", "PB",
-           "NON", "NI", "CF", "C1m", "C2m", "BON", "NBON"):
+           "ZF", "ZS", "L2", "XF", "YF", "XA", "YA", "XB", "YB", "NON", "NI", "CF", "C1m", "C2m", "BON", "NBON"):
     _b(_n, 128)
 _b("D2", 128, F4); _b("one", W); _b("sg", 1, F4)
 _b("WF", 2048); _b("sa", 2048); _b("w0", 64, F4)
-_b("R8", 1024); _b("R16", 1024)
-_b("x", V); _b("s", V); _b("zi", V); _b("ui", V, I4); _b("pi", 224, I4); _b("po", 224, U2)
+_b("R8", 1536); _b("R16", 1024)
+_b("x", V); _b("s", V); _b("zi", V); _b("ui", V + 16, I4); _b("pi", 224, I4); _b("po", 224, U2)
 _b("oF", M, U2); _b("oN", M, U2); _b("OL", M, F2)
 for _r in range(RO):
     _b("ov%d" % _r, 1024, U2); _b("O%d" % _r, 1024, F2)
     _b("C%d" % _r, V + R + F); _b("ar%d" % _r, R); _b("gs%d" % _r, R)
-_b("lt0", 1552, F4); _b("lt1", 1552, F4)
 _b("S1", 528); _b("S2", 3600); _b("S3", 3600); _b("K", 3600)
 _b("ga", 16 * M); _b("sc", 16 * M); _b("kg", 48 * W)
 _b("fd", V); _b("d0", R)
@@ -45,7 +50,7 @@ ND = 64
 SEMAPHORES = ["eV", "eS", "eP", "eG"] + ["d%d" % _i for _i in range(ND)] + ["%s%d" % (_p, _r) for _p in ("ra", "rb", "la", "lb") for _r in range(RO - 1)]
 EXT = {"piv": BF, "safe": BF, "lem": BF, "leaf": BF, "uses": I4, "prem": I4, "yc": BF, "ys": BF}
 
-CYC, XLAT, GCY, PCY = 0.83, 150.0, 1.5, 0.6
+CYC, XLAT, GCY, PCY = 0.83, 220.0, 1.3, 0.5
 PEN, SLACK, FAC = 8000.0, 150.0, (0.6, 0.7)
 
 
@@ -72,7 +77,7 @@ def _covers(a, b):
 
 
 def _program():
-    ops, bufs, last, nd = [], {}, {}, [0]
+    ops, bufs, last, nd = [], {}, {}, [0, 0]
 
     def add(kind, engs, cyc, reads, writes, **kw):
         i = len(ops)
@@ -119,8 +124,13 @@ def _program():
 
     def dma(out, in_):
         k = nd[0]; nd[0] += 1
-        n = max(out[2], in_[2]) * (2 if _two(out) else 4)
-        add("dma", "Y", {"Y": (60, 0, 0, 0)}, [in_], [out], out=out, in_=in_, lat=2000.0 + n * 128 / 150.0, sem=("d%d" % k, 16))
+        n = max(out[2], in_[2]) * (2 if _two(out) else 4) * 128
+        load = in_[0] in EXT
+        if load:
+            nd[1] += n
+        i = add("dma", "Y", {"Y": (60, 0, 0, 0)}, [in_], [out], out=out, in_=in_, lat=2200.0 + (nd[1] if load else n) / 250.0, sem=("d%d" % k, 16))
+        if load and k:
+            ops[i]["preds"][i - 1] = "order"
 
     def memset(out, val):
         add("memset", "V", {"V": (60, out[2] * (.5 if _two(out) else 1), 0, 0)}, [], [out], out=out, val=val)
@@ -171,14 +181,18 @@ def _program():
     def fill(out, val):
         iota(out, [[0, out[2]]], val, 0)
 
-    dma(c("s", 0, R), c("safe", 0, R))
     dma(c("x", 0, R), c("piv", 0, R))
-    dma(c("ui", 0, M), c("uses", 0, M))
-    dma(c("x", R, V - R), c("piv", R, V - R))
-    dma(c("ui", M, 1024), c("uses", M, 1024))
+    dma(c("s", 0, R), c("safe", 0, R))
+    dma(c("ui", 0, W), c("uses", 0, W))
+    dma(c("ui", W, M - W), c("uses", W, M - W))
+    dma(c("x", R, M), c("piv", R, M))
+    dma(c("ui", M, M), c("uses", M, M))
+    dma(c("x", R + M, M), c("piv", R + M, M))
     dma(all_("pi"), c("prem", 0, 224))
     dma(c("C0", V, R), c("lem", 0, R))
-    for r in range(RO):
+    dma(c("C0", V + R, F), c("leaf", 0, F))
+    dma(c("ui", 2 * M + 16, R), c("uses", 2 * M, R))
+    for r in range(1, RO):
         dma(c("C%d" % r, V + R, F), c("leaf", 0, F))
     one = c("one", 0, 128)
     memset(all_("one"), 1.0)
@@ -199,13 +213,16 @@ def _program():
     def mix(out, a, b, t="g1", u="g2"):
         row(t, 0, a); row(u, 8, b)
         tt(all_(out), all_(t), all_(u), A.add)
-    half("LO", "ON", 0)
+    asel(all_("L2"), all_("ON"), [[0, 8], [1, 4], [0, 4]], A.not_equal, -2, 0)
     half("HI", "ON", 1)
-    scaled(all_("NON"), all_("ON"), -1)
+    tt(all_("g3"), all_("L2"), all_("HI"), A.add)
+    scaled(all_("NON"), all_("g3"), -1)
+    scaled(all_("NI"), all_("I"), -1)
     iota(all_("B"), [[-16, 8], [0, 16]], 0, 1)
     row("HB", 0, 256)
-    mix("GA", -512, 256)
-    memset(all_("R8"), 0.0); memset(c("R8", 0, 128, 8), 255.0)
+    row("g1", 8, 256); row("g2", 12, -256)
+    tt(all_("GA"), all_("g1"), all_("g2"), A.add)
+    memset(all_("R8"), 0.0); memset(c("R8", 0, 192, 8), 255.0)
     memset(all_("R16"), 0.0); memset(c("R16", 0, 64, 16), 255.0)
     memset(c("S1", 512, 16), 255.0)
     fill(c("S2", 2048, 1552), 255); fill(c("S3", E, 16), 255)
@@ -219,14 +236,15 @@ def _program():
     for k in range(3):
         if any(k in ONE[r] for r in range(RO)):
             ts(c("oN", k * W, W), c("ui", k * W, W), 512, A.min)
-        ts(c("OL", k * W, W), c("ui", k * W, W), -H, A.add)
         if any(k not in ONE[r] for r in range(RO)):
+            ts(c("OL", k * W, W), c("ui", k * W, W), -H, A.add)
             halves(c("oF", k * W, W), c("OL", k * W, W), c("b%d" % (6 + k % 2), 0, W), 512)
 
     def second(k):
-        ts(c("O0", k * W, W), c("ui", M + k * W, W), -H, A.add)
+        u = c("ui", M + k * W + 16 * (k == 3), W)
+        ts(c("O0", k * W, W), u, -H, A.add)
         if k + 3 in ONE[0]:
-            vcopy(c("ov0", k * W, W), c("ui", M + k * W, W))
+            vcopy(c("ov0", k * W, W), u)
         else:
             halves(c("ov0", k * W, W), c("O0", k * W, W), c("b%d" % (7 - k % 2), 0, W), E)
         if k < 3:
@@ -235,14 +253,11 @@ def _program():
                 j = h + n0 // 16
                 ts(c("po", j, w // 16), c("pi", j, w // 16), -t, A.add)
 
-    def widen(out, src, bank):
-        group(bank, [("I", src)])
-        ecopy(out, bank)
-
     def late():
         scaled(all_("HA"), all_("HB"), -1)
         row("PB", 8, 256)
         scaled(all_("NB"), all_("PB"), -1)
+        half("LO", "ON", 0)
         scaled(all_("g3"), all_("LO"), 8192)
         tt(all_("QA"), all_("g3"), all_("HI"), A.add)
         tt(all_("QB"), all_("HI"), all_("LO"), A.subtract)
@@ -250,8 +265,12 @@ def _program():
         mix("g4", 1, 1)
         half("g1", "g3", 0); half("g2", "g4", 1)
         tt(all_("QF"), all_("g1"), all_("g2"), A.add)
-        if STEST:
-            scaled(all_("NI"), all_("I"), -1)
+        for n, m, k in (("XF", "g3", 1024), ("YF", "g3", -1024), ("XA", "ON", 2 ** 23), ("YA", "ON", -2 ** 23), ("XB", "ON", -1024), ("YB", "ON", 1024)):
+            scaled(all_(n), all_(m), k)
+        if AHEAD:
+            scaled(all_("ZF"), all_("g4"), 1024)
+            row("g1", 0, -2)
+            tt(all_("ZS"), all_("g1"), all_("QB"), A.mult)
         for k in range(0, V, 2 * W):
             n = min(2 * W, V - k)
             ts(c("zi", k, n), c("x", k, n), 0.0, A.is_equal, 255.0, A.mult)
@@ -270,10 +289,7 @@ def _program():
         for k in range(0, 2048, 512):
             scaled(c("sa", k, 512), c("sa", k, 512), -1.0 / 512)
         fill(c("K", 0, 512), 0); fill(c("K", E, 16), 0)
-        for k in range(6):
-            widen(c("lt0", k * W, W), c("OL", k * W, W) if k < 3 else c("O0", (k - 3) * W, W), c("b%d" % (6 + k % 2), 0, W))
-        memset(c("lt0", 1536, 16), float(H)); memset(c("lt1", 1536, 16), float(H))
-        dma(c("lt1", 0, M), c("lt0", 0, M))
+        memset(c("ui", 2 * M, 16), E)
 
     def offsets(r, k):
         if k >= 3:
@@ -290,11 +306,13 @@ def _program():
                 scan(c("sc", g0 + 16 * h, 16 * U), all_("R16"), c("ga", g0 + 16 * h, 16 * U), A.max, A.min)
             return c("sc", g0 + 15, W, 16)
         s0 = g0 + (k // 3 % 2) * 8 * W
-        for h in range(0, W // 2, U):
-            a, b = c("ga", g0 + 16 * h, 16 * U), c("ga", g0 + 8 * W + 16 * h, 16 * U)
-            gather(a, win, c(off, o0 + h, U))
-            gmin(b, win, c(off, o0 + W // 2 + h, U), a)
-            scan(c("sc", s0 + 16 * h, 16 * U), all_("R8"), b, A.max, A.min)
+        h = 0
+        for u in PIECES[k % 3 if k < 6 else 3]:
+            a, b = c("ga", g0 + 16 * h, 16 * u), c("ga", g0 + 8 * W + 16 * h, 16 * u)
+            gather(a, win, c(off, o0 + h, u))
+            gmin(b, win, c(off, o0 + W // 2 + h, u), a)
+            scan(c("sc", s0 + 16 * h, 16 * u), c("R8", 0, 16 * u), b, A.max, A.min)
+            h += u
         return c("sc", s0 + 7, W, 8)
 
     def state(n0):
@@ -309,54 +327,78 @@ def _program():
     def down(r, n0, stream, Mv):
         p, q = "b%d" % (2 * stream), "b%d" % (2 * stream + 1)
         x, s, dm = c("x", n0, W), c("s", n0, W), state(n0)
-        sv = s
+        k = n0 // W
+        sv = s if r or Mv is None else Mv
+        ya, yb = [("I", x)] + [("HA", dm)] * (r > 0), [("PM", x)] + [("HB", dm)] * (r > 0)
         if r:
-            group(c(q, W, W), [("I", Mv), ("NB", dm)])
-            group(c(p, 0, W), [("I", x), ("HA", dm)])
-            group(c(p, W, W), [("PM", x), ("HB", dm)])
+            group(c(q, W, W), [("NB", dm), ("I", Mv)])
             tt(s, s, c(q, W, W), A.max)
-        else:
-            group(c(p, 0, W), [("I", x)])
-            group(c(p, W, W), [("PM", x)])
-            if Mv is not None:
-                sv = Mv
         t = "S1" if n0 < R else "S2" if n0 < 1024 else "S3"
         ta, tb = c(t, 2 * n0, W, 2), c(t, 2 * n0 + 1, W, 2)
-        tt(ta, sv, c(p, 0, W), A.max)
-        tt(tb, sv, c(p, W, W), A.max)
-        group(c(q, 0, W), [("NON", sv), ("LO", ta), ("HI", tb)])
         fd = c("fd", n0, W)
+        if k in GAP[r]:
+            v = "v%d" % stream
+            group(c(p, 0, W), ya + [("NI", sv)])
+            group(c(p, W, W), yb + [("NI", sv)])
+            either(c(v, 0, 2 * W), c(p, 0, 2 * W), AF.Relu, 1.0, 0.0, 0.0, A.max)
+            group(c(q, 0, W), [("L2", c(v, 0, W)), ("HI", c(v, W, W))])
+            wa, wb = [("I", sv), ("I", c(v, 0, W))], [("I", sv), ("I", c(v, W, W))]
+        else:
+            group(c(p, 0, W), ya)
+            group(c(p, W, W), yb)
+            tt(ta, sv, c(p, 0, W), A.max)
+            tt(tb, sv, c(p, W, W), A.max)
+            group(c(q, 0, W), [("NON", sv), ("L2", ta), ("HI", tb)])
+            wa, wb = [("I", ta)], [("I", tb)]
         either(fd, c(q, 0, W), AF.Relu, -1.0, 1.0, 0.0, A.is_equal)
-        group(c(q, 0, W), [("GA", fd)])
-        group(c(q, W, W), [("HB", fd)])
-        tt(ta, ta, c(q, 0, W), A.max)
-        tt(tb, tb, c(q, W, W), A.max)
+        if k in GAP[r] or k in SUM[r]:
+            o = p if k in GAP[r] or k < 4 or k in STEST else q
+            group(c(q, 0, W), wa + [("GA", fd)])
+            group(c(o, W, W), wb + [("HB", fd)])
+            ecopy(ta, c(q, 0, W))
+            ecopy(tb, c(o, W, W))
+        else:
+            group(c(q, 0, W), [("GA", fd)])
+            group(c(q, W, W), [("HB", fd)])
+            tt(ta, ta, c(q, 0, W), A.max)
+            tt(tb, tb, c(q, W, W), A.max)
         if sv != s:
-            ecopy(s, sv)
+            asel(s, sv, [[0, W]], A.is_equal, 0, 0)
         if n0 >= 1024:
-            premises(r, n0, stream)
-            tt(c("z%d" % stream, 0, 2 * W), c("ab%d" % stream, 0, 2 * W), c(p, 0, 2 * W), A.is_lt)
+            test(r, n0, stream, "z%d" % stream, k in GAP[r] or k in STEST)
 
-    def up(r, n0, stream):
-        p, q = "b%d" % (2 * stream), "b%d" % (2 * stream + 1)
-        x, s, fd, dm, zi = c("x", n0, W), c("s", n0, W), c("fd", n0, W), state(n0), c("zi", n0, W)
-        ab, v, C = "ab%d" % stream, "v%d" % stream, "C%d" % r
-        if n0 >= 1024:
-            v = "z%d" % stream
-        elif n0 in STEST:
-            premises(r, n0, stream)
+    def test(r, n0, stream, v, fresh=True):
+        p, ab, x = "b%d" % (2 * stream), "ab%d" % stream, c("x", n0, W)
+        premises(r, n0, stream)
+        if n0 // W in STEST:
             group(c(p, 0, W), [("I", x), ("NI", c(ab, 0, W))])
             group(c(p, W, W), [("PM", x), ("NI", c(ab, W, W))])
             either(c(v, 0, 2 * W), c(p, 0, 2 * W), AF.Relu, 1.0, 0.0, 0.0, A.max)
-        else:
+            return
+        if fresh:
             group(c(p, 0, W), [("I", x)])
             group(c(p, W, W), [("PM", x)])
-            premises(r, n0, stream)
-            tt(c(v, 0, 2 * W), c(ab, 0, 2 * W), c(p, 0, 2 * W), A.is_lt)
-        group(c(q, 0, W), [("QF", fd), ("QA", c(v, 0, W)), ("QB", c(v, W, W))])
-        either(dm, c(q, 0, W), AF.Sign, 1.0, 0.0, -1.0, A.max, 1.0, A.min)
-        group(c(p, 0, W), [("I", zi), ("HB", dm)])
-        group(c(p, W, W), [("PM", zi), ("HA", dm)])
+        tt(c(v, 0, 2 * W), c(ab, 0, 2 * W), c(p, 0, 2 * W), A.is_lt)
+
+    def up(r, n0, stream):
+        p, q = "b%d" % (2 * stream), "b%d" % (2 * stream + 1)
+        s, fd, dm, zi = c("s", n0, W), c("fd", n0, W), state(n0), c("zi", n0, W)
+        ab, v, C = "ab%d" % stream, "v%d" % stream, "C%d" % r
+        if n0 >= 1024:
+            v = "z%d" % stream
+        else:
+            test(r, n0, stream, v)
+        va, vb = c(v, 0, W), c(v, W, W)
+        short = n0 // W in SHORT[r]
+        if short:
+            group(c(p, 0, W), [("I", zi), ("XF", fd), ("XA", va), ("XB", vb)])
+            group(c(p, W, W), [("PM", zi), ("YF", fd), ("YA", va), ("YB", vb)])
+        if r < RO - 1 or not short:
+            group(c(q, 0, W), [("QF", fd), ("QA", va), ("QB", vb)])
+            either(dm, c(q, 0, W), AF.Sign, 1.0, 0.0, -1.0, A.max, 1.0, A.min)
+        if not short:
+            group(c(p, 0, W), [("I", zi), ("HB", dm)])
+            group(c(p, W, W), [("PM", zi), ("HA", dm)])
         tm = c("tm%d" % stream, 0, W)
         tt(tm, c(ab, 0, W), c(p, 0, W), A.min)
         tt(c(p, W, W), c(ab, W, W), c(p, W, W), A.min)
@@ -366,8 +408,29 @@ def _program():
             return
         if n0 >= R:
             either(c("K", 2 * n0 + 1, W, 2), dm, AF.Copy, all_("sg"), 0.0, all_("sg"), A.mult)
-        group(c(q, W, W), [("I", s), ("PB", dm)])
-        either(s, c(q, W, W), AF.Relu, 1.0, -256.0, -256.0, A.add, 0.0, A.max)
+        if n0 >= R or not AHEAD:
+            group(c(q, W, W), [("I", s), ("PB", dm)])
+            either(s, c(q, W, W), AF.Relu, 1.0, -256.0, -256.0, A.add, 0.0, A.max)
+
+    def roots(r):
+        x, s, fd, Mv, p, q = c("x", 0, W), c("s", 0, W), c("fd", 0, W), all_("ar%d" % r), "b2", "b3"
+        wa, wb, fw, va, vb = c("v1", 0, W), c("v1", W, W), c("tm1", 0, W), c("v0", 0, W), c("v0", W, W)
+        group(c(p, 0, W), [("I", x)])
+        group(c(p, W, W), [("PM", x)])
+        tt(wa, Mv, c(p, 0, W), A.max)
+        tt(wb, Mv, c(p, W, W), A.max)
+        group(c(q, 0, W), [("NON", Mv), ("L2", wa), ("HI", wb)])
+        either(fw, c(q, 0, W), AF.Relu, -1.0, 1.0, 0.0, A.is_equal)
+        group(c(q, W, W), [("ZF", fd), ("YB", va), ("YB", vb)])
+        group(c(p, 0, W), [("I", wa), ("GA", fw), ("YF", fd), ("YA", va), ("YB", vb)])
+        group(c(p, W, W), [("I", wb), ("HB", fw), ("XF", fd), ("XA", va), ("XB", vb)])
+        tt(s, s, c(q, W, W), A.min)
+        tt(c("S1", 0, W, 2), s, c(p, 0, W), A.max)
+        tt(c("S1", 1, W, 2), s, c(p, W, W), A.max)
+        group(c(q, 0, W), [("NB", all_("d0")), ("I", Mv)])
+        tt(s, s, c(q, 0, W), A.max)
+        group(c(q, W, W), [("ZS", all_("d0")), ("I", fw)])
+        ts(fd, c(q, W, W), 0.0, A.max, 1.0, A.min)
 
     def wrap(out, src, k0):
         group(out, [(c("sa", 128 * q, 128), c(src, k0 + q, out[2], 16)) for q in range(16)])
@@ -381,8 +444,10 @@ def _program():
         O, On, k0, z = "O%d" % (r - 1), "O%d" % r, (k - 3) * W, "b%d" % (6 + k % 2)
         off, o0 = offsets(r - 1, k)
         g0 = (k % 3) * 16 * W
-        for h in range(0, W, KU):
-            gather(c("kg", g0 + 16 * h, 16 * KU), all_("K"), c(off, o0 + h, KU))
+        h = 0
+        for u in KS[k - 3]:
+            gather(c("kg", g0 + 16 * h, 16 * u), all_("K"), c(off, o0 + h, u))
+            h += u
         if k in ONE[r - 1]:
             parts = [(0, W, 1, lambda j: j)]
         else:
@@ -397,7 +462,7 @@ def _program():
         tt(c("w1", wo, m), c("w0", wo, m), w, A.add)
         vcopy(c("wu", wo, m), c("w1", wo, m))
         Ox, tg, cc, mv, on = c("Ox", k0, W), c("tg", k0, W), c("cc", k0, W), c("mm", k0, W), c("one", 0, W)
-        gather(tg, all_("lt1" if r == 2 and k == 6 else "lt0"), c("wu", wo, m), "V")
+        add("gts", "V", {"V": (50, 0, W, 0)}, [c("ui", 0, 2 * M + 16), c("wu", wo, m)], [tg], out=tg, win=c("ui", 0, 2 * M + 16), off=c("wu", wo, m), s1=-H)
         group(c(z, 0, W), [("PM", tg)])
         tt(cc, Ox, c(z, 0, W), A.max)
         group(c(z, W, W), [("C1m", on), ("BON", cc)])
@@ -406,19 +471,21 @@ def _program():
         nl = c(On, k0, W)
         tt(nl, mv, c(z, 0, W), A.min)
         if k in ONE[r]:
-            group(c(z, W, W), [("I", nl)])
-            ts(c("ov%d" % r, k0, W), c(z, W, W), float(H), A.add)
+            ts(c("ov%d" % r, k0, W), nl, float(H), A.add)
         else:
             halves(c("ov%d" % r, k0, W), nl, c(z, W, W), E)
-        if r == 1 and k < 6:
-            widen(c("lt1", M + k0, W), nl, c(z, 0, W))
+        if r == 1 and k == 6:
+            ts(c("ui", M, M), c(On, 0, M), H, A.add)
 
     def send(src, dst, lo, to, rs, ls):
         j = add("send", "G", {"G": (300, 0, 0, 0)}, [src], [], src=src, dst=dst, at=(lo, lo + R), to=to, rs=rs, lat=2500.0, sem=(ls, 8))
-        add("arrive", "R", {"R": (0, 0, 0, 0)}, [], [c(dst, lo, R)], lat=1000.0, sem=(rs, 8), after=j)
+        add("arrive", "R", {"R": (0, 0, 0, 0)}, [], [c(dst, lo, R)], lat=FAR[rs], sem=(rs, 8), after=j)
 
     for r in range(RO):
-        down(r, 0, 0, None if r == 0 else all_("ar%d" % r))
+        if r and AHEAD:
+            roots(r)
+        else:
+            down(r, 0, 0, None if r == 0 else all_("ar%d" % r))
         dma(c("S2", 0, 512), c("S1", 0, 512))
         for k in range(3):
             if r and EARLY:
@@ -526,7 +593,7 @@ def _schedule(ops):
     return order, eng, max(done)
 
 
-STEAL, PEN, TOL, MIX, PASSES = 200.0, 4.0, 0.0, 0.6, 4
+STEAL, PEN, TOL, MIX, PASSES = 1500.0, 4.0, 0.0, 0.6, 4
 
 
 def _forward(ops, succ, lst, tol):
@@ -541,7 +608,9 @@ def _forward(ops, succ, lst, tol):
             t = 0.0
             for p, hard in o["preds"].items():
                 d = done[p]
-                if eng[p] != e or ops[p]["sem"]:
+                if hard == "order":
+                    d -= ops[p]["lat"]
+                elif eng[p] != e or ops[p]["sem"]:
                     d += XLAT
                 elif hard is not None and e != "P":
                     d += 60.0
@@ -638,7 +707,9 @@ def _backward(ops, succ, eng, done):
         t = o["lat"]
         for j in succ[i]:
             d = back[j] + o["lat"]
-            if eng[j] != e or o["sem"]:
+            if ops[j]["preds"][i] == "order":
+                d = back[j]
+            elif eng[j] != e or o["sem"]:
                 d += XLAT
             elif ops[j]["preds"][i] is not None and e != "P":
                 d += 60.0
@@ -676,7 +747,131 @@ def _schedule(ops):
             best = (order, eng, max(done))
         new = _backward(ops, succ, eng, done)
         lst = [MIX * a + (1 - MIX) * b for a, b in zip(new, lst)] if k else new
-    return best
+    return _improve(ops, best[0], best[1]) if STEPS else best
+
+
+STEPS, SEED, HEAT, LEAN = 36000, 2, 100.0, 0.1
+CASES = ((1.04, 0.55, 180.0), (1.6, 0.45, 150.0))
+
+
+def _improve(ops, order, eng):
+    n = len(ops)
+    names = "VSPGYR"
+    pre = [[(p, bool(ops[p]["sem"]), h is not None) for p, h in o["preds"].items() if h != "order"] for o in ops]
+    pset = [set(o["preds"]) for o in ops]
+    lat = [o["lat"] for o in ops]
+    costs = [[{names.index(e): f + CYC * (a + ge * g) + p * pc for e, (f, a, ge, p) in o["cyc"].items()} for o in ops] for g, pc, xl in CASES]
+    flex = [len(o["engs"]) > 1 for o in ops]
+    both = [j for j in range(n) if flex[j]]
+    eng = [names.index(e) for e in eng]
+    state = [SEED]
+
+    def rnd():
+        state[0] = (state[0] * 6364136223846793005 + 1442695040888963407) % 2 ** 64
+        return (state[0] >> 11) / 2.0 ** 53
+
+    def run(order, eng, cost, xl, a, old):
+        done, why, q = (list(old[0]), list(old[1]), list(old[2])) if old else ([0.0] * n, [-1] * n, [False] * n)
+        free, last = [0.0] * 6, [-1] * 6
+        k, miss = a - 1, 5
+        while k >= 0 and miss:
+            j = order[k]; e = eng[j]
+            if e != 5 and last[e] < 0:
+                last[e] = j; free[e] = done[j] - lat[j]; miss -= 1
+            k -= 1
+        for i in order[a:]:
+            e = eng[i]; t = free[e]; w = last[e]; isq = True
+            for p, s, h in pre[i]:
+                d = done[p]
+                if s or eng[p] != e:
+                    d += xl
+                elif h and e != 2:
+                    d += 60.0
+                if d > t:
+                    t = d; w = p; isq = False
+            t += cost[i][e]
+            if e != 5:
+                free[e] = t; last[e] = i
+            done[i] = t + lat[i]; why[i] = w; q[i] = isq
+        return done, why, q
+
+    def value(order, eng, a, old):
+        out = [run(order, eng, c, CASES[k][2], a, old[k] if old else None) for k, c in enumerate(costs)]
+        return sum(max(r[0]) for r in out) / len(out) + LEAN * sum(costs[0][j][0] for j in both if not eng[j]), out
+
+    def chains(info):
+        res = []
+        for done, why, q in info:
+            i = done.index(max(done)); path = []
+            while i >= 0:
+                if flex[i] or q[i]:
+                    path.append(i)
+                i = why[i]
+            res.append(path)
+        return res
+
+    cur, info = value(order, eng, 0, None)
+    pth = chains(info)
+    best = (cur, order, eng)
+    for step in range(STEPS):
+        k = int(rnd() * len(info))
+        done, why, q = info[k]
+        v = pth[k][int(rnd() * len(pth[k]))]
+        r = rnd()
+        if step % 256 == 0:
+            d0, c0 = info[0][0], costs[0]
+            at = {j: (d0[j] - lat[j] - c0[j][eng[j]], z) for z, j in enumerate(order)}
+            order = sorted(order, key=lambda j: at[j])
+        if r < 0.1:
+            v = both[int(rnd() * len(both))]
+            if eng[v]:
+                continue
+        no, ne = order, eng
+        if flex[v] and (r < 0.4 or not q[v]):
+            ne = list(eng); ne[v] = 1 - eng[v]; a = order.index(v)
+        elif why[v] >= 0:
+            u = why[v]
+            a, b = order.index(u), order.index(v)
+            far = (0, 0, 1, 2, 4, 8)[int(rnd() * 6)]
+            if r > 0.7:
+                for _ in range(far):
+                    z = b + 1
+                    while z < n and eng[order[z]] != eng[v]:
+                        z += 1
+                    if z < n:
+                        b = z
+                mv = {u}
+                for j in order[a + 1:b + 1]:
+                    if pset[j] & mv:
+                        mv.add(j)
+                if v in mv:
+                    continue
+                seg = order[a:b + 1]
+                no = order[:a] + [j for j in seg if j not in mv] + [j for j in seg if j in mv] + order[b + 1:]
+            else:
+                for _ in range(far):
+                    z = a - 1
+                    while z >= 0 and eng[order[z]] != eng[v]:
+                        z -= 1
+                    if z >= 0:
+                        a = z
+                need, mv = set(pset[v]), {v}
+                for j in reversed(order[a:b]):
+                    if j in need:
+                        mv.add(j); need |= pset[j]
+                if u in mv:
+                    continue
+                seg = order[a:b + 1]
+                no = order[:a] + [j for j in seg if j in mv] + [j for j in seg if j not in mv] + order[b + 1:]
+        else:
+            continue
+        val, inf = value(no, ne, a, info)
+        if val <= cur or rnd() < math.exp((cur - val) / max(1.0, HEAT * (1 - step / STEPS))):
+            cur, info, order, eng = val, inf, no, ne
+            pth = chains(info)
+            if cur < best[0]:
+                best = (cur, order, eng)
+    return best[1], [names[e] for e in best[2]], best[0]
 
 
 def _waits(ops, order, eng):
@@ -689,7 +884,7 @@ def _waits(ops, order, eng):
         k = know[e]
         w = {}
         if e != "R":
-            ps = [p for p, hard in o["preds"].items() if ops[p]["sem"] or eng[p] != e or (hard is not None and e != "P")]
+            ps = [p for p, hard in o["preds"].items() if hard != "order" and (ops[p]["sem"] or eng[p] != e or (hard is not None and e != "P"))]
             ps.sort(key=lambda p: -pos[p])
             for p in ps:
                 s, val = sem[p]
@@ -779,6 +974,8 @@ def rank_program(g, core, T, topo):
         elif kind == "gather":
             src = ap(o["win"]).indirect(ap(o["off"]))
             x = q.tensor_copy(out, src) if e == "V" else q.activation(out, src, AF.Copy)
+        elif kind == "gts":
+            x = q.tensor_scalar(out, ap(o["win"]).indirect(ap(o["off"])), o["s1"], None, A.add)
         elif kind == "gmin":
             x = q.tensor_tensor(out, ap(o["win"]).indirect(ap(o["off"])), ap(o["b"]), A.min)
         elif kind == "mm":

@@ -1,22 +1,22 @@
 import math
 
-from concourse.mybir import AluOpType as A, AxisListType, ActivationFunctionType as AF
+from concourse.mybir import AluOpType as A, ActivationFunctionType as AF
 
 R, M, V, F, RO = 256, 768, 1792, 512, 3
 E = 2 * V
 H = V
 W = 256
-U = 64
 BF, F2, F4, I4, U2 = "bfloat16", "float16", "float32", "int32", "uint16"
 BIG = 8192.0
 
-ONE = ((0, 1, 4, 6), (4, 5, 6), (4, 5, 6))
-STEST = ()
-PIECES = ((32, 96), (64, 64), (64, 64), (64, 64))
+ONE = ((0, 4, 5, 6), (4, 5), (4, 5, 6))
+PIECES = ((32, 96), (64, 64), (64, 64))
+WHOLE = (64, 64, 64, 64)
 KS = ((32,) * 8, (32,) * 8, (64,) * 4, (64,) * 4)
-GAP, SUM, SHORT = ((), (), ()), (range(7),) * 3, ((), (), range(7))
-EARLY, GHOST, AHEAD = False, 0, False
-FAR = {"ra0": 6000.0, "ra1": 4000.0, "rb0": 9000.0, "rb1": 9000.0}
+WIDE = ((0, 512, "a"), (512, 256, "b"))
+NARROW = ((0, 256, "a"), (256, 256, "d"), (512, 256, "b"))
+TAIL = ((0, 256, "b"), (256, 384, "e"), (640, 128, "b"))
+PARTS = (TAIL, NARROW, WIDE)
 
 SCRATCH = {}
 
@@ -25,37 +25,40 @@ def _b(name, n, d=BF):
     SCRATCH[name] = ("sbuf", [128, n], d)
 
 
-for _n in ("I", "tb", "ON", "PM", "t1", "t2", "DL", "DH", "LO", "HI", "B", "g1", "g2", "g3", "g4", "GA", "QA", "QB", "QF", "HA", "HB", "NB", "PB",
-           "ZF", "ZS", "L2", "XF", "YF", "XA", "YA", "XB", "YB", "NON", "NI", "CF", "C1m", "C2m", "BON", "NBON"):
+for _n in ("I", "tb", "ON", "PM", "t1", "t2", "DL", "DH", "HI", "L2", "B", "g1", "g2", "g3", "g4", "GA", "QA", "QB", "QF", "HA", "HB", "NB", "PB",
+           "XF", "YF", "XA", "YA", "XB", "YB", "NON", "CF", "C1m", "C2m", "BON", "NBON"):
     _b(_n, 128)
 _b("D2", 128, F4); _b("one", W); _b("sg", 1, F4)
 _b("WF", 2048); _b("sa", 2048); _b("w0", 64, F4)
-_b("R8", 1536); _b("R16", 1024)
+_b("R8", 2048); _b("R16", 2048)
 _b("x", V); _b("s", V); _b("zi", V); _b("ui", V + 16, I4); _b("pi", 224, I4); _b("po", 224, U2)
 _b("oF", M, U2); _b("oN", M, U2); _b("OL", M, F2)
 for _r in range(RO):
     _b("ov%d" % _r, 1024, U2); _b("O%d" % _r, 1024, F2)
     _b("C%d" % _r, V + R + F); _b("ar%d" % _r, R); _b("gs%d" % _r, R)
 _b("S1", 528); _b("S2", 3600); _b("S3", 3600); _b("K", 3600)
-_b("ga", 16 * M); _b("sc", 16 * M); _b("kg", 48 * W)
+_b("ga", 16 * M); _b("sc", 80 * W); _b("kg", 48 * W)
 _b("fd", V); _b("d0", R)
-for _i in range(3):
-    _b("v%d" % _i, 512); _b("z%d" % _i, 512); _b("ab%d" % _i, 512); _b("tm%d" % _i, 256)
+for _n in "abcde":
+    _b("v" + _n, 1024); _b("ab" + _n, 1024); _b("tm" + _n, 512)
 _b("Ox", 1024, F2); _b("tg", 1024, F2); _b("cc", 1024, F2); _b("mm", 1024, F2)
 _b("w1", 64, I4); _b("wu", 64, U2)
-BANKS = ["b%d" % _i for _i in range(8)]
-for _n in BANKS:
-    SCRATCH[_n] = ("psum", [128, 512], F4)
-ND = 64
+PSUM = {"pa": 1024, "qa": 1024, "pb": 512, "qb": 512, "z0": 512, "z1": 512}
+for _n in PSUM:
+    SCRATCH[_n] = ("psum", [128, PSUM[_n]], F4)
+ND = 48
 SEMAPHORES = ["eV", "eS", "eP", "eG"] + ["d%d" % _i for _i in range(ND)] + ["%s%d" % (_p, _r) for _p in ("ra", "rb", "la", "lb") for _r in range(RO - 1)]
 EXT = {"piv": BF, "safe": BF, "lem": BF, "leaf": BF, "uses": I4, "prem": I4, "yc": BF, "ys": BF}
 
-CYC, XLAT, GCY, PCY = 0.83, 220.0, 1.3, 0.5
-PEN, SLACK, FAC = 8000.0, 150.0, (0.6, 0.7)
+CYC, GCY, PCY, XLAT = 0.83, 1.3, 0.5, 220.0
+CASES = ((1.2, 0.58, 220.0), (1.72, 0.45, 150.0))
+FAR = {"ra0": 6000.0, "ra1": 4000.0, "rb0": 9000.0, "rb1": 9000.0}
+STEAL, PEN, MIX, PASSES = 1500.0, 4.0, 0.6, 4
+STEPS, SEED, HEAT, LEAN = 150000, 2, 50.0, 0.05
 
 
 def _psum(v):
-    return v[0] in BANKS
+    return v[0] in PSUM
 
 
 def _two(v):
@@ -77,7 +80,7 @@ def _covers(a, b):
 
 
 def _program():
-    ops, bufs, last, nd = [], {}, {}, [0, 0]
+    ops, bufs, last, nd, gate = [], {}, {}, [0, 0], {}
 
     def add(kind, engs, cyc, reads, writes, **kw):
         i = len(ops)
@@ -95,25 +98,29 @@ def _program():
             for (q, j) in b["r"]:
                 if _over(q, reg):
                     preds.setdefault(j, False)
-        for v in list(reads) + list(writes):
-            if _psum(v) and v[0] in last and last[v[0]] != i:
-                preds.setdefault(last[v[0]], None)
-        for v in list(reads) + list(writes):
-            if _psum(v):
-                last[v[0]] = i
-        preds.pop(i, None)
+        banks = {(v[0], k) for v in list(reads) + list(writes) if _psum(v) for k in range(v[1] // 512, (_hi(v) - 1) // 512 + 1)}
+        for k in sorted(banks):
+            if k in last:
+                preds.setdefault(last[k], None)
+            last[k] = i
         for v in writes:
             reg = (v[1], _hi(v), v[3]); b = bufs[v[0]]
             b["w"] = [z for z in b["w"] if not _covers(reg, z[0])] + [(reg, i)]
             b["r"] = [z for z in b["r"] if not _covers(reg, z[0])]
         for v in reads:
             bufs[v[0]]["r"].append(((v[1], _hi(v), v[3]), i))
+        if engs in gate:
+            preds.setdefault(gate[engs], None)
         op = {"kind": kind, "engs": engs, "cyc": cyc, "preds": preds, "id": i, "lat": 0.0, "sem": None}
         op.update(kw)
         ops.append(op)
         return i
 
     def c(name, lo, n, st=1):
+        if name in ("pd", "qd"):
+            return (name[0] + "a", lo + 512, n, st)
+        if name in ("pe", "qe"):
+            return (name[0] + "a", lo + 128, n, st)
         return (name, lo, n, st)
 
     def all_(name):
@@ -139,15 +146,14 @@ def _program():
         add("tt", "V", {"V": (60, out[2] * (1 if _psum(a) or _psum(b) else 2), 0, 0)}, [a, b], [out], out=out, a=a, b=b, op=op)
 
     def ts(out, a, s1, op0, s2=None, op1=None):
-        rd = [a] + ([s1] if isinstance(s1, tuple) else [])
-        add("ts", "V", {"V": (60, out[2] * _fast(out, a), 0, 0)}, rd, [out], out=out, a=a, s1=s1, s2=s2, op0=op0, op1=op1)
+        add("ts", "V", {"V": (60, out[2] * _fast(out, a), 0, 0)}, [a], [out], out=out, a=a, s1=s1, s2=s2, op0=op0, op1=op1)
 
     def vcopy(out, a):
         add("copy", "V", {"V": (60, out[2] * _fast(out, a), 0, 0)}, [a], [out], out=out, a=a)
 
-    def either(out, a, func, scale, bias, s1, op0, s2=None, op1=None, engs="SV"):
+    def either(out, a, func, scale, bias, s1, op0, s2=None, op1=None):
         rd = [a] + ([s1] if isinstance(s1, tuple) else [])
-        add("either", engs, {"S": (70, out[2], 0, 0), "V": (60, out[2] * _fast(out, a), 0, 0)}, rd, [out], out=out, a=a,
+        add("either", "SV", {"S": (70, out[2], 0, 0), "V": (60, out[2] * _fast(out, a), 0, 0)}, rd, [out], out=out, a=a,
             func=func, scale=scale, bias=bias, s1=s1, op0=op0, s2=s2, op1=op1)
 
     def scaled(out, a, k):
@@ -156,24 +162,23 @@ def _program():
     def ecopy(out, a):
         add("copy", "SV", {"S": (70, out[2], 0, 0), "V": (60, out[2] * _fast(out, a), 0, 0)}, [a], [out], out=out, a=a)
 
-    def scan(out, d0, d1, op0, op1):
-        add("scan", "V", {"V": (60, out[2] * .5, 0, 0)}, [d0, d1], [out], out=out, d0=d0, d1=d1, op0=op0, op1=op1)
+    def scan(out, d0, d1):
+        add("scan", "V", {"V": (60, out[2] * .5, 0, 0)}, [d0, d1], [out], out=out, d0=d0, d1=d1, op0=A.max, op1=A.min)
 
-    def gather(out, win, off, engs="SV"):
-        add("gather", engs, {"S": (65, 0, out[2], 0), "V": (50, 0, out[2], 0)}, [win, off], [out], out=out, win=win, off=off)
+    def gather(out, win, off):
+        add("gather", "SV", {"S": (65, 0, out[2], 0), "V": (50, 0, out[2], 0)}, [win, off], [out], out=out, win=win, off=off)
 
     def gmin(out, win, off, b):
         add("gmin", "V", {"V": (50, 0, out[2], 0)}, [win, off, b], [out], out=out, win=win, off=off, b=b)
 
-    def mm(out, lhs, rhs, start, stop):
-        add("mm", "P", {"P": (30, 0, 0, max(64, out[2]))}, [lhs, rhs], [out], out=out, lhs=lhs, rhs=rhs, start=start, stop=stop)
+    def group(out, terms, by=1):
+        full = [(l if isinstance(l, tuple) else all_(l), r, k == 0, k == len(terms) - 1) for k, (l, r) in enumerate(terms)]
+        for k in range(0, len(full), by):
+            z = full[k:k + by]
+            add("mm", "P", {"P": (30 * len(z), 0, 0, max(64, out[2]) * len(z))}, [v for t in z for v in t[:2]], [out], out=out, terms=z)
 
-    def group(out, terms):
-        for k, (l, r) in enumerate(terms):
-            mm(out, l if isinstance(l, tuple) else all_(l), r, k == 0, k == len(terms) - 1)
-
-    def asel(out, in_, pat, op, base, cm):
-        add("asel", "G", {"G": (170, out[2] * 2, 0, 0)}, [in_], [out], out=out, in_=in_, pat=pat, op=op, base=base, cm=cm)
+    def asel(out, in_, pat, op, base, cm, val=0.0):
+        add("asel", "G", {"G": (170, out[2] * 2, 0, 0)}, [in_], [out], out=out, in_=in_, pat=pat, op=op, base=base, cm=cm, fill=val)
 
     def iota(out, pat, base, cm):
         add("iota", "G", {"G": (130, out[2] * 2, 0, 0)}, [], [out], out=out, pat=pat, base=base, cm=cm)
@@ -194,43 +199,35 @@ def _program():
     dma(c("ui", 2 * M + 16, R), c("uses", 2 * M, R))
     for r in range(1, RO):
         dma(c("C%d" % r, V + R, F), c("leaf", 0, F))
-    one = c("one", 0, 128)
     memset(all_("one"), 1.0)
     iota(all_("D2"), [[-16, 8], [248, 2], [-1, 8]], 0, 1)
     for n, k in (("DL", 0), ("DH", 256), ("t1", 8), ("t2", 248)):
         ts(all_(n), all_("D2"), float(k), A.is_equal)
     tt(all_("I"), all_("DL"), all_("DH"), A.add)
     tt(all_("PM"), all_("t1"), all_("t2"), A.add)
-    asel(all_("tb"), one, [[-16, 8], [0, 16]], A.is_ge, 0, 1)
+    asel(all_("tb"), c("one", 0, 128), [[-16, 8], [0, 16]], A.is_ge, 0, 1)
     asel(all_("ON"), all_("tb"), [[16, 8], [0, 16]], A.is_ge, 15, -1)
-
-    def half(out, in_, h):
-        asel(all_(out), all_(in_), [[0, 8], [1, 2], [0, 8]], A.is_equal, -h, 0)
-
-    def row(out, k, a):
-        ts(all_(out), all_("B"), float(k), A.is_equal, float(a), A.mult)
-
-    def mix(out, a, b, t="g1", u="g2"):
-        row(t, 0, a); row(u, 8, b)
-        tt(all_(out), all_(t), all_(u), A.add)
     asel(all_("L2"), all_("ON"), [[0, 8], [1, 4], [0, 4]], A.not_equal, -2, 0)
-    half("HI", "ON", 1)
+    asel(all_("HI"), all_("ON"), [[0, 8], [1, 2], [0, 8]], A.is_equal, -1, 0)
     tt(all_("g3"), all_("L2"), all_("HI"), A.add)
     scaled(all_("NON"), all_("g3"), -1)
-    scaled(all_("NI"), all_("I"), -1)
+    gate["G"] = len(ops) - 3
     iota(all_("B"), [[-16, 8], [0, 16]], 0, 1)
-    row("HB", 0, 256)
-    row("g1", 8, 256); row("g2", 12, -256)
+    gate["G"] = len(ops) - 1
+    for n, k, a in (("HB", 0, 256), ("g1", 8, 256), ("g2", 12, -256)):
+        ts(all_(n), all_("B"), float(k), A.is_equal, float(a), A.mult)
     tt(all_("GA"), all_("g1"), all_("g2"), A.add)
-    memset(all_("R8"), 0.0); memset(c("R8", 0, 192, 8), 255.0)
-    memset(all_("R16"), 0.0); memset(c("R16", 0, 64, 16), 255.0)
+    ga = len(ops) - 1
     memset(c("S1", 512, 16), 255.0)
+    for n, k, u in (("R16", 16, max(WHOLE)), ("R8", 8, max(max(z) for z in PIECES))):
+        memset(c(n, 0, 16 * u), 0.0); memset(c(n, 0, 16 * u // k, k), 255.0)
+        gate["V"] = ga
     fill(c("S2", 2048, 1552), 255); fill(c("S3", E, 16), 255)
 
     def halves(out, src, bank, cap):
         ev, od = c(src[0], src[1], W // 2, 2), c(src[0], src[1] + 1, W // 2, 2)
-        group(c(bank[0], bank[1], W // 2), [("DL", ev), ("DH", od)])
-        group(c(bank[0], bank[1] + W // 2, W // 2), [("t1", ev), ("t2", od)])
+        group(c(bank[0], bank[1], W // 2), [("DL", ev), ("DH", od)], 2)
+        group(c(bank[0], bank[1] + W // 2, W // 2), [("t1", ev), ("t2", od)], 2)
         ts(out, bank, float(H), A.add, float(cap), A.min)
 
     for k in range(3):
@@ -238,15 +235,16 @@ def _program():
             ts(c("oN", k * W, W), c("ui", k * W, W), 512, A.min)
         if any(k not in ONE[r] for r in range(RO)):
             ts(c("OL", k * W, W), c("ui", k * W, W), -H, A.add)
-            halves(c("oF", k * W, W), c("OL", k * W, W), c("b%d" % (6 + k % 2), 0, W), 512)
+            halves(c("oF", k * W, W), c("OL", k * W, W), c("z%d" % (k % 2), 0, W), 512)
 
     def second(k):
         u = c("ui", M + k * W + 16 * (k == 3), W)
-        ts(c("O0", k * W, W), u, -H, A.add)
         if k + 3 in ONE[0]:
             vcopy(c("ov0", k * W, W), u)
+            ts(c("O0", k * W, W), c("ov0", k * W, W), -H, A.add)
         else:
-            halves(c("ov0", k * W, W), c("O0", k * W, W), c("b%d" % (7 - k % 2), 0, W), E)
+            ts(c("O0", k * W, W), u, -H, A.add)
+            halves(c("ov0", k * W, W), c("O0", k * W, W), c("z%d" % (1 - k % 2), 0, W), E)
         if k < 3:
             n0, w, t = ((1024, 768, 1792), (256, 768, 1024), (0, 256, 256))[k]
             for h in (0, 112):
@@ -254,40 +252,35 @@ def _program():
                 ts(c("po", j, w // 16), c("pi", j, w // 16), -t, A.add)
 
     def late():
-        scaled(all_("HA"), all_("HB"), -1)
-        row("PB", 8, 256)
-        scaled(all_("NB"), all_("PB"), -1)
-        half("LO", "ON", 0)
-        scaled(all_("g3"), all_("LO"), 8192)
-        tt(all_("QA"), all_("g3"), all_("HI"), A.add)
-        tt(all_("QB"), all_("HI"), all_("LO"), A.subtract)
-        mix("g3", 2.0 ** 28, -2.0 ** 27)
-        mix("g4", 1, 1)
-        half("g1", "g3", 0); half("g2", "g4", 1)
-        tt(all_("QF"), all_("g1"), all_("g2"), A.add)
-        for n, m, k in (("XF", "g3", 1024), ("YF", "g3", -1024), ("XA", "ON", 2 ** 23), ("YA", "ON", -2 ** 23), ("XB", "ON", -1024), ("YB", "ON", 1024)):
+        def rows(n, lo, hi):
+            asel(all_(n), all_(n), [[-16, 8], [0, 16]], A.is_ge, -lo, 1)
+            asel(all_(n), all_(n), [[16, 8], [0, 16]], A.is_ge, hi, -1)
+        for n, lo, hi in (("QA", 32, 1), ("QB", -1, 1)):
+            iota(all_(n), [[0, 8], [hi - lo, 2], [0, 8]], lo, 0)
+            rows(n, 0, 15)
+        for n, k in (("QF", 2048), ("g4", 0)):
+            iota(all_(n), [[2048, 8], [k, 2], [0, 8]], 960, -128)
+            rows(n, 0, 11)
+        fill(all_("PB"), 32)
+        rows("PB", 8, 15)
+        fill(all_("C1m"), H // 14)
+        asel(all_("C1m"), all_("C1m"), [[-16, 8], [0, 16]], A.not_equal, 0, 1, -BIG * 16 * H)
+        rows("C1m", 0, 14)
+        for n, m, k in (("HA", "HB", -1), ("NB", "PB", -1), ("XF", "g4", 256), ("YF", "g4", -256), ("XA", "ON", 8192), ("YA", "ON", -8192),
+                        ("XB", "ON", -256), ("YB", "ON", 256), ("CF", "I", H - 4096), ("C2m", "C1m", -1), ("BON", "ON", BIG), ("NBON", "ON", -BIG)):
             scaled(all_(n), all_(m), k)
-        if AHEAD:
-            scaled(all_("ZF"), all_("g4"), 1024)
-            row("g1", 0, -2)
-            tt(all_("ZS"), all_("g1"), all_("QB"), A.mult)
         for k in range(0, V, 2 * W):
             n = min(2 * W, V - k)
-            ts(c("zi", k, n), c("x", k, n), 0.0, A.is_equal, 255.0, A.mult)
-        tt(all_("g4"), all_("DH"), all_("DL"), A.subtract)
-        add("red", "V", {"V": (60, 128, 0, 0)}, [all_("g4")], [all_("sg")], out=all_("sg"), a=all_("g4"))
-        scaled(all_("CF"), all_("I"), H - 4096)
-        mix("C1m", -BIG * 16 * H, H)
-        scaled(all_("C2m"), all_("C1m"), -1)
-        scaled(all_("BON"), all_("ON"), BIG)
-        scaled(all_("NBON"), all_("ON"), -BIG)
+            either(c("zi", k, n), c("x", k, n), AF.Relu, -255.0, 255.0, 0.0, A.is_equal, 255.0, A.mult)
+        group(c("z1", 0, 1), [("QB", c("one", 0, 1))])
+        scaled(all_("sg"), c("z1", 0, 1), 1.0 / 16)
         iota(all_("WF"), [[512, 16], [0, 8], [-512, 16]], 256, 0)
         asel(all_("WF"), all_("WF"), [[-1, 16], [0, 8], [1, 16]], A.is_ge, 0, 0)
         asel(all_("WF"), all_("WF"), [[0, 16], [-16, 8], [0, 16]], A.is_ge, 0, 1)
         asel(all_("WF"), all_("WF"), [[0, 16], [16, 8], [0, 16]], A.is_ge, 15, -1)
         asel(all_("sa"), all_("WF"), [[1, 16], [0, 8], [-1, 16]], A.is_equal, 0, 0)
-        for k in range(0, 2048, 512):
-            scaled(c("sa", k, 512), c("sa", k, 512), -1.0 / 512)
+        for k in range(0, 2048, 1024):
+            scaled(c("sa", k, 1024), c("sa", k, 1024), -1.0 / 512)
         fill(c("K", 0, 512), 0); fill(c("K", E, 16), 0)
         memset(c("ui", 2 * M, 16), E)
 
@@ -299,152 +292,99 @@ def _program():
     def lists(r, k):
         win = all_("S1" if k < 3 else "S2" if k < 6 else "S3")
         off, o0 = offsets(r, k)
-        g0 = (k % 3) * 16 * W
+        g0, h = (k % 3) * 16 * W, 0
+        s0 = 40 * W * (k // 3 % 2) + sum(16 * W if j in ONE[r] else 8 * W for j in range(k - k % 3, k))
         if k in ONE[r]:
-            for h in range(0, W, U):
-                gather(c("ga", g0 + 16 * h, 16 * U), win, c(off, o0 + h, U))
-                scan(c("sc", g0 + 16 * h, 16 * U), all_("R16"), c("ga", g0 + 16 * h, 16 * U), A.max, A.min)
-            return c("sc", g0 + 15, W, 16)
-        s0 = g0 + (k // 3 % 2) * 8 * W
-        h = 0
-        for u in PIECES[k % 3 if k < 6 else 3]:
+            for u in WHOLE:
+                gather(c("ga", g0 + 16 * h, 16 * u), win, c(off, o0 + h, u))
+                scan(c("sc", s0 + 16 * h, 16 * u), c("R16", 0, 16 * u), c("ga", g0 + 16 * h, 16 * u))
+                h += u
+            return s0 + 15, 16
+        for u in PIECES[k % 3 if k < 6 else 2]:
             a, b = c("ga", g0 + 16 * h, 16 * u), c("ga", g0 + 8 * W + 16 * h, 16 * u)
             gather(a, win, c(off, o0 + h, u))
             gmin(b, win, c(off, o0 + W // 2 + h, u), a)
-            scan(c("sc", s0 + 16 * h, 16 * u), c("R8", 0, 16 * u), b, A.max, A.min)
+            scan(c("sc", s0 + 16 * h, 16 * u), c("R8", 0, 16 * u), b)
             h += u
-        return c("sc", s0 + 7, W, 8)
+        return s0 + 7, 8
 
-    def state(n0):
-        return all_("d0") if n0 < R else c("K", 2 * n0, W, 2)
+    def state(n0, n):
+        return all_("d0") if n0 < R else c("K", 2 * n0, n, 2)
 
-    def premises(r, n0, stream):
+    def test(r, n0, n, z, fresh):
         lo = 256 if n0 < R else 1024 if n0 < 1024 else 1792
-        win = c("C%d" % r, lo, V + R + F - lo)
         for h in (0, 1):
-            gather(c("ab%d" % stream, h * W, W), win, c("po", 112 * h + n0 // 16, W // 16))
-
-    def down(r, n0, stream, Mv):
-        p, q = "b%d" % (2 * stream), "b%d" % (2 * stream + 1)
-        x, s, dm = c("x", n0, W), c("s", n0, W), state(n0)
-        k = n0 // W
-        sv = s if r or Mv is None else Mv
-        ya, yb = [("I", x)] + [("HA", dm)] * (r > 0), [("PM", x)] + [("HB", dm)] * (r > 0)
-        if r:
-            group(c(q, W, W), [("NB", dm), ("I", Mv)])
-            tt(s, s, c(q, W, W), A.max)
-        t = "S1" if n0 < R else "S2" if n0 < 1024 else "S3"
-        ta, tb = c(t, 2 * n0, W, 2), c(t, 2 * n0 + 1, W, 2)
-        fd = c("fd", n0, W)
-        if k in GAP[r]:
-            v = "v%d" % stream
-            group(c(p, 0, W), ya + [("NI", sv)])
-            group(c(p, W, W), yb + [("NI", sv)])
-            either(c(v, 0, 2 * W), c(p, 0, 2 * W), AF.Relu, 1.0, 0.0, 0.0, A.max)
-            group(c(q, 0, W), [("L2", c(v, 0, W)), ("HI", c(v, W, W))])
-            wa, wb = [("I", sv), ("I", c(v, 0, W))], [("I", sv), ("I", c(v, W, W))]
-        else:
-            group(c(p, 0, W), ya)
-            group(c(p, W, W), yb)
-            tt(ta, sv, c(p, 0, W), A.max)
-            tt(tb, sv, c(p, W, W), A.max)
-            group(c(q, 0, W), [("NON", sv), ("L2", ta), ("HI", tb)])
-            wa, wb = [("I", ta)], [("I", tb)]
-        either(fd, c(q, 0, W), AF.Relu, -1.0, 1.0, 0.0, A.is_equal)
-        if k in GAP[r] or k in SUM[r]:
-            o = p if k in GAP[r] or k < 4 or k in STEST else q
-            group(c(q, 0, W), wa + [("GA", fd)])
-            group(c(o, W, W), wb + [("HB", fd)])
-            ecopy(ta, c(q, 0, W))
-            ecopy(tb, c(o, W, W))
-        else:
-            group(c(q, 0, W), [("GA", fd)])
-            group(c(q, W, W), [("HB", fd)])
-            tt(ta, ta, c(q, 0, W), A.max)
-            tt(tb, tb, c(q, W, W), A.max)
-        if sv != s:
-            asel(s, sv, [[0, W]], A.is_equal, 0, 0)
-        if n0 >= 1024:
-            test(r, n0, stream, "z%d" % stream, k in GAP[r] or k in STEST)
-
-    def test(r, n0, stream, v, fresh=True):
-        p, ab, x = "b%d" % (2 * stream), "ab%d" % stream, c("x", n0, W)
-        premises(r, n0, stream)
-        if n0 // W in STEST:
-            group(c(p, 0, W), [("I", x), ("NI", c(ab, 0, W))])
-            group(c(p, W, W), [("PM", x), ("NI", c(ab, W, W))])
-            either(c(v, 0, 2 * W), c(p, 0, 2 * W), AF.Relu, 1.0, 0.0, 0.0, A.max)
-            return
+            gather(c("ab" + z, h * n, n), c("C%d" % r, lo, V + R + F - lo), c("po", 112 * h + n0 // 16, n // 16))
+        p = "pb" if z == "c" else "p" + z
         if fresh:
-            group(c(p, 0, W), [("I", x)])
-            group(c(p, W, W), [("PM", x)])
-        tt(c(v, 0, 2 * W), c(ab, 0, 2 * W), c(p, 0, 2 * W), A.is_lt)
+            group(c(p, 0, n), [("I", c("x", n0, n))])
+            group(c(p, n, n), [("PM", c("x", n0, n))])
+        tt(c("v" + z, 0, 2 * n), c("ab" + z, 0, 2 * n), c(p, 0, 2 * n), A.is_lt)
 
-    def up(r, n0, stream):
-        p, q = "b%d" % (2 * stream), "b%d" % (2 * stream + 1)
-        s, fd, dm, zi = c("s", n0, W), c("fd", n0, W), state(n0), c("zi", n0, W)
-        ab, v, C = "ab%d" % stream, "v%d" % stream, "C%d" % r
+    def down(r, n0, n, z, Mv):
+        p, q = "p" + z, "q" + z
+        x, s, dm, fd = c("x", n0, n), c("s", n0, n), state(n0, n), c("fd", n0, n)
+        sv = s if r or Mv is None else Mv
+        if r:
+            group(c(q, n, n), [("NB", dm), ("I", Mv)])
+            tt(s, s, c(q, n, n), A.max)
+        t = "S1" if n0 < R else "S2" if n0 < 1024 else "S3"
+        ta, tb = c(t, 2 * n0, n, 2), c(t, 2 * n0 + 1, n, 2)
+        group(c(p, 0, n), [("I", x)] + [("HA", dm)] * (r > 0), 2)
+        group(c(p, n, n), [("PM", x)] + [("HB", dm)] * (r > 0), 2)
+        tt(ta, sv, c(p, 0, n), A.max)
+        tt(tb, sv, c(p, n, n), A.max)
+        group(c(q, 0, n), [("NON", sv), ("L2", ta), ("HI", tb)])
+        either(fd, c(q, 0, n), AF.Relu, -1.0, 1.0, 0.0, A.is_equal)
+        o = q if n0 >= 1024 else p
+        group(c(q, 0, n), [("I", ta), ("GA", fd)])
+        group(c(o, n, n), [("I", tb), ("HB", fd)])
+        ecopy(ta, c(q, 0, n))
+        ecopy(tb, c(o, n, n))
+        if sv != s:
+            asel(s, sv, [[0, n]], A.is_equal, 0, 0)
         if n0 >= 1024:
-            v = "z%d" % stream
-        else:
-            test(r, n0, stream, v)
-        va, vb = c(v, 0, W), c(v, W, W)
-        short = n0 // W in SHORT[r]
-        if short:
-            group(c(p, 0, W), [("I", zi), ("XF", fd), ("XA", va), ("XB", vb)])
-            group(c(p, W, W), [("PM", zi), ("YF", fd), ("YA", va), ("YB", vb)])
-        if r < RO - 1 or not short:
-            group(c(q, 0, W), [("QF", fd), ("QA", va), ("QB", vb)])
-            either(dm, c(q, 0, W), AF.Sign, 1.0, 0.0, -1.0, A.max, 1.0, A.min)
-        if not short:
-            group(c(p, 0, W), [("I", zi), ("HB", dm)])
-            group(c(p, W, W), [("PM", zi), ("HA", dm)])
-        tm = c("tm%d" % stream, 0, W)
-        tt(tm, c(ab, 0, W), c(p, 0, W), A.min)
-        tt(c(p, W, W), c(ab, W, W), c(p, W, W), A.min)
-        tt(c(C, n0, W), tm, c(p, W, W), A.max)
+            test(r, n0, n, z, False)
+
+    def up(r, n0, n, z):
+        y = "c" if n0 < R else z
+        p, q = "p" + z, "q" + z
+        s, fd, dm, zi = c("s", n0, n), c("fd", n0, n), state(n0, n), c("zi", n0, n)
+        if n0 < 1024:
+            test(r, n0, n, y, True)
+        va, vb = c("v" + y, 0, n), c("v" + y, n, n)
         if r == RO - 1:
-            dma(c("yc", n0, W), c(C, n0, W))
+            group(c(p, 0, n), [("I", zi), ("XF", fd), ("XA", va), ("XB", vb)])
+            group(c(p, n, n), [("PM", zi), ("YF", fd), ("YA", va), ("YB", vb)])
+        else:
+            group(c(q, 0, n), [("QF", fd), ("QA", va), ("QB", vb)])
+            either(dm, c(q, 0, n), AF.Sign, 1.0, 0.0, -1.0, A.max, 1.0, A.min)
+            group(c(p, 0, n), [("I", zi), ("HB", dm)])
+            group(c(p, n, n), [("PM", zi), ("HA", dm)])
+        tm, C = c("tm" + y, 0, n), c("C%d" % r, n0, n)
+        tt(tm, c("ab" + y, 0, n), c(p, 0, n), A.min)
+        tt(c(p, n, n), c("ab" + y, n, n), c(p, n, n), A.min)
+        tt(C, tm, c(p, n, n), A.max)
+        if r == RO - 1:
+            dma(c("yc", n0, n), C)
             return
         if n0 >= R:
-            either(c("K", 2 * n0 + 1, W, 2), dm, AF.Copy, all_("sg"), 0.0, all_("sg"), A.mult)
-        if n0 >= R or not AHEAD:
-            group(c(q, W, W), [("I", s), ("PB", dm)])
-            either(s, c(q, W, W), AF.Relu, 1.0, -256.0, -256.0, A.add, 0.0, A.max)
-
-    def roots(r):
-        x, s, fd, Mv, p, q = c("x", 0, W), c("s", 0, W), c("fd", 0, W), all_("ar%d" % r), "b2", "b3"
-        wa, wb, fw, va, vb = c("v1", 0, W), c("v1", W, W), c("tm1", 0, W), c("v0", 0, W), c("v0", W, W)
-        group(c(p, 0, W), [("I", x)])
-        group(c(p, W, W), [("PM", x)])
-        tt(wa, Mv, c(p, 0, W), A.max)
-        tt(wb, Mv, c(p, W, W), A.max)
-        group(c(q, 0, W), [("NON", Mv), ("L2", wa), ("HI", wb)])
-        either(fw, c(q, 0, W), AF.Relu, -1.0, 1.0, 0.0, A.is_equal)
-        group(c(q, W, W), [("ZF", fd), ("YB", va), ("YB", vb)])
-        group(c(p, 0, W), [("I", wa), ("GA", fw), ("YF", fd), ("YA", va), ("YB", vb)])
-        group(c(p, W, W), [("I", wb), ("HB", fw), ("XF", fd), ("XA", va), ("XB", vb)])
-        tt(s, s, c(q, W, W), A.min)
-        tt(c("S1", 0, W, 2), s, c(p, 0, W), A.max)
-        tt(c("S1", 1, W, 2), s, c(p, W, W), A.max)
-        group(c(q, 0, W), [("NB", all_("d0")), ("I", Mv)])
-        tt(s, s, c(q, 0, W), A.max)
-        group(c(q, W, W), [("ZS", all_("d0")), ("I", fw)])
-        ts(fd, c(q, W, W), 0.0, A.max, 1.0, A.min)
+            either(c("K", 2 * n0 + 1, n, 2), dm, AF.Copy, all_("sg"), 0.0, all_("sg"), A.mult)
+        group(c(q, n, n), [("I", s), ("PB", dm)])
+        either(s, c(q, n, n), AF.Relu, 1.0, -256.0, -256.0, A.add, 0.0, A.max)
 
     def wrap(out, src, k0):
-        group(out, [(c("sa", 128 * q, 128), c(src, k0 + q, out[2], 16)) for q in range(16)])
+        group(out, [(c("sa", 128 * q, 128), c(src, k0 + q, out[2], 16)) for q in range(16)], 8)
 
     def sums(r):
-        w = c("b6", W, 64)
+        w = c("z0", W, 64)
         wrap(w, "O%d" % r, 0)
         either(all_("w0"), w, AF.Identity, -1.0, 1535.75, -1.0, A.mult, 1535.75, A.add)
 
     def splice(r, k):
-        O, On, k0, z = "O%d" % (r - 1), "O%d" % r, (k - 3) * W, "b%d" % (6 + k % 2)
+        O, On, k0, z = "O%d" % (r - 1), "O%d" % r, (k - 3) * W, "z%d" % (k % 2)
         off, o0 = offsets(r - 1, k)
-        g0 = (k % 3) * 16 * W
-        h = 0
+        g0, h = (k % 3) * 16 * W, 0
         for u in KS[k - 3]:
             gather(c("kg", g0 + 16 * h, 16 * u), all_("K"), c(off, o0 + h, u))
             h += u
@@ -453,22 +393,22 @@ def _program():
         else:
             parts = [(0, W // 2, 2, lambda j: j if j < 8 else 8 * W + j - 8), (1, W // 2, 2, lambda j: j if j >= 8 else 8 * W + j + 8)]
         for h, n, st, at in parts:
-            group(c(z, h * n, n), [("CF", c("one", 0, n))] + [(c("WF", 128 * j, 128), c("kg", g0 + at(j), n, 16)) for j in range(16)])
+            group(c(z, h * n, n), [("CF", c("one", 0, n))] + [(c("WF", 128 * j, 128), c("kg", g0 + at(j), n, 16)) for j in range(16)], 3 * st)
         for h, n, st, at in parts:
             tt(c("Ox", k0 + h, n, st), c(O, k0 + h, n, st), c(z, h * n, n), A.max)
         m = W // 16
-        w = c(z, W, m); wo = k0 // 16
+        w, wo = c(z, W, m), k0 // 16
         wrap(w, "Ox", k0)
         tt(c("w1", wo, m), c("w0", wo, m), w, A.add)
         vcopy(c("wu", wo, m), c("w1", wo, m))
-        Ox, tg, cc, mv, on = c("Ox", k0, W), c("tg", k0, W), c("cc", k0, W), c("mm", k0, W), c("one", 0, W)
-        add("gts", "V", {"V": (50, 0, W, 0)}, [c("ui", 0, 2 * M + 16), c("wu", wo, m)], [tg], out=tg, win=c("ui", 0, 2 * M + 16), off=c("wu", wo, m), s1=-H)
+        Ox, tg, cc, mv, on, nl = c("Ox", k0, W), c("tg", k0, W), c("cc", k0, W), c("mm", k0, W), all_("one"), c(On, k0, W)
+        win, wu = c("ui", 0, 2 * M + 16), c("wu", wo, m)
+        add("gts", "V", {"V": (50, 0, W, 0)}, [win, wu], [tg], out=tg, win=win, off=wu, s1=-H)
         group(c(z, 0, W), [("PM", tg)])
         tt(cc, Ox, c(z, 0, W), A.max)
         group(c(z, W, W), [("C1m", on), ("BON", cc)])
-        group(c(z, 0, W), [("C2m", on), ("NBON", cc), ("I", Ox), ("PM", tg)])
+        group(c(z, 0, W), [("C2m", on), ("NBON", cc), ("I", Ox), ("PM", tg)], 2)
         tt(mv, c(O, k0, W), c(z, W, W), A.max)
-        nl = c(On, k0, W)
         tt(nl, mv, c(z, 0, W), A.min)
         if k in ONE[r]:
             ts(c("ov%d" % r, k0, W), nl, float(H), A.add)
@@ -479,48 +419,41 @@ def _program():
 
     def send(src, dst, lo, to, rs, ls):
         j = add("send", "G", {"G": (300, 0, 0, 0)}, [src], [], src=src, dst=dst, at=(lo, lo + R), to=to, rs=rs, lat=2500.0, sem=(ls, 8))
-        add("arrive", "R", {"R": (0, 0, 0, 0)}, [], [c(dst, lo, R)], lat=FAR[rs], sem=(rs, 8), after=j)
+        i = add("arrive", "R", {"R": (0, 0, 0, 0)}, [], [c(dst, lo, R)], lat=FAR[rs], sem=(rs, 8))
+        ops[i]["preds"].setdefault(j, False)
+
+    def level(r, l, between):
+        at = []
+        for n0, n, z in PARTS[l]:
+            k0 = len(at)
+            at += [lists(r, 3 * l + k) for k in range(k0, (n0 + n - 1) // W + 1)]
+            s0, st = at[n0 // W]
+            if l and n0 + n == M:
+                up(r, R + M, *PARTS[l][0][1:])
+            down(r, R + l * M + n0, n, z, c("sc", s0 + n0 % W * st, n, st))
+            between(k0, len(at))
 
     for r in range(RO):
-        if r and AHEAD:
-            roots(r)
-        else:
-            down(r, 0, 0, None if r == 0 else all_("ar%d" % r))
+        down(r, 0, R, "b", None if r == 0 else all_("ar%d" % r))
         dma(c("S2", 0, 512), c("S1", 0, 512))
-        for k in range(3):
-            if r and EARLY:
-                splice(r, 3 + k)
-            down(r, R + k * W, (k + 1) % 3, lists(r, k))
-            if r and not EARLY:
-                splice(r, 3 + k)
-            if r == 0:
-                second(k)
+        level(r, 0, lambda a, b: [splice(r, 3 + k) if r else second(k) for k in range(a, b)])
         dma(c("S3", 0, 2048), c("S2", 0, 2048))
-        for k in range(3):
-            down(r, 1024 + k * W, k, lists(r, 3 + k))
-            if k == 0 and r:
-                splice(r, 6)
-            if k == 0 and r == 0:
-                second(3)
-                late()
+        level(r, 1, lambda a, b: None if a else splice(r, 6) if r else (second(3), late()))
         if r == RO - 1:
-            for k in range(7):
-                dma(c("ys", k * W, W), c("s", k * W, W))
+            for n0, n in ((0, R), (R, 512), (768, 256), (1024, 512), (1536, 256)):
+                dma(c("ys", n0, n), c("s", n0, n))
         else:
             sums(r)
-        for k in range(GHOST):
-            up(r, 1024 + k * W, k)
-        gs = all_("gs%d" % r)
-        ecopy(gs, lists(r, 6))
+        gs, at = all_("gs%d" % r), lists(r, 6)
+        ecopy(gs, c("sc", at[0], R, at[1]))
         if r < RO - 1:
             send(gs, "ar%d" % (r + 1), 0, 1, "ra%d" % r, "la%d" % r)
         else:
             dma(c("ys", V, R), gs)
-        for k in range(GHOST, 3):
-            up(r, 1024 + k * W, k)
-        for k in range(3):
-            up(r, R + k * W, k)
-        up(r, 0, 0)
+        for l in (1, 0):
+            for n0, n, z in PARTS[2 - l][l:]:
+                up(r, R + l * M + n0, n, z)
+        up(r, 0, R, "b")
         if r < RO - 1:
             send(c("C%d" % r, 0, R), "C%d" % (r + 1), V, -1, "rb%d" % r, "lb%d" % r)
     return ops
@@ -531,72 +464,7 @@ def _cost(o, e):
     return f + CYC * (n + g * GCY) + p * PCY
 
 
-def _schedule(ops):
-    n = len(ops)
-    for o in ops:
-        if "after" in o:
-            o["preds"].setdefault(o["after"], False)
-    succ = [[] for _ in range(n)]
-    left = [len(o["preds"]) for o in ops]
-    for o in ops:
-        for p in o["preds"]:
-            succ[p].append(o["id"])
-    base = [_cost(o, o["engs"][0]) for o in ops]
-    rank = [0.0] * n
-    for i in range(n - 1, -1, -1):
-        o = ops[i]
-        acc, best = 0.0, 0.0
-        for j in sorted(succ[i], key=lambda j: -rank[j]):
-            best = max(best, rank[j] + 100 + acc)
-            acc += base[j] * FAC[ops[j]["kind"] in ("gather", "gmin")]
-        rank[i] = base[i] + o["lat"] + best
-    free = {"V": 0.0, "S": 0.0, "P": 0.0, "G": 0.0, "Y": 0.0, "R": 0.0}
-    done, eng, order = [0.0] * n, [None] * n, []
-    ready = [i for i in range(n) if left[i] == 0]
-    while ready:
-        cand, first = [], 1e18
-        for i in ready:
-            o = ops[i]
-            for e in o["engs"]:
-                t = free[e]
-                for p, hard in o["preds"].items():
-                    d = done[p]
-                    if eng[p] != e or ops[p]["sem"]:
-                        d += XLAT
-                    elif hard is not None and e != "P":
-                        d += 60.0
-                    if d > t:
-                        t = d
-                cand.append((t, i, e))
-                if t < first:
-                    first = t
-        best = None
-        for t, i, e in cand:
-            if t <= first + SLACK:
-                pr = rank[i]
-                if len(ops[i]["engs"]) > 1 and e == "V":
-                    pr -= PEN if ops[i]["kind"] == "gather" else PEN * 0.3
-                if best is None or pr > best[0] or (pr == best[0] and t < best[1]):
-                    best = (pr, t, i, e)
-        pr, t, i, e = best
-        o = ops[i]
-        eng[i] = e
-        if e != "R":
-            free[e] = t + _cost(o, e)
-        done[i] = t + _cost(o, e) + o["lat"]
-        order.append(i)
-        ready.remove(i)
-        for j in succ[i]:
-            left[j] -= 1
-            if left[j] == 0:
-                ready.append(j)
-    return order, eng, max(done)
-
-
-STEAL, PEN, TOL, MIX, PASSES = 1500.0, 4.0, 0.0, 0.6, 4
-
-
-def _forward(ops, succ, lst, tol):
+def _forward(ops, succ, lst, look):
     n = len(ops)
     left = [len(o["preds"]) for o in ops]
     free = {e: 0.0 for e in "VSPGYR"}
@@ -666,14 +534,14 @@ def _forward(ops, succ, lst, tol):
                 continue
             now = sorted([x for x in cand if x[0] <= t0 + 1], key=lambda x: x[1])
             ok = now[0]
-            if e in "VS":
+            if e in "VS" and look:
                 if est is None:
                     est = coming()
                 soon = [(t, lst[j]) for j, t in est.items() if e in ops[j]["engs"] and t0 + 1 < t < t0 + 1500 and (e == "S" or ops[j]["engs"] == "V")]
                 ok = None
                 for t, p, i in now:
                     end = t + ops[i]["cost"][e]
-                    if not any(u < end and l + tol < end and l < p for u, l in soon):
+                    if not any(u < end and l < end and l < p for u, l in soon):
                         ok = (t, p, i)
                         break
                 if ok is None:
@@ -730,31 +598,7 @@ def _backward(ops, succ, eng, done):
     return [(end - b) * 0.97 for b in back]
 
 
-def _schedule(ops):
-    n = len(ops)
-    succ = [[] for _ in ops]
-    for o in ops:
-        if "after" in o:
-            o["preds"].setdefault(o["after"], False)
-        o["cost"] = {e: _cost(o, e) for e in o["engs"]}
-        o["min"] = min(o["cost"].values())
-        for p in o["preds"]:
-            succ[p].append(o["id"])
-    lst, best = [i * 110.0 for i in range(n)], None
-    for k in range(PASSES):
-        order, eng, done = _forward(ops, succ, lst, TOL if k else 1e9)
-        if best is None or max(done) < best[2]:
-            best = (order, eng, max(done))
-        new = _backward(ops, succ, eng, done)
-        lst = [MIX * a + (1 - MIX) * b for a, b in zip(new, lst)] if k else new
-    return _improve(ops, best[0], best[1]) if STEPS else best
-
-
-STEPS, SEED, HEAT, LEAN = 36000, 2, 100.0, 0.1
-CASES = ((1.04, 0.55, 180.0), (1.6, 0.45, 150.0))
-
-
-def _improve(ops, order, eng):
+def _improve(ops, succ, order, eng):
     n = len(ops)
     names = "VSPGYR"
     pre = [[(p, bool(ops[p]["sem"]), h is not None) for p, h in o["preds"].items() if h != "order"] for o in ops]
@@ -764,13 +608,17 @@ def _improve(ops, order, eng):
     flex = [len(o["engs"]) > 1 for o in ops]
     both = [j for j in range(n) if flex[j]]
     eng = [names.index(e) for e in eng]
+    fixed = [[[(p, xl if s or eng[p] != eng[i] else 60.0 if h and eng[i] != 2 else 0.0) for p, s, h in pre[i] if not (flex[i] or flex[p])]
+              for i in range(n)] for g, pc, xl in CASES]
+    loose = [[x for x in pre[i] if flex[i] or flex[x[0]]] for i in range(n)]
     state = [SEED]
 
     def rnd():
         state[0] = (state[0] * 6364136223846793005 + 1442695040888963407) % 2 ** 64
         return (state[0] >> 11) / 2.0 ** 53
 
-    def run(order, eng, cost, xl, a, old):
+    def run(order, eng, case, a, b, old, bar):
+        cost, fix, xl = costs[case], fixed[case], CASES[case][2]
         done, why, q = (list(old[0]), list(old[1]), list(old[2])) if old else ([0.0] * n, [-1] * n, [False] * n)
         free, last = [0.0] * 6, [-1] * 6
         k, miss = a - 1, 5
@@ -779,24 +627,45 @@ def _improve(ops, order, eng):
             if e != 5 and last[e] < 0:
                 last[e] = j; free[e] = done[j] - lat[j]; miss -= 1
             k -= 1
-        for i in order[a:]:
+        late = same = 0
+        moved = set()
+        for k in range(a, n):
+            i = order[k]
             e = eng[i]; t = free[e]; w = last[e]; isq = True
-            for p, s, h in pre[i]:
-                d = done[p]
-                if s or eng[p] != e:
-                    d += xl
-                elif h and e != 2:
-                    d += 60.0
+            for p, x in fix[i]:
+                d = done[p] + x
+                if d > t:
+                    t = d; w = p; isq = False
+            for p, s, h in loose[i]:
+                d = done[p] + (xl if s or eng[p] != e else 60.0 if h else 0.0)
                 if d > t:
                     t = d; w = p; isq = False
             t += cost[i][e]
             if e != 5:
                 free[e] = t; last[e] = i
-            done[i] = t + lat[i]; why[i] = w; q[i] = isq
+            t += lat[i]
+            d = t - done[i]
+            done[i] = t; why[i] = w; q[i] = isq
+            if d:
+                moved.add(i); same = 0
+                late = late + 1 if d > bar else 0
+                if late > 60 and k > b:
+                    return None
+            else:
+                late = 0; same += 1
+                if same == 40 and k > b + 40 and not moved.intersection(last):
+                    rest = set(order[k + 1:])
+                    if not any(j in rest for m in moved for j in succ[m]):
+                        break
+                    same = 0
         return done, why, q
 
-    def value(order, eng, a, old):
-        out = [run(order, eng, c, CASES[k][2], a, old[k] if old else None) for k, c in enumerate(costs)]
+    def value(order, eng, a, b, old, bar):
+        out = []
+        for k in range(len(CASES)):
+            out.append(run(order, eng, k, a, b, old[k] if old else None, bar))
+            if out[-1] is None:
+                return None, None
         return sum(max(r[0]) for r in out) / len(out) + LEAN * sum(costs[0][j][0] for j in both if not eng[j]), out
 
     def chains(info):
@@ -810,7 +679,7 @@ def _improve(ops, order, eng):
             res.append(path)
         return res
 
-    cur, info = value(order, eng, 0, None)
+    cur, info = value(order, eng, 0, n, None, 0.0)
     pth = chains(info)
     best = (cur, order, eng)
     for step in range(STEPS):
@@ -828,7 +697,7 @@ def _improve(ops, order, eng):
                 continue
         no, ne = order, eng
         if flex[v] and (r < 0.4 or not q[v]):
-            ne = list(eng); ne[v] = 1 - eng[v]; a = order.index(v)
+            ne = list(eng); ne[v] = 1 - eng[v]; a = b = order.index(v)
         elif why[v] >= 0:
             u = why[v]
             a, b = order.index(u), order.index(v)
@@ -865,13 +734,31 @@ def _improve(ops, order, eng):
                 no = order[:a] + [j for j in seg if j in mv] + [j for j in seg if j not in mv] + order[b + 1:]
         else:
             continue
-        val, inf = value(no, ne, a, info)
-        if val <= cur or rnd() < math.exp((cur - val) / max(1.0, HEAT * (1 - step / STEPS))):
+        heat = max(1.0, HEAT * (1 - step / STEPS))
+        val, inf = value(no, ne, a, b, info, 4 * heat + 100)
+        if inf and (val <= cur or rnd() < math.exp((cur - val) / heat)):
             cur, info, order, eng = val, inf, no, ne
             pth = chains(info)
             if cur < best[0]:
                 best = (cur, order, eng)
     return best[1], [names[e] for e in best[2]], best[0]
+
+
+def _schedule(ops):
+    succ = [[] for _ in ops]
+    for o in ops:
+        o["cost"] = {e: _cost(o, e) for e in o["engs"]}
+        o["min"] = min(o["cost"].values())
+        for p in o["preds"]:
+            succ[p].append(o["id"])
+    lst, best = [i * 110.0 for i in range(len(ops))], None
+    for k in range(PASSES):
+        order, eng, done = _forward(ops, succ, lst, k > 0)
+        if best is None or max(done) < best[2]:
+            best = (order, eng, max(done))
+        new = _backward(ops, succ, eng, done)
+        lst = [MIX * a + (1 - MIX) * b for a, b in zip(new, lst)] if k else new
+    return _improve(ops, succ, best[0], best[1])
 
 
 def _waits(ops, order, eng):
@@ -901,7 +788,7 @@ def _waits(ops, order, eng):
         if o["sem"]:
             sem[i] = o["sem"]
         else:
-            count[e] += 1
+            count[e] += len(o["terms"]) if e == "P" else 1
             sem[i] = ("e" + e, count[e])
         final[sem[i][0]] = max(final.get(sem[i][0], 0), sem[i][1])
         clock[i] = dict(k) if e != "R" else {}
@@ -917,7 +804,7 @@ def _plan():
         ops = _program()
         order, eng, est = _schedule(ops)
         need, sem, tail = _waits(ops, order, eng)
-        _PLAN.update({"ops": ops, "order": order, "eng": eng, "need": need, "sem": sem, "tail": tail, "est": est})
+        _PLAN.update({"ops": ops, "order": order, "eng": eng, "need": need, "sem": sem, "tail": tail})
     return _PLAN
 
 
@@ -969,8 +856,6 @@ def rank_program(g, core, T, topo):
             x = q.activation(out, ap(o["a"]), o["func"], bias=o["bias"], scale=ap(o["scale"]))
         elif kind == "scan":
             x = q.tensor_tensor_scan(out, ap(o["d0"]), ap(o["d1"]), 0.0, o["op0"], o["op1"])
-        elif kind == "red":
-            x = q.tensor_reduce(out, ap(o["a"]), AxisListType.X, A.add)
         elif kind == "gather":
             src = ap(o["win"]).indirect(ap(o["off"]))
             x = q.tensor_copy(out, src) if e == "V" else q.activation(out, src, AF.Copy)
@@ -979,9 +864,11 @@ def rank_program(g, core, T, topo):
         elif kind == "gmin":
             x = q.tensor_tensor(out, ap(o["win"]).indirect(ap(o["off"])), ap(o["b"]), A.min)
         elif kind == "mm":
-            x = q.matmul(out, ap(o["lhs"]), ap(o["rhs"]), o["start"], o["stop"])
+            for lhs, rhs, start, stop in o["terms"]:
+                q.matmul(out, ap(lhs), ap(rhs), start, stop).then_inc(T.sem[s], 1)
+            continue
         elif kind == "asel":
-            x = q.affine_select(out, ap(o["in_"]), o["pat"], o["op"], 0.0, o["base"], o["cm"])
+            x = q.affine_select(out, ap(o["in_"]), o["pat"], o["op"], o["fill"], o["base"], o["cm"])
         else:
             x = q.iota(out, o["pat"], o["base"], o["cm"], allow_small_or_imprecise_dtypes=True)
         x.then_inc(T.sem[s], 1)

import math

from concourse.mybir import AluOpType as A, ActivationFunctionType as AF

R, M, V, F, RO = 256, 768, 1792, 512, 3
E = 2 * V
H = V
W = 256
BF, F2, F4, I4, U2 = "bfloat16", "float16", "float32", "int32", "uint16"
BIG = 8192.0

ONE = ((0, 4, 5, 6), (4, 5), (4, 5, 6))
PIECES = ((32, 96), (64, 64), (64, 64))
WHOLE = (64, 64, 64, 64)
KS = ((32,) * 8, (32,) * 8, (64,) * 4, (64,) * 4)
WIDE = ((0, 512, "a"), (512, 256, "b"))
NARROW = ((0, 256, "a"), (256, 256, "d"), (512, 256, "b"))
TAIL = ((0, 256, "b"), (256, 384, "e"), (640, 128, "b"))
PARTS = (TAIL, NARROW, WIDE)

SCRATCH = {}


def _b(name, n, d=BF):
    SCRATCH[name] = ("sbuf", [128, n], d)


for _n in ("I", "tb", "ON", "PM", "t1", "t2", "DL", "DH", "HI", "L2", "B", "g1", "g2", "g3", "g4", "GA", "QA", "QB", "QF", "HA", "HB", "NB", "PB",
           "XF", "YF", "XA", "YA", "XB", "YB", "NON", "CF", "C1m", "C2m", "BON", "NBON"):
    _b(_n, 128)
_b("D2", 128, F4); _b("one", W); _b("sg", 1, F4)
_b("WF", 2048); _b("sa", 2048); _b("w0", 64, F4)
_b("R8", 2048); _b("R16", 2048)
_b("x", V); _b("s", V); _b("zi", V); _b("ui", V + 16, I4); _b("pi", 224, I4); _b("po", 224, U2)
_b("oF", M, U2); _b("oN", M, U2); _b("OL", M, F2)
for _r in range(RO):
    _b("ov%d" % _r, 1024, U2); _b("O%d" % _r, 1024, F2)
    _b("C%d" % _r, V + R + F); _b("ar%d" % _r, R); _b("gs%d" % _r, R)
_b("S1", 528); _b("S2", 3600); _b("S3", 3600); _b("K", 3600)
_b("ga", 16 * M); _b("sc", 80 * W); _b("kg", 48 * W)
_b("fd", V); _b("d0", R)
for _n in "abcde":
    _b("v" + _n, 1024); _b("ab" + _n, 1024); _b("tm" + _n, 512)
_b("Ox", 1024, F2); _b("tg", 1024, F2); _b("cc", 1024, F2); _b("mm", 1024, F2)
_b("w1", 64, I4); _b("wu", 64, U2)
PSUM = {"pa": 1024, "qa": 1024, "pb": 512, "qb": 512, "z0": 512, "z1": 512}
for _n in PSUM:
    SCRATCH[_n] = ("psum", [128, PSUM[_n]], F4)
ND = 48
SEMAPHORES = ["eV", "eS", "eP", "eG"] + ["d%d" % _i for _i in range(ND)] + ["%s%d" % (_p, _r) for _p in ("ra", "rb", "la", "lb") for _r in range(RO - 1)]
EXT = {"piv": BF, "safe": BF, "lem": BF, "leaf": BF, "uses": I4, "prem": I4, "yc": BF, "ys": BF}

CYC, GCY, PCY, XLAT = 0.83, 1.3, 0.5, 220.0
CASES = ((1.2, 0.58, 220.0), (1.72, 0.45, 150.0))
FAR = {"ra0": 6000.0, "ra1": 4000.0, "rb0": 9000.0, "rb1": 9000.0}
STEAL, PEN, MIX, PASSES = 1500.0, 4.0, 0.6, 4
STEPS, SEED, HEAT, LEAN = 150000, 2, 50.0, 0.05


def _psum(v):
    return v[0] in PSUM


def _two(v):
    return (SCRATCH[v[0]][2] if v[0] in SCRATCH else EXT[v[0]]) in (BF, F2, U2)


def _hi(v):
    return v[1] + (v[2] - 1) * v[3] + 1


def _over(a, b):
    if a[0] >= b[1] or b[0] >= a[1]:
        return False
    return not (a[2] == b[2] and a[2] > 1 and (a[0] - b[0]) % a[2])


def _covers(a, b):
    return a[0] <= b[0] and a[1] >= b[1] and (a[2] == 1 or (a[2] == b[2] and (a[0] - b[0]) % a[2] == 0))


def _program():
    ops, bufs, last, nd, gate = [], {}, {}, [0, 0], {}

    def add(kind, engs, cyc, reads, writes, **kw):
        i = len(ops)
        preds = {}
        for v in reads:
            reg = (v[1], _hi(v), v[3]); b = bufs.setdefault(v[0], {"w": [], "r": []})
            for (q, j) in b["w"]:
                if _over(q, reg):
                    preds[j] = True
        for v in writes:
            reg = (v[1], _hi(v), v[3]); b = bufs.setdefault(v[0], {"w": [], "r": []})
            for (q, j) in b["w"]:
                if _over(q, reg):
                    preds[j] = True
            for (q, j) in b["r"]:
                if _over(q, reg):
                    preds.setdefault(j, False)
        banks = {(v[0], k) for v in list(reads) + list(writes) if _psum(v) for k in range(v[1] // 512, (_hi(v) - 1) // 512 + 1)}
        for k in sorted(banks):
            if k in last:
                preds.setdefault(last[k], None)
            last[k] = i
        for v in writes:
            reg = (v[1], _hi(v), v[3]); b = bufs[v[0]]
            b["w"] = [z for z in b["w"] if not _covers(reg, z[0])] + [(reg, i)]
            b["r"] = [z for z in b["r"] if not _covers(reg, z[0])]
        for v in reads:
            bufs[v[0]]["r"].append(((v[1], _hi(v), v[3]), i))
        if engs in gate:
            preds.setdefault(gate[engs], None)
        op = {"kind": kind, "engs": engs, "cyc": cyc, "preds": preds, "id": i, "lat": 0.0, "sem": None}
        op.update(kw)
        ops.append(op)
        return i

    def c(name, lo, n, st=1):
        if name in ("pd", "qd"):
            return (name[0] + "a", lo + 512, n, st)
        if name in ("pe", "qe"):
            return (name[0] + "a", lo + 128, n, st)
        return (name, lo, n, st)

    def all_(name):
        return (name, 0, SCRATCH[name][1][1], 1)

    def _fast(out, a):
        return .5 if _two(out) and _two(a) and not _psum(a) else 1

    def dma(out, in_):
        k = nd[0]; nd[0] += 1
        n = max(out[2], in_[2]) * (2 if _two(out) else 4) * 128
        load = in_[0] in EXT
        if load:
            nd[1] += n
        i = add("dma", "Y", {"Y": (60, 0, 0, 0)}, [in_], [out], out=out, in_=in_, lat=2200.0 + (nd[1] if load else n) / 250.0, sem=("d%d" % k, 16))
        if load and k:
            ops[i]["preds"][i - 1] = "order"

    def memset(out, val):
        add("memset", "V", {"V": (60, out[2] * (.5 if _two(out) else 1), 0, 0)}, [], [out], out=out, val=val)

    def tt(out, a, b, op):
        add("tt", "V", {"V": (60, out[2] * (1 if _psum(a) or _psum(b) else 2), 0, 0)}, [a, b], [out], out=out, a=a, b=b, op=op)

    def ts(out, a, s1, op0, s2=None, op1=None):
        add("ts", "V", {"V": (60, out[2] * _fast(out, a), 0, 0)}, [a], [out], out=out, a=a, s1=s1, s2=s2, op0=op0, op1=op1)

    def vcopy(out, a):
        add("copy", "V", {"V": (60, out[2] * _fast(out, a), 0, 0)}, [a], [out], out=out, a=a)

    def either(out, a, func, scale, bias, s1, op0, s2=None, op1=None):
        rd = [a] + ([s1] if isinstance(s1, tuple) else [])
        add("either", "SV", {"S": (70, out[2], 0, 0), "V": (60, out[2] * _fast(out, a), 0, 0)}, rd, [out], out=out, a=a,
            func=func, scale=scale, bias=bias, s1=s1, op0=op0, s2=s2, op1=op1)

    def scaled(out, a, k):
        either(out, a, AF.Copy, float(k), 0.0, float(k), A.mult)

    def ecopy(out, a):
        add("copy", "SV", {"S": (70, out[2], 0, 0), "V": (60, out[2] * _fast(out, a), 0, 0)}, [a], [out], out=out, a=a)

    def scan(out, d0, d1):
        add("scan", "V", {"V": (60, out[2] * .5, 0, 0)}, [d0, d1], [out], out=out, d0=d0, d1=d1, op0=A.max, op1=A.min)

    def gather(out, win, off):
        add("gather", "SV", {"S": (65, 0, out[2], 0), "V": (50, 0, out[2], 0)}, [win, off], [out], out=out, win=win, off=off)

    def gmin(out, win, off, b):
        add("gmin", "V", {"V": (50, 0, out[2], 0)}, [win, off, b], [out], out=out, win=win, off=off, b=b)

    def group(out, terms, by=1):
        full = [(l if isinstance(l, tuple) else all_(l), r, k == 0, k == len(terms) - 1) for k, (l, r) in enumerate(terms)]
        for k in range(0, len(full), by):
            z = full[k:k + by]
            add("mm", "P", {"P": (30 * len(z), 0, 0, max(64, out[2]) * len(z))}, [v for t in z for v in t[:2]], [out], out=out, terms=z)

    def asel(out, in_, pat, op, base, cm, val=0.0):
        add("asel", "G", {"G": (170, out[2] * 2, 0, 0)}, [in_], [out], out=out, in_=in_, pat=pat, op=op, base=base, cm=cm, fill=val)

    def iota(out, pat, base, cm):
        add("iota", "G", {"G": (130, out[2] * 2, 0, 0)}, [], [out], out=out, pat=pat, base=base, cm=cm)

    def fill(out, val):
        iota(out, [[0, out[2]]], val, 0)

    dma(c("x", 0, R), c("piv", 0, R))
    dma(c("s", 0, R), c("safe", 0, R))
    dma(c("ui", 0, W), c("uses", 0, W))
    dma(c("ui", W, M - W), c("uses", W, M - W))
    dma(c("x", R, M), c("piv", R, M))
    dma(c("ui", M, M), c("uses", M, M))
    dma(c("x", R + M, M), c("piv", R + M, M))
    dma(all_("pi"), c("prem", 0, 224))
    dma(c("C0", V, R), c("lem", 0, R))
    dma(c("C0", V + R, F), c("leaf", 0, F))
    dma(c("ui", 2 * M + 16, R), c("uses", 2 * M, R))
    for r in range(1, RO):
        dma(c("C%d" % r, V + R, F), c("leaf", 0, F))
    memset(all_("one"), 1.0)
    iota(all_("D2"), [[-16, 8], [248, 2], [-1, 8]], 0, 1)
    for n, k in (("DL", 0), ("DH", 256), ("t1", 8), ("t2", 248)):
        ts(all_(n), all_("D2"), float(k), A.is_equal)
    tt(all_("I"), all_("DL"), all_("DH"), A.add)
    tt(all_("PM"), all_("t1"), all_("t2"), A.add)
    asel(all_("tb"), c("one", 0, 128), [[-16, 8], [0, 16]], A.is_ge, 0, 1)
    asel(all_("ON"), all_("tb"), [[16, 8], [0, 16]], A.is_ge, 15, -1)
    asel(all_("L2"), all_("ON"), [[0, 8], [1, 4], [0, 4]], A.not_equal, -2, 0)
    asel(all_("HI"), all_("ON"), [[0, 8], [1, 2], [0, 8]], A.is_equal, -1, 0)
    tt(all_("g3"), all_("L2"), all_("HI"), A.add)
    scaled(all_("NON"), all_("g3"), -1)
    gate["G"] = len(ops) - 3
    iota(all_("B"), [[-16, 8], [0, 16]], 0, 1)
    gate["G"] = len(ops) - 1
    for n, k, a in (("HB", 0, 256), ("g1", 8, 256), ("g2", 12, -256)):
        ts(all_(n), all_("B"), float(k), A.is_equal, float(a), A.mult)
    tt(all_("GA"), all_("g1"), all_("g2"), A.add)
    ga = len(ops) - 1
    memset(c("S1", 512, 16), 255.0)
    for n, k, u in (("R16", 16, max(WHOLE)), ("R8", 8, max(max(z) for z in PIECES))):
        memset(c(n, 0, 16 * u), 0.0); memset(c(n, 0, 16 * u // k, k), 255.0)
        gate["V"] = ga
    fill(c("S2", 2048, 1552), 255); fill(c("S3", E, 16), 255)

    def halves(out, src, bank, cap):
        ev, od = c(src[0], src[1], W // 2, 2), c(src[0], src[1] + 1, W // 2, 2)
        group(c(bank[0], bank[1], W // 2), [("DL", ev), ("DH", od)], 2)
        group(c(bank[0], bank[1] + W // 2, W // 2), [("t1", ev), ("t2", od)], 2)
        ts(out, bank, float(H), A.add, float(cap), A.min)

    for k in range(3):
        if any(k in ONE[r] for r in range(RO)):
            ts(c("oN", k * W, W), c("ui", k * W, W), 512, A.min)
        if any(k not in ONE[r] for r in range(RO)):
            ts(c("OL", k * W, W), c("ui", k * W, W), -H, A.add)
            halves(c("oF", k * W, W), c("OL", k * W, W), c("z%d" % (k % 2), 0, W), 512)

    def second(k):
        u = c("ui", M + k * W + 16 * (k == 3), W)
        if k + 3 in ONE[0]:
            vcopy(c("ov0", k * W, W), u)
            ts(c("O0", k * W, W), c("ov0", k * W, W), -H, A.add)
        else:
            ts(c("O0", k * W, W), u, -H, A.add)
            halves(c("ov0", k * W, W), c("O0", k * W, W), c("z%d" % (1 - k % 2), 0, W), E)
        if k < 3:
            n0, w, t = ((1024, 768, 1792), (256, 768, 1024), (0, 256, 256))[k]
            for h in (0, 112):
                j = h + n0 // 16
                ts(c("po", j, w // 16), c("pi", j, w // 16), -t, A.add)

    def late():
        def rows(n, lo, hi):
            asel(all_(n), all_(n), [[-16, 8], [0, 16]], A.is_ge, -lo, 1)
            asel(all_(n), all_(n), [[16, 8], [0, 16]], A.is_ge, hi, -1)
        for n, lo, hi in (("QA", 32, 1), ("QB", -1, 1)):
            iota(all_(n), [[0, 8], [hi - lo, 2], [0, 8]], lo, 0)
            rows(n, 0, 15)
        for n, k in (("QF", 2048), ("g4", 0)):
            iota(all_(n), [[2048, 8], [k, 2], [0, 8]], 960, -128)
            rows(n, 0, 11)
        fill(all_("PB"), 32)
        rows("PB", 8, 15)
        fill(all_("C1m"), H // 14)
        asel(all_("C1m"), all_("C1m"), [[-16, 8], [0, 16]], A.not_equal, 0, 1, -BIG * 16 * H)
        rows("C1m", 0, 14)
        for n, m, k in (("HA", "HB", -1), ("NB", "PB", -1), ("XF", "g4", 256), ("YF", "g4", -256), ("XA", "ON", 8192), ("YA", "ON", -8192),
                        ("XB", "ON", -256), ("YB", "ON", 256), ("CF", "I", H - 4096), ("C2m", "C1m", -1), ("BON", "ON", BIG), ("NBON", "ON", -BIG)):
            scaled(all_(n), all_(m), k)
        for k in range(0, V, 2 * W):
            n = min(2 * W, V - k)
            either(c("zi", k, n), c("x", k, n), AF.Relu, -255.0, 255.0, 0.0, A.is_equal, 255.0, A.mult)
        group(c("z1", 0, 1), [("QB", c("one", 0, 1))])
        scaled(all_("sg"), c("z1", 0, 1), 1.0 / 16)
        iota(all_("WF"), [[512, 16], [0, 8], [-512, 16]], 256, 0)
        asel(all_("WF"), all_("WF"), [[-1, 16], [0, 8], [1, 16]], A.is_ge, 0, 0)
        asel(all_("WF"), all_("WF"), [[0, 16], [-16, 8], [0, 16]], A.is_ge, 0, 1)
        asel(all_("WF"), all_("WF"), [[0, 16], [16, 8], [0, 16]], A.is_ge, 15, -1)
        asel(all_("sa"), all_("WF"), [[1, 16], [0, 8], [-1, 16]], A.is_equal, 0, 0)
        for k in range(0, 2048, 1024):
            scaled(c("sa", k, 1024), c("sa", k, 1024), -1.0 / 512)
        fill(c("K", 0, 512), 0); fill(c("K", E, 16), 0)
        memset(c("ui", 2 * M, 16), E)

    def offsets(r, k):
        if k >= 3:
            return "ov%d" % r, (k - 3) * W
        return ("oN" if k in ONE[r] else "oF"), k * W

    def lists(r, k):
        win = all_("S1" if k < 3 else "S2" if k < 6 else "S3")
        off, o0 = offsets(r, k)
        g0, h = (k % 3) * 16 * W, 0
        s0 = 40 * W * (k // 3 % 2) + sum(16 * W if j in ONE[r] else 8 * W for j in range(k - k % 3, k))
        if k in ONE[r]:
            for u in WHOLE:
                gather(c("ga", g0 + 16 * h, 16 * u), win, c(off, o0 + h, u))
                scan(c("sc", s0 + 16 * h, 16 * u), c("R16", 0, 16 * u), c("ga", g0 + 16 * h, 16 * u))
                h += u
            return s0 + 15, 16
        for u in PIECES[k % 3 if k < 6 else 2]:
            a, b = c("ga", g0 + 16 * h, 16 * u), c("ga", g0 + 8 * W + 16 * h, 16 * u)
            gather(a, win, c(off, o0 + h, u))
            gmin(b, win, c(off, o0 + W // 2 + h, u), a)
            scan(c("sc", s0 + 16 * h, 16 * u), c("R8", 0, 16 * u), b)
            h += u
        return s0 + 7, 8

    def state(n0, n):
        return all_("d0") if n0 < R else c("K", 2 * n0, n, 2)

    def test(r, n0, n, z, fresh):
        lo = 256 if n0 < R else 1024 if n0 < 1024 else 1792
        for h in (0, 1):
            gather(c("ab" + z, h * n, n), c("C%d" % r, lo, V + R + F - lo), c("po", 112 * h + n0 // 16, n // 16))
        p = "pb" if z == "c" else "p" + z
        if fresh:
            group(c(p, 0, n), [("I", c("x", n0, n))])
            group(c(p, n, n), [("PM", c("x", n0, n))])
        tt(c("v" + z, 0, 2 * n), c("ab" + z, 0, 2 * n), c(p, 0, 2 * n), A.is_lt)

    def down(r, n0, n, z, Mv):
        p, q = "p" + z, "q" + z
        x, s, dm, fd = c("x", n0, n), c("s", n0, n), state(n0, n), c("fd", n0, n)
        sv = s if r or Mv is None else Mv
        if r:
            group(c(q, n, n), [("NB", dm), ("I", Mv)])
            tt(s, s, c(q, n, n), A.max)
        t = "S1" if n0 < R else "S2" if n0 < 1024 else "S3"
        ta, tb = c(t, 2 * n0, n, 2), c(t, 2 * n0 + 1, n, 2)
        group(c(p, 0, n), [("I", x)] + [("HA", dm)] * (r > 0), 2)
        group(c(p, n, n), [("PM", x)] + [("HB", dm)] * (r > 0), 2)
        tt(ta, sv, c(p, 0, n), A.max)
        tt(tb, sv, c(p, n, n), A.max)
        group(c(q, 0, n), [("NON", sv), ("L2", ta), ("HI", tb)])
        either(fd, c(q, 0, n), AF.Relu, -1.0, 1.0, 0.0, A.is_equal)
        o = q if n0 >= 1024 else p
        group(c(q, 0, n), [("I", ta), ("GA", fd)])
        group(c(o, n, n), [("I", tb), ("HB", fd)])
        ecopy(ta, c(q, 0, n))
        ecopy(tb, c(o, n, n))
        if sv != s:
            asel(s, sv, [[0, n]], A.is_equal, 0, 0)
        if n0 >= 1024:
            test(r, n0, n, z, False)

    def up(r, n0, n, z):
        y = "c" if n0 < R else z
        p, q = "p" + z, "q" + z
        s, fd, dm, zi = c("s", n0, n), c("fd", n0, n), state(n0, n), c("zi", n0, n)
        if n0 < 1024:
            test(r, n0, n, y, True)
        va, vb = c("v" + y, 0, n), c("v" + y, n, n)
        if r == RO - 1:
            group(c(p, 0, n), [("I", zi), ("XF", fd), ("XA", va), ("XB", vb)])
            group(c(p, n, n), [("PM", zi), ("YF", fd), ("YA", va), ("YB", vb)])
        else:
            group(c(q, 0, n), [("QF", fd), ("QA", va), ("QB", vb)])
            either(dm, c(q, 0, n), AF.Sign, 1.0, 0.0, -1.0, A.max, 1.0, A.min)
            group(c(p, 0, n), [("I", zi), ("HB", dm)])
            group(c(p, n, n), [("PM", zi), ("HA", dm)])
        tm, C = c("tm" + y, 0, n), c("C%d" % r, n0, n)
        tt(tm, c("ab" + y, 0, n), c(p, 0, n), A.min)
        tt(c(p, n, n), c("ab" + y, n, n), c(p, n, n), A.min)
        tt(C, tm, c(p, n, n), A.max)
        if r == RO - 1:
            dma(c("yc", n0, n), C)
            return
        if n0 >= R:
            either(c("K", 2 * n0 + 1, n, 2), dm, AF.Copy, all_("sg"), 0.0, all_("sg"), A.mult)
        group(c(q, n, n), [("I", s), ("PB", dm)])
        either(s, c(q, n, n), AF.Relu, 1.0, -256.0, -256.0, A.add, 0.0, A.max)

    def wrap(out, src, k0):
        group(out, [(c("sa", 128 * q, 128), c(src, k0 + q, out[2], 16)) for q in range(16)], 8)

    def sums(r):
        w = c("z0", W, 64)
        wrap(w, "O%d" % r, 0)
        either(all_("w0"), w, AF.Identity, -1.0, 1535.75, -1.0, A.mult, 1535.75, A.add)

    def splice(r, k):
        O, On, k0, z = "O%d" % (r - 1), "O%d" % r, (k - 3) * W, "z%d" % (k % 2)
        off, o0 = offsets(r - 1, k)
        g0, h = (k % 3) * 16 * W, 0
        for u in KS[k - 3]:
            gather(c("kg", g0 + 16 * h, 16 * u), all_("K"), c(off, o0 + h, u))
            h += u
        if k in ONE[r - 1]:
            parts = [(0, W, 1, lambda j: j)]
        else:
            parts = [(0, W // 2, 2, lambda j: j if j < 8 else 8 * W + j - 8), (1, W // 2, 2, lambda j: j if j >= 8 else 8 * W + j + 8)]
        for h, n, st, at in parts:
            group(c(z, h * n, n), [("CF", c("one", 0, n))] + [(c("WF", 128 * j, 128), c("kg", g0 + at(j), n, 16)) for j in range(16)], 3 * st)
        for h, n, st, at in parts:
            tt(c("Ox", k0 + h, n, st), c(O, k0 + h, n, st), c(z, h * n, n), A.max)
        m = W // 16
        w, wo = c(z, W, m), k0 // 16
        wrap(w, "Ox", k0)
        tt(c("w1", wo, m), c("w0", wo, m), w, A.add)
        vcopy(c("wu", wo, m), c("w1", wo, m))
        Ox, tg, cc, mv, on, nl = c("Ox", k0, W), c("tg", k0, W), c("cc", k0, W), c("mm", k0, W), all_("one"), c(On, k0, W)
        win, wu = c("ui", 0, 2 * M + 16), c("wu", wo, m)
        add("gts", "V", {"V": (50, 0, W, 0)}, [win, wu], [tg], out=tg, win=win, off=wu, s1=-H)
        group(c(z, 0, W), [("PM", tg)])
        tt(cc, Ox, c(z, 0, W), A.max)
        group(c(z, W, W), [("C1m", on), ("BON", cc)])
        group(c(z, 0, W), [("C2m", on), ("NBON", cc), ("I", Ox), ("PM", tg)], 2)
        tt(mv, c(O, k0, W), c(z, W, W), A.max)
        tt(nl, mv, c(z, 0, W), A.min)
        if k in ONE[r]:
            ts(c("ov%d" % r, k0, W), nl, float(H), A.add)
        else:
            halves(c("ov%d" % r, k0, W), nl, c(z, W, W), E)
        if r == 1 and k == 6:
            ts(c("ui", M, M), c(On, 0, M), H, A.add)

    def send(src, dst, lo, to, rs, ls):
        j = add("send", "G", {"G": (300, 0, 0, 0)}, [src], [], src=src, dst=dst, at=(lo, lo + R), to=to, rs=rs, lat=2500.0, sem=(ls, 8))
        i = add("arrive", "R", {"R": (0, 0, 0, 0)}, [], [c(dst, lo, R)], lat=FAR[rs], sem=(rs, 8))
        ops[i]["preds"].setdefault(j, False)

    def level(r, l, between):
        at = []
        for n0, n, z in PARTS[l]:
            k0 = len(at)
            at += [lists(r, 3 * l + k) for k in range(k0, (n0 + n - 1) // W + 1)]
            s0, st = at[n0 // W]
            if l and n0 + n == M:
                up(r, R + M, *PARTS[l][0][1:])
            down(r, R + l * M + n0, n, z, c("sc", s0 + n0 % W * st, n, st))
            between(k0, len(at))

    for r in range(RO):
        down(r, 0, R, "b", None if r == 0 else all_("ar%d" % r))
        dma(c("S2", 0, 512), c("S1", 0, 512))
        level(r, 0, lambda a, b: [splice(r, 3 + k) if r else second(k) for k in range(a, b)])
        dma(c("S3", 0, 2048), c("S2", 0, 2048))
        level(r, 1, lambda a, b: None if a else splice(r, 6) if r else (second(3), late()))
        if r == RO - 1:
            for n0, n in ((0, R), (R, 512), (768, 256), (1024, 512), (1536, 256)):
                dma(c("ys", n0, n), c("s", n0, n))
        else:
            sums(r)
        gs, at = all_("gs%d" % r), lists(r, 6)
        ecopy(gs, c("sc", at[0], R, at[1]))
        if r < RO - 1:
            send(gs, "ar%d" % (r + 1), 0, 1, "ra%d" % r, "la%d" % r)
        else:
            dma(c("ys", V, R), gs)
        for l in (1, 0):
            for n0, n, z in PARTS[2 - l][l:]:
                up(r, R + l * M + n0, n, z)
        up(r, 0, R, "b")
        if r < RO - 1:
            send(c("C%d" % r, 0, R), "C%d" % (r + 1), V, -1, "rb%d" % r, "lb%d" % r)
    return ops


def _cost(o, e):
    f, n, g, p = o["cyc"][e]
    return f + CYC * (n + g * GCY) + p * PCY


def _forward(ops, succ, lst, look):
    n = len(ops)
    left = [len(o["preds"]) for o in ops]
    free = {e: 0.0 for e in "VSPGYR"}
    done, eng, order, rdy = [None] * n, [None] * n, [], {}

    def enter(i):
        o = ops[i]; r = {}
        for e in o["engs"]:
            t = 0.0
            for p, hard in o["preds"].items():
                d = done[p]
                if hard == "order":
                    d -= ops[p]["lat"]
                elif eng[p] != e or ops[p]["sem"]:
                    d += XLAT
                elif hard is not None and e != "P":
                    d += 60.0
                if d > t:
                    t = d
            r[e] = t
        rdy[i] = r

    def coming():
        est = {i: min(max(free[e], t) for e, t in r.items()) for i, r in rdy.items()}
        front = list(rdy)
        for _ in range(5):
            nxt = []
            for i in front:
                for j in succ[i]:
                    if j in est:
                        continue
                    t = 0.0
                    for p in ops[j]["preds"]:
                        if done[p] is not None:
                            d = done[p]
                        elif p in est:
                            d = est[p] + ops[p]["min"] + ops[p]["lat"]
                        else:
                            t = None
                            break
                        d += 0 if ops[p]["engs"] == ops[j]["engs"] == "P" else XLAT
                        if d > t:
                            t = d
                    if t is not None:
                        est[j] = t; nxt.append(j)
            front = nxt
        return est
    for i in range(n):
        if left[i] == 0:
            enter(i)
    while rdy:
        est = pick = None
        for e in "RYGPSV":
            cand = []
            for i, r in rdy.items():
                if e in r:
                    t = max(free[e], r[e]); p = lst[i]
                    if e == "V" and "S" in r:
                        if max(free["S"], r["S"]) - t < STEAL:
                            continue
                        p += PEN * ops[i]["cost"]["V"]
                    cand.append((t, p, i))
            if not cand:
                continue
            t0 = min(cand)[0]
            if pick is not None and t0 >= pick[0]:
                continue
            now = sorted([x for x in cand if x[0] <= t0 + 1], key=lambda x: x[1])
            ok = now[0]
            if e in "VS" and look:
                if est is None:
                    est = coming()
                soon = [(t, lst[j]) for j, t in est.items() if e in ops[j]["engs"] and t0 + 1 < t < t0 + 1500 and (e == "S" or ops[j]["engs"] == "V")]
                ok = None
                for t, p, i in now:
                    end = t + ops[i]["cost"][e]
                    if not any(u < end and l < end and l < p for u, l in soon):
                        ok = (t, p, i)
                        break
                if ok is None:
                    free[e] = min([u for u, l in soon if l < now[-1][1]] + [x[0] for x in cand if x[0] > t0 + 1])
                    pick = None
                    break
            pick = (ok[0], ok[2], e)
        if pick is None:
            continue
        t, i, e = pick
        o = ops[i]
        eng[i] = e
        if e != "R":
            free[e] = t + o["cost"][e]
        done[i] = t + o["cost"][e] + o["lat"]
        order.append(i)
        del rdy[i]
        for j in succ[i]:
            left[j] -= 1
            if left[j] == 0:
                enter(j)
    return order, eng, done


def _backward(ops, succ, eng, done):
    n = len(ops)
    st = {e: [] for e in "VSPGY"}; en = {e: [] for e in "VSPGY"}
    back = [0.0] * n
    for i in sorted(range(n), key=lambda i: (-done[i], -i)):
        o, e = ops[i], eng[i]
        t = o["lat"]
        for j in succ[i]:
            d = back[j] + o["lat"]
            if ops[j]["preds"][i] == "order":
                d = back[j]
            elif eng[j] != e or o["sem"]:
                d += XLAT
            elif ops[j]["preds"][i] is not None and e != "P":
                d += 60.0
            if d > t:
                t = d
        c = o["cost"][e]
        if e != "R":
            S, N = st[e], en[e]
            k = len(N)
            while k and N[k - 1] > t:
                k -= 1
            while k < len(S) and S[k] < t + c:
                t = max(t, N[k])
                k += 1
            S.insert(k, t); N.insert(k, t + c)
        back[i] = t + c
    end = max(back)
    return [(end - b) * 0.97 for b in back]


def _improve(ops, succ, order, eng):
    n = len(ops)
    names = "VSPGYR"
    pre = [[(p, bool(ops[p]["sem"]), h is not None) for p, h in o["preds"].items() if h != "order"] for o in ops]
    pset = [set(o["preds"]) for o in ops]
    lat = [o["lat"] for o in ops]
    costs = [[{names.index(e): f + CYC * (a + ge * g) + p * pc for e, (f, a, ge, p) in o["cyc"].items()} for o in ops] for g, pc, xl in CASES]
    flex = [len(o["engs"]) > 1 for o in ops]
    both = [j for j in range(n) if flex[j]]
    eng = [names.index(e) for e in eng]
    fixed = [[[(p, xl if s or eng[p] != eng[i] else 60.0 if h and eng[i] != 2 else 0.0) for p, s, h in pre[i] if not (flex[i] or flex[p])]
              for i in range(n)] for g, pc, xl in CASES]
    loose = [[x for x in pre[i] if flex[i] or flex[x[0]]] for i in range(n)]
    state = [SEED]

    def rnd():
        state[0] = (state[0] * 6364136223846793005 + 1442695040888963407) % 2 ** 64
        return (state[0] >> 11) / 2.0 ** 53

    def run(order, eng, case, a, b, old, bar):
        cost, fix, xl = costs[case], fixed[case], CASES[case][2]
        done, why, q = (list(old[0]), list(old[1]), list(old[2])) if old else ([0.0] * n, [-1] * n, [False] * n)
        free, last = [0.0] * 6, [-1] * 6
        k, miss = a - 1, 5
        while k >= 0 and miss:
            j = order[k]; e = eng[j]
            if e != 5 and last[e] < 0:
                last[e] = j; free[e] = done[j] - lat[j]; miss -= 1
            k -= 1
        late = same = 0
        moved = set()
        for k in range(a, n):
            i = order[k]
            e = eng[i]; t = free[e]; w = last[e]; isq = True
            for p, x in fix[i]:
                d = done[p] + x
                if d > t:
                    t = d; w = p; isq = False
            for p, s, h in loose[i]:
                d = done[p] + (xl if s or eng[p] != e else 60.0 if h else 0.0)
                if d > t:
                    t = d; w = p; isq = False
            t += cost[i][e]
            if e != 5:
                free[e] = t; last[e] = i
            t += lat[i]
            d = t - done[i]
            done[i] = t; why[i] = w; q[i] = isq
            if d:
                moved.add(i); same = 0
                late = late + 1 if d > bar else 0
                if late > 60 and k > b:
                    return None
            else:
                late = 0; same += 1
                if same == 40 and k > b + 40 and not moved.intersection(last):
                    rest = set(order[k + 1:])
                    if not any(j in rest for m in moved for j in succ[m]):
                        break
                    same = 0
        return done, why, q

    def value(order, eng, a, b, old, bar):
        out = []
        for k in range(len(CASES)):
            out.append(run(order, eng, k, a, b, old[k] if old else None, bar))
            if out[-1] is None:
                return None, None
        return sum(max(r[0]) for r in out) / len(out) + LEAN * sum(costs[0][j][0] for j in both if not eng[j]), out

    def chains(info):
        res = []
        for done, why, q in info:
            i = done.index(max(done)); path = []
            while i >= 0:
                if flex[i] or q[i]:
                    path.append(i)
                i = why[i]
            res.append(path)
        return res

    cur, info = value(order, eng, 0, n, None, 0.0)
    pth = chains(info)
    best = (cur, order, eng)
    for step in range(STEPS):
        k = int(rnd() * len(info))
        done, why, q = info[k]
        v = pth[k][int(rnd() * len(pth[k]))]
        r = rnd()
        if step % 256 == 0:
            d0, c0 = info[0][0], costs[0]
            at = {j: (d0[j] - lat[j] - c0[j][eng[j]], z) for z, j in enumerate(order)}
            order = sorted(order, key=lambda j: at[j])
        if r < 0.1:
            v = both[int(rnd() * len(both))]
            if eng[v]:
                continue
        no, ne = order, eng
        if flex[v] and (r < 0.4 or not q[v]):
            ne = list(eng); ne[v] = 1 - eng[v]; a = b = order.index(v)
        elif why[v] >= 0:
            u = why[v]
            a, b = order.index(u), order.index(v)
            far = (0, 0, 1, 2, 4, 8)[int(rnd() * 6)]
            if r > 0.7:
                for _ in range(far):
                    z = b + 1
                    while z < n and eng[order[z]] != eng[v]:
                        z += 1
                    if z < n:
                        b = z
                mv = {u}
                for j in order[a + 1:b + 1]:
                    if pset[j] & mv:
                        mv.add(j)
                if v in mv:
                    continue
                seg = order[a:b + 1]
                no = order[:a] + [j for j in seg if j not in mv] + [j for j in seg if j in mv] + order[b + 1:]
            else:
                for _ in range(far):
                    z = a - 1
                    while z >= 0 and eng[order[z]] != eng[v]:
                        z -= 1
                    if z >= 0:
                        a = z
                need, mv = set(pset[v]), {v}
                for j in reversed(order[a:b]):
                    if j in need:
                        mv.add(j); need |= pset[j]
                if u in mv:
                    continue
                seg = order[a:b + 1]
                no = order[:a] + [j for j in seg if j in mv] + [j for j in seg if j not in mv] + order[b + 1:]
        else:
            continue
        heat = max(1.0, HEAT * (1 - step / STEPS))
        val, inf = value(no, ne, a, b, info, 4 * heat + 100)
        if inf and (val <= cur or rnd() < math.exp((cur - val) / heat)):
            cur, info, order, eng = val, inf, no, ne
            pth = chains(info)
            if cur < best[0]:
                best = (cur, order, eng)
    return best[1], [names[e] for e in best[2]], best[0]


def _schedule(ops):
    succ = [[] for _ in ops]
    for o in ops:
        o["cost"] = {e: _cost(o, e) for e in o["engs"]}
        o["min"] = min(o["cost"].values())
        for p in o["preds"]:
            succ[p].append(o["id"])
    lst, best = [i * 110.0 for i in range(len(ops))], None
    for k in range(PASSES):
        order, eng, done = _forward(ops, succ, lst, k > 0)
        if best is None or max(done) < best[2]:
            best = (order, eng, max(done))
        new = _backward(ops, succ, eng, done)
        lst = [MIX * a + (1 - MIX) * b for a, b in zip(new, lst)] if k else new
    return _improve(ops, succ, best[0], best[1])


def _waits(ops, order, eng):
    pos = {i: k for k, i in enumerate(order)}
    count = {"V": 0, "S": 0, "P": 0, "G": 0}
    know = {e: {} for e in "VSPGYR"}
    sem, clock, need, final, waited = {}, {}, {}, {}, {}
    for i in order:
        o, e = ops[i], eng[i]
        k = know[e]
        w = {}
        if e != "R":
            ps = [p for p, hard in o["preds"].items() if hard != "order" and (ops[p]["sem"] or eng[p] != e or (hard is not None and e != "P"))]
            ps.sort(key=lambda p: -pos[p])
            for p in ps:
                s, val = sem[p]
                if k.get(s, 0) >= val:
                    continue
                w[s] = max(w.get(s, 0), val)
                k[s] = val
                for a, b in clock[p].items():
                    if k.get(a, 0) < b:
                        k[a] = b
        need[i] = sorted(w.items())
        for s, val in w.items():
            waited[s] = max(waited.get(s, 0), val)
        if o["sem"]:
            sem[i] = o["sem"]
        else:
            count[e] += len(o["terms"]) if e == "P" else 1
            sem[i] = ("e" + e, count[e])
        final[sem[i][0]] = max(final.get(sem[i][0], 0), sem[i][1])
        clock[i] = dict(k) if e != "R" else {}
    tail = [(s, v) for s, v in sorted(final.items()) if waited.get(s, 0) < v]
    return need, sem, tail


_PLAN = {}


def _plan():
    if not _PLAN:
        ops = _program()
        order, eng, est = _schedule(ops)
        need, sem, tail = _waits(ops, order, eng)
        _PLAN.update({"ops": ops, "order": order, "eng": eng, "need": need, "sem": sem, "tail": tail})
    return _PLAN


def rank_program(g, core, T, topo):
    rank = T.rank_of(core)
    if rank is None:
        return
    pl = _plan()
    queue = {"V": g.vector, "S": g.scalar, "P": g.tensor, "G": g, "Y": g.sync}

    def ap(v):
        if not isinstance(v, tuple):
            return v
        if v[3] == 1:
            return T[v[0]][:, v[1]:v[1] + v[2]]
        return T[v[0]][:, v[1]:_hi(v):v[3]]

    for i in pl["order"]:
        o, e = pl["ops"][i], pl["eng"][i]
        if e == "R":
            continue
        q = queue[e]
        for s, val in pl["need"][i]:
            q.wait_ge(T.sem[s], val)
        kind = o["kind"]
        s, val = pl["sem"][i]
        if kind == "send":
            dst = T.cores[(rank + o["to"]) % len(T.cores)]
            rid, pid, se = topo.addr(dst)
            g.remote_dma(out_ap=T[o["dst"]][:, o["at"][0]:o["at"][1]], in_ap=ap(o["src"]), remote_sem=T.sem[o["rs"]], local_sem=T.sem[s],
                         pid=pid, routing_id=rid, dma_engine_mask=topo.mask(core, dst))
            continue
        if kind == "dma":
            q.dma_start(out=ap(o["out"]), in_=ap(o["in_"])).then_inc(T.sem[s], 16)
            continue
        out = ap(o["out"])
        if kind == "memset":
            x = q.memset(out, o["val"])
        elif kind == "tt":
            x = q.tensor_tensor(out, ap(o["a"]), ap(o["b"]), o["op"])
        elif kind == "ts" or (kind == "either" and e == "V"):
            if o["op1"] is None:
                x = q.tensor_scalar(out, ap(o["a"]), ap(o["s1"]), None, o["op0"])
            else:
                x = q.tensor_scalar(out, ap(o["a"]), ap(o["s1"]), o["s2"], o["op0"], o["op1"])
        elif kind == "copy":
            x = q.tensor_copy(out, ap(o["a"])) if e == "V" else q.activation(out, ap(o["a"]), AF.Copy)
        elif kind == "either":
            x = q.activation(out, ap(o["a"]), o["func"], bias=o["bias"], scale=ap(o["scale"]))
        elif kind == "scan":
            x = q.tensor_tensor_scan(out, ap(o["d0"]), ap(o["d1"]), 0.0, o["op0"], o["op1"])
        elif kind == "gather":
            src = ap(o["win"]).indirect(ap(o["off"]))
            x = q.tensor_copy(out, src) if e == "V" else q.activation(out, src, AF.Copy)
        elif kind == "gts":
            x = q.tensor_scalar(out, ap(o["win"]).indirect(ap(o["off"])), o["s1"], None, A.add)
        elif kind == "gmin":
            x = q.tensor_tensor(out, ap(o["win"]).indirect(ap(o["off"])), ap(o["b"]), A.min)
        elif kind == "mm":
            for lhs, rhs, start, stop in o["terms"]:
                q.matmul(out, ap(lhs), ap(rhs), start, stop).then_inc(T.sem[s], 1)
            continue
        elif kind == "asel":
            x = q.affine_select(out, ap(o["in_"]), o["pat"], o["op"], o["fill"], o["base"], o["cm"])
        else:
            x = q.iota(out, o["pat"], o["base"], o["cm"], allow_small_or_imprecise_dtypes=True)
        x.then_inc(T.sem[s], 1)
    for s, val in pl["tail"]:
        g.wait_ge(T.sem[s], val)
